import numpy as np
import ml_dtypes


def mxq(x, axis, fmt="e4m3"):
    dtype, down = {"e4m3": (ml_dtypes.float8_e4m3fn, 7), "e5m2": (ml_dtypes.float8_e5m2, 14)}[fmt]
    v = np.moveaxis(np.asarray(x, np.float32).astype(ml_dtypes.bfloat16).astype(np.float64), axis, -1)
    blocks = v.reshape(v.shape[:-1] + (-1, 32))
    amax = np.abs(blocks).max(-1, keepdims=True)
    byte = np.maximum(np.where(amax > 0, np.frexp(amax)[1] - 1 + 127, 0) - down, 1)
    scale = np.exp2(byte - 127.0)
    codes = (blocks / scale).astype(np.float32).astype(dtype).astype(np.float64)
    return np.moveaxis((codes * scale).reshape(v.shape), -1, axis)


WIDE = False


def mx_kscale(k):
    if not WIDE:
        return np.ones(k)
    levels = np.array([10, -10, 5, -5, 0])
    if k % 512:
        return np.exp2(np.random.permutation(np.resize(levels, k // 32))).repeat(32)
    a = np.empty((k // 512, 16))
    for p in range(k // 512):
        a[p, :8] = np.random.permutation(np.resize(levels, 8))
        for g in range(8):
            far = levels[np.abs(levels - a[p, g]) >= 10]
            a[p, g + 8] = far[np.random.randint(len(far))]
    return np.exp2(a.ravel()).repeat(32)


def f64(x):
    return np.asarray(x).astype(np.float64)


def striped(idx):
    return np.tile(idx.reshape(-1, 16).T, (8, 1)).astype(np.uint16)


def unstriped(offs):
    return offs[:16].T.reshape(-1).astype(np.int64)


E2M1 = np.array([0.0, 0.5, 1.0, 1.5, 2.0, 3.0, 4.0, 6.0, -0.0, -0.5, -1.0, -1.5, -2.0, -3.0, -4.0, -6.0])


def pack_weight(w, fmt):
    k, n = w.shape
    w = f64(np.asarray(w, np.float32).astype(ml_dtypes.bfloat16)).reshape(k // 32, 32, n)
    amax = np.abs(w).max(1)
    if fmt == "e4m3":
        byte = np.frexp(amax)[1] - 1 + 127 - 7
    else:
        mant, ex = np.frexp(amax / 6.0)
        byte = np.where(mant > 0.5, ex, ex - 1) + 127
    byte = np.clip(np.where(amax > 0, byte, 1), 1, 254)
    scaled = (w * np.exp2(127.0 - byte)[:, None, :]).reshape(k, n).astype(np.float32)
    by_word = np.ascontiguousarray(scaled.reshape(k // 512, 128, 4, n).transpose(0, 1, 3, 2))
    if fmt == "e4m3":
        words = by_word.astype(ml_dtypes.float8_e4m3fn).view(np.uint8)
    else:
        c = by_word.astype(ml_dtypes.float4_e2m1fn).view(np.uint8) & 0xF
        words = (c[..., 0::2] | (c[..., 1::2] << 4)).reshape(k // 512, 128, 2 * n)
    return np.ascontiguousarray(words), np.ascontiguousarray(byte.astype(np.uint8).reshape(k // 512, 16, n))


def unpack_weight(words, scales, fmt):
    g, _, n = scales.shape
    words = np.ascontiguousarray(words).reshape(g, 128, n, -1)
    if fmt == "e4m3":
        vals = words.view(ml_dtypes.float8_e4m3fn).astype(np.float64)
    else:
        nib = np.empty((g, 128, n, 4), np.uint8)
        nib[..., 0::2] = words & 0xF
        nib[..., 1::2] = words >> 4
        vals = E2M1[nib]
    vals = vals * np.repeat(np.exp2(scales.astype(np.float64) - 127.0), 8, axis=1)[..., None]
    return vals.transpose(0, 1, 3, 2).reshape(g * 512, n)


def gelu(v):
    return 0.5 * v * (1.0 + np.tanh(np.sqrt(2.0 / np.pi) * (v + 0.044715 * v**3)))


T, S, T2, K, H = 2048, 1024, 2048, 512, 1024

def setup_inputs():
    n = np.random.standard_normal
    s = mx_kscale(K)[:, None]
    u = mx_kscale(H)[:, None]
    tab_words, tab_scales = pack_weight(n((K, T)) * s, "e4m3")
    xT = (np.round(16 * n((K, T2))) / 16 * s).astype(np.float32)
    w1_words, w1_scales = pack_weight(n((K, H)) / np.sqrt(K) / s * u.T, "e2m1")
    w2 = (n((K, H)) / np.sqrt(K) / s).astype(np.float32)
    b2 = (0.5 * n(H)).astype(np.float32)
    w3_words, w3_scales = pack_weight(1.5 * n((H, H)) / np.sqrt(H) / u, "e4m3")
    res = (0.5 * np.exp(0.3 * n(H)) / u[:, 0]).astype(np.float32)
    return {"tab_words": tab_words, "tab_scales": tab_scales,
            "offs": striped(np.random.permutation(T)[:S]),
            "xT": xT,
            "offs2": striped(np.random.permutation(T2)[:S]),
            "offs3": striped(np.random.permutation(T2)[:S]),
            "w1_words": w1_words, "w1_scales": w1_scales,
            "w2": w2, "b2": b2,
            "w3_words": w3_words, "w3_scales": w3_scales, "res": res}

def reference(tab_words, tab_scales, offs, xT, offs2, offs3, w1_words, w1_scales, w2, b2, w3_words, w3_scales, res):
    v = unpack_weight(tab_words, tab_scales, "e4m3")[:, unstriped(offs)]
    x = f64(xT)[:, unstriped(offs2)] - f64(xT)[:, unstriped(offs3)]
    a = unpack_weight(w1_words, w1_scales, "e2m1").T @ v
    d = mxq(f64(w2), 0, "e4m3").T @ mxq(x, 0, "e4m3")
    gate = 1.0 / (1.0 + np.exp(-(d + f64(b2)[:, None])))
    h = a * gate
    y = unpack_weight(w3_words, w3_scales, "e4m3").T @ mxq(h, 0, "e4m3")
    return y + f64(res)[:, None] * a

@@ -1,0 +1,255 @@
+from contextlib import ExitStack
+
+import concourse.mybir as mybir
+
+T, S, K, H = 2048, 1024, 512, 1024
+FLOPS = 2 * S * (2 * K * H + H * H)
+
+F32 = mybir.dt.float32
+BF16 = mybir.dt.bfloat16
+I32 = mybir.dt.int32
+U32 = mybir.dt.uint32
+U16 = mybir.dt.uint16
+U8 = mybir.dt.uint8
+FP8X4 = mybir.dt.float8_e4m3fn_x4
+FP4X4 = mybir.dt.float4_e2m1fn_x4
+ALU = mybir.AluOpType
+ACT = mybir.ActivationFunctionType
+
+P = 128
+PACK = 4
+PASS = P * PACK
+HALVES = H // PASS
+CHUNK = 512
+LIST_COLS = CHUNK // 16
+
+
+def tile_list_cyclone_intensification_guidance_kernel(
+    tc, tab_words, tab_scales, offs, xT, offs2, offs3, w1_words, w1_scales, w2, b2, w3_words, w3_scales, res, out
+):
+    nc = tc.nc
+    with ExitStack() as ctx:
+        keep = ctx.enter_context(tc.tile_pool(name="keep", bufs=1))
+        work = ctx.enter_context(tc.tile_pool(name="work", bufs=2))
+        outs = ctx.enter_context(tc.tile_pool(name="outs", bufs=6))
+        ps_a = ctx.enter_context(tc.psum_pool(name="ps_a", bufs=2))
+        ps_d = ctx.enter_context(tc.psum_pool(name="ps_d", bufs=2))
+        ps_y = ctx.enter_context(tc.psum_pool(name="ps_y", bufs=4))
+
+        list_tab = keep.tile([P, S // 16], U16, name="list_tab")
+        list_late = keep.tile([P, S // 16], U16, name="list_late")
+        list_early = keep.tile([P, S // 16], U16, name="list_early")
+        tabw = keep.tile([P, T], U32, name="tabw", align_bytes=64)
+        tabs = keep.tile([P, T], U8, name="tabs", align_bytes=64)
+        w1_raw = keep.tile([P, 2 * H], U8, name="w1_raw", align_bytes=64)
+        ws_raw = keep.tile([P, H], U8, name="ws_raw", align_bytes=64)
+        w3_raw = keep.tile([P, HALVES * H], U32, name="w3_raw", align_bytes=64)
+        planes = [keep.tile([P, T], F32, name="plane%d" % t) for t in range(PACK)]
+        w2_raw = [keep.tile([P, PACK, PASS], F32, name="w2_raw%d" % b) for b in range(HALVES)]
+        bias = keep.tile([P, HALVES, PACK], F32, name="bias")
+        gain = keep.tile([P, HALVES, PACK], F32, name="gain")
+        warm = keep.tile([P, 2], F32, name="warm")
+
+        vs = keep.tile([P, S], U8, name="vs", align_bytes=64)
+        nc.vector.memset(tabs[:].bitcast(I32), 0)
+        nc.gpsimd.memset(ws_raw[:].bitcast(I32), 0)
+        nc.gpsimd.memset(vs[:].bitcast(I32), 0)
+        nc.gpsimd.memset(warm[:, 0:1], 0.0)
+
+        x_rows = xT.rearrange("(p t) c -> t p c", t=PACK)
+        w2_rows = w2.rearrange("(p j) c -> p j c", j=PACK)
+        nc.sync.dma_start(list_tab[:], offs)
+        nc.scalar.dma_start(tabs[0:16, :].bitcast(I32), tab_scales[0].bitcast(I32))
+        nc.sync.dma_start(tabw[:].bitcast(I32), tab_words[0].rearrange("p c i -> p (c i)").bitcast(I32))
+        nc.sync.dma_start(w1_raw[:].bitcast(I32), w1_words[0].bitcast(I32))
+        nc.sync.dma_start(planes[0][:], x_rows[0])
+        for q in range(4):
+            nc.scalar.dma_start(ws_raw[32 * q : 32 * q + 4, :].bitcast(I32), w1_scales[0, 4 * q : 4 * q + 4, :].bitcast(I32))
+            nc.scalar.dma_start(ws_raw[32 * q + 4 : 32 * q + 12, :].bitcast(I32), w3_scales[:, 4 * q : 4 * q + 4, :].bitcast(I32))
+        nc.scalar.activation(warm[:, 1:2], warm[:, 0:1], ACT.Sigmoid)
+        nc.sync.dma_start(list_early[:], offs3)
+        nc.sync.dma_start(list_late[:], offs2)
+        nc.sync.dma_start(w2_raw[0][:], w2_rows[:, :, 0:PASS])
+        nc.sync.dma_start(planes[1][:], x_rows[1])
+        nc.sync.dma_start(planes[2][:], x_rows[2])
+        nc.sync.dma_start(w2_raw[1][:], w2_rows[:, :, PASS : 2 * PASS])
+        nc.sync.dma_start(planes[3][:], x_rows[3])
+        nc.sync.dma_start(bias[:], b2.rearrange("(b p t) -> p b t", b=HALVES, t=PACK))
+        nc.sync.dma_start(gain[:], res.rearrange("(b p t) -> p b t", b=HALVES, t=PACK))
+        nc.sync.dma_start(
+            w3_raw[:].bitcast(I32).rearrange("p (a c) -> p a c", a=HALVES),
+            w3_words.rearrange("a p c i -> p a (c i)").bitcast(I32),
+        )
+
+        vw = keep.tile([P, S], U32, name="vw", align_bytes=64)
+        vs_rows = keep.tile([P, S], U8, name="vs_rows", align_bytes=64)
+        nc.vector.tensor_copy(vs_rows[:], tabs[:].indirect(list_tab[:]))
+        nc.vector.tensor_copy(vw[:], tabw[:].indirect(list_tab[:]))
+        for q in range(4):
+            nc.scalar.dma_start(vs[32 * q : 32 * q + 4, :].bitcast(I32), vs_rows[4 * q : 4 * q + 4, :].bitcast(I32))
+
+        w1p = keep.tile([P, 2 * H], U8, name="w1p", align_bytes=64)
+        nc.vector.tensor_copy(
+            w1p[:].bitcast(U16).rearrange("p (b t c i) -> p b c t i", b=HALVES, t=PACK, i=8),
+            w1_raw[:].bitcast(U16).rearrange("p (b c i t) -> p b c t i", b=HALVES, t=PACK, i=8),
+        )
+        wsp = keep.tile([P, H], U8, name="wsp", align_bytes=64)
+        w3p = keep.tile([P, HALVES * H], U32, name="w3p", align_bytes=64)
+
+        def list_cols(c):
+            return slice(c * LIST_COLS, (c + 1) * LIST_COLS)
+
+        def gather_early(c, t, tag):
+            early = keep.tile([P, CHUNK], F32, name="early", tag=tag, align_bytes=64)
+            nc.vector.tensor_copy(early[:], planes[t][:].indirect(list_early[:, list_cols(c)]))
+            return early
+
+        def gather_change(diff, c, t, early):
+            nc.vector.tensor_tensor(diff[:, t, :], planes[t][:].indirect(list_late[:, list_cols(c)]), early[:], ALU.subtract)
+
+        def weave_x(diff, tag):
+            x_bf = keep.tile([P, CHUNK * PACK], BF16, name="x_bf", tag=tag, align_bytes=64)
+            nc.scalar.copy(
+                x_bf[:].rearrange("p (c i t) -> p c t i", i=2, t=PACK),
+                diff[:].rearrange("p t (c i) -> p c t i", i=2),
+            )
+            return x_bf
+
+        def quantise(src, name):
+            codes = keep.tile([P, PASS], U32, name="codes", tag=name + "_codes", align_bytes=64)
+            scales = keep.tile([P, PASS], U8, name="scales", tag=name + "_scales", align_bytes=64)
+            nc.vector.quantize_mx(out=codes[:].bitcast(FP8X4), scales=scales[:], in_=src[:])
+            return codes, scales
+
+        def weave_w2(b):
+            w2_bf = keep.tile([P, PASS * PACK], BF16, name="w2_bf", tag="hold_w2_%d" % b, align_bytes=64)
+            nc.scalar.copy(
+                w2_bf[:].rearrange("p (u e m j) -> p u m j e", u=2, e=2, j=PACK),
+                w2_raw[b][:].rearrange("p j (m u e) -> p u m j e", u=2, e=2),
+            )
+            return w2_bf
+
+        def memory_product(c, b, tag):
+            a_sb = keep.tile([P, PACK, CHUNK], F32, name="a_sb", tag=tag)
+            for t in range(PACK):
+                m0 = (b * PACK + t) * P
+                acc = ps_a.tile([P, CHUNK], F32, name="acc_a")
+                nc.tensor.matmul_mx(
+                    out=acc[:],
+                    lhsT=w1p[:, 2 * m0 : 2 * (m0 + P)].bitcast(FP4X4),
+                    lhsT_scale=wsp[:, m0 : m0 + P],
+                    rhs=vw[:, c * CHUNK : (c + 1) * CHUNK].bitcast(FP8X4),
+                    rhs_scale=vs[:, c * CHUNK : (c + 1) * CHUNK],
+                    start=True,
+                    stop=True,
+                )
+                nc.scalar.copy(a_sb[:, t, :], acc[:])
+            return a_sb
+
+        def frame_gate(b, w2q, xq):
+            gate = work.tile([P, PACK, CHUNK], F32, name="gate")
+            for t in range(PACK):
+                acc = ps_d.tile([P, CHUNK], F32, name="acc_d")
+                nc.tensor.matmul_mx(
+                    out=acc[:],
+                    lhsT=w2q[0][:, t * P : (t + 1) * P].bitcast(FP8X4),
+                    lhsT_scale=w2q[1][:, t * P : (t + 1) * P],
+                    rhs=xq[0][:].bitcast(FP8X4),
+                    rhs_scale=xq[1][:],
+                    start=True,
+                    stop=True,
+                )
+                nc.scalar.activation(gate[:, t, :], acc[:], ACT.Sigmoid, bias=bias[:, b, t : t + 1])
+            return gate
+
+        def gated(a_sb, gate, tag):
+            h_bf = keep.tile([P, CHUNK * PACK], BF16, name="h_bf", tag=tag, align_bytes=64)
+            nc.vector.tensor_tensor(
+                h_bf[:].rearrange("p (c i t) -> p c t i", i=2, t=PACK),
+                a_sb[:].rearrange("p t (c i) -> p c t i", i=2),
+                gate[:].rearrange("p t (c i) -> p c t i", i=2),
+                ALU.mult,
+            )
+            return h_bf
+
+        out_rows = out.rearrange("(b p t) j -> b t p j", b=HALVES, t=PACK)
+
+        def finish(c, b, t, a_sb, hq, tag=None):
+            m0 = (b * PACK + t) * P
+            acc = ps_y.tile([P, CHUNK], F32, name="acc_y")
+            for g in range(HALVES):
+                nc.tensor.matmul_mx(
+                    out=acc[:],
+                    lhsT=w3p[:, g * H + m0 : g * H + m0 + P].bitcast(FP8X4),
+                    lhsT_scale=wsp[4 + 4 * g : P, m0 : m0 + P],
+                    rhs=hq[g][0][:].bitcast(FP8X4),
+                    rhs_scale=hq[g][1][:],
+                    start=(g == 0),
+                    stop=(g == HALVES - 1),
+                )
+            if tag is None:
+                result = outs.tile([P, CHUNK], F32, name="result")
+            else:
+                result = keep.tile([P, CHUNK], F32, name="result_late", tag=tag, align_bytes=64)
+            nc.vector.scalar_tensor_tensor(result[:], a_sb[:, t, :], gain[:, b, t : t + 1], acc[:], ALU.mult, ALU.add)
+            nc.sync.dma_start(out_rows[b, t][:, c * CHUNK : (c + 1) * CHUNK], result[:])
+
+        nc.vector.tensor_copy(
+            wsp[:].rearrange("p (b t c i) -> p b c t i", b=HALVES, t=PACK, i=16),
+            ws_raw[:].rearrange("p (b c i t) -> p b c t i", b=HALVES, t=PACK, i=16),
+        )
+        w2_bf0 = weave_w2(0)
+        a0 = [memory_product(0, b, "a0_%d" % b) for b in range(HALVES)]
+        w2_bf1 = weave_w2(1)
+
+        diff0 = keep.tile([P, PACK, CHUNK], F32, name="diff0", tag="diff0", align_bytes=64)
+        early1 = []
+        for t in range(2):
+            early = gather_early(0, t, "early0_%d" % t)
+            early1.append(gather_early(1, t, "early1_%d" % t))
+            gather_change(diff0, 0, t, early)
+        early = gather_early(0, 2, "early0_0")
+        w2q0 = quantise(w2_bf0, "w2q0")
+        gather_change(diff0, 0, 2, early)
+        early = gather_early(0, 3, "diff1")
+        w2q1 = quantise(w2_bf1, "w2q1")
+        gather_change(diff0, 0, 3, early)
+        x_bf0 = weave_x(diff0, "x_bf0")
+
+        diff1 = keep.tile([P, PACK, CHUNK], F32, name="diff1", tag="diff1", align_bytes=64)
+        for t in range(2):
+            gather_change(diff1, 1, t, early1[t])
+        nc.vector.tensor_copy(
+            w3p[:].rearrange("p (g t c i) -> p g c t i", g=HALVES * HALVES, t=PACK, i=4),
+            w3_raw[:].rearrange("p (g c i t) -> p g c t i", g=HALVES * HALVES, t=PACK, i=4),
+        )
+        xq0 = quantise(x_bf0, "xq0")
+        gate00 = frame_gate(0, w2q0, xq0)
+        gate01 = frame_gate(1, w2q1, xq0)
+        early1.append(gather_early(1, 2, "x_bf0"))
+        early1.append(gather_early(1, 3, "diff0"))
+        for t in range(2, 4):
+            gather_change(diff1, 1, t, early1[t])
+        x_bf1 = weave_x(diff1, "xq0_codes")
+
+        h00 = gated(a0[0], gate00, "h0")
+        h01 = gated(a0[1], gate01, "h1")
+        xq1 = quantise(x_bf1, "xq1")
+        hq0 = [quantise(h00, "hq00"), quantise(h01, "hq01")]
+        a10 = memory_product(1, 0, "a1_0")
+        gate10 = frame_gate(0, w2q0, xq1)
+        a11 = memory_product(1, 1, "a1_1")
+        gate11 = frame_gate(1, w2q1, xq1)
+        a1 = [a10, a11]
+        for b in range(HALVES):
+            for t in range(PACK):
+                if (b, t) < (1, 2):
+                    finish(0, b, t, a0[b], hq0)
+        h10 = gated(a1[0], gate10, "h0")
+        h11 = gated(a1[1], gate11, "h1")
+        hq1 = [quantise(h10, "hq10"), quantise(h11, "hq11")]
+        finish(0, 1, 2, a0[1], hq0, "h1")
+        finish(0, 1, 3, a0[1], hq0, "h0")
+        for b in range(HALVES):
+            for t in range(PACK):
+                finish(1, b, t, a1[b], hq1)

@@ -22,6 +22,12 @@ PASS = P * PACK
 HALVES = H // PASS
 CHUNK = 512
 LIST_COLS = CHUNK // 16
+QUADRANTS = 4
+SCALE_ROWS = 16
+LINE = 16
+FIRST_BANKS = 4
+LAST_BANKS = 4
+PLAIN_RESULTS = 13
 
 
 def tile_list_cyclone_intensification_guidance_kernel(
@@ -30,71 +36,69 @@ def tile_list_cyclone_intensification_guidance_kernel(
     nc = tc.nc
     with ExitStack() as ctx:
         keep = ctx.enter_context(tc.tile_pool(name="keep", bufs=1))
-        work = ctx.enter_context(tc.tile_pool(name="work", bufs=2))
-        outs = ctx.enter_context(tc.tile_pool(name="outs", bufs=6))
-        ps_a = ctx.enter_context(tc.psum_pool(name="ps_a", bufs=2))
-        ps_d = ctx.enter_context(tc.psum_pool(name="ps_d", bufs=2))
-        ps_y = ctx.enter_context(tc.psum_pool(name="ps_y", bufs=4))
+        outs = ctx.enter_context(tc.tile_pool(name="outs", bufs=PLAIN_RESULTS))
+        ps_first = ctx.enter_context(tc.psum_pool(name="ps_first", bufs=FIRST_BANKS))
+        ps_last = ctx.enter_context(tc.psum_pool(name="ps_last", bufs=LAST_BANKS))
 
         list_tab = keep.tile([P, S // 16], U16, name="list_tab")
         list_late = keep.tile([P, S // 16], U16, name="list_late")
         list_early = keep.tile([P, S // 16], U16, name="list_early")
-        tabw = keep.tile([P, T], U32, name="tabw", align_bytes=64)
-        tabs = keep.tile([P, T], U8, name="tabs", align_bytes=64)
+        tab_w = keep.tile([P, T], U32, name="tab_w", align_bytes=64)
+        tab_s = keep.tile([P, T], U8, name="tab_s", align_bytes=64)
         w1_raw = keep.tile([P, 2 * H], U8, name="w1_raw", align_bytes=64)
         ws_raw = keep.tile([P, H], U8, name="ws_raw", align_bytes=64)
         w3_raw = keep.tile([P, HALVES * H], U32, name="w3_raw", align_bytes=64)
         planes = [keep.tile([P, T], F32, name="plane%d" % t) for t in range(PACK)]
-        w2_raw = [keep.tile([P, PACK, PASS], F32, name="w2_raw%d" % b) for b in range(HALVES)]
+        w2_raw = [
+            keep.tile([P, PACK, PASS], F32, name="w2_raw", tag="w2_raw%d" % b, align_bytes=64) for b in range(HALVES)
+        ]
         bias = keep.tile([P, HALVES, PACK], F32, name="bias")
         gain = keep.tile([P, HALVES, PACK], F32, name="gain")
-        warm = keep.tile([P, 2], F32, name="warm")
+        v_s = keep.tile([P, S], U8, name="v_s", align_bytes=64)
 
-        vs = keep.tile([P, S], U8, name="vs", align_bytes=64)
-        nc.vector.memset(tabs[:].bitcast(I32), 0)
+        nc.vector.memset(tab_s[:].bitcast(I32), 0)
         nc.gpsimd.memset(ws_raw[:].bitcast(I32), 0)
-        nc.gpsimd.memset(vs[:].bitcast(I32), 0)
-        nc.gpsimd.memset(warm[:, 0:1], 0.0)
+        nc.gpsimd.memset(v_s[:].bitcast(I32), 0)
 
         x_rows = xT.rearrange("(p t) c -> t p c", t=PACK)
         w2_rows = w2.rearrange("(p j) c -> p j c", j=PACK)
         nc.sync.dma_start(list_tab[:], offs)
-        nc.scalar.dma_start(tabs[0:16, :].bitcast(I32), tab_scales[0].bitcast(I32))
-        nc.sync.dma_start(tabw[:].bitcast(I32), tab_words[0].rearrange("p c i -> p (c i)").bitcast(I32))
+        nc.scalar.dma_start(tab_s[0:SCALE_ROWS, :].bitcast(I32), tab_scales[0].bitcast(I32))
+        nc.sync.dma_start(tab_w[:].bitcast(I32), tab_words[0].rearrange("p c i -> p (c i)").bitcast(I32))
         nc.sync.dma_start(w1_raw[:].bitcast(I32), w1_words[0].bitcast(I32))
         nc.sync.dma_start(planes[0][:], x_rows[0])
-        for q in range(4):
-            nc.scalar.dma_start(ws_raw[32 * q : 32 * q + 4, :].bitcast(I32), w1_scales[0, 4 * q : 4 * q + 4, :].bitcast(I32))
-            nc.scalar.dma_start(ws_raw[32 * q + 4 : 32 * q + 12, :].bitcast(I32), w3_scales[:, 4 * q : 4 * q + 4, :].bitcast(I32))
-        nc.scalar.activation(warm[:, 1:2], warm[:, 0:1], ACT.Sigmoid)
+        for q in range(QUADRANTS):
+            rows = slice(4 * q, 4 * q + 4)
+            nc.scalar.dma_start(ws_raw[32 * q : 32 * q + 4, :].bitcast(I32), w1_scales[0, rows, :].bitcast(I32))
+            nc.scalar.dma_start(ws_raw[32 * q + 4 : 32 * q + 12, :].bitcast(I32), w3_scales[:, rows, :].bitcast(I32))
         nc.sync.dma_start(list_early[:], offs3)
         nc.sync.dma_start(list_late[:], offs2)
         nc.sync.dma_start(w2_raw[0][:], w2_rows[:, :, 0:PASS])
         nc.sync.dma_start(planes[1][:], x_rows[1])
-        nc.sync.dma_start(planes[2][:], x_rows[2])
         nc.sync.dma_start(w2_raw[1][:], w2_rows[:, :, PASS : 2 * PASS])
+        nc.sync.dma_start(planes[2][:], x_rows[2])
         nc.sync.dma_start(planes[3][:], x_rows[3])
         nc.sync.dma_start(bias[:], b2.rearrange("(b p t) -> p b t", b=HALVES, t=PACK))
         nc.sync.dma_start(gain[:], res.rearrange("(b p t) -> p b t", b=HALVES, t=PACK))
         nc.sync.dma_start(
-            w3_raw[:].bitcast(I32).rearrange("p (a c) -> p a c", a=HALVES),
-            w3_words.rearrange("a p c i -> p a (c i)").bitcast(I32),
+            w3_raw[:].bitcast(I32).rearrange("p (g c) -> p g c", g=HALVES),
+            w3_words.rearrange("g p c i -> p g (c i)").bitcast(I32),
         )
 
-        vw = keep.tile([P, S], U32, name="vw", align_bytes=64)
-        vs_rows = keep.tile([P, S], U8, name="vs_rows", align_bytes=64)
-        nc.vector.tensor_copy(vs_rows[:], tabs[:].indirect(list_tab[:]))
-        nc.vector.tensor_copy(vw[:], tabw[:].indirect(list_tab[:]))
-        for q in range(4):
-            nc.scalar.dma_start(vs[32 * q : 32 * q + 4, :].bitcast(I32), vs_rows[4 * q : 4 * q + 4, :].bitcast(I32))
+        v_w = keep.tile([P, S], U32, name="v_w", align_bytes=64)
+        v_s_rows = keep.tile([P, S], U8, name="v_s_rows", align_bytes=64)
+        nc.vector.tensor_copy(v_s_rows[:], tab_s[:].indirect(list_tab[:]))
+        nc.vector.tensor_copy(v_w[:], tab_w[:].indirect(list_tab[:]))
+        for q in range(QUADRANTS):
+            nc.scalar.dma_start(
+                v_s[32 * q : 32 * q + 4, :].bitcast(I32), v_s_rows[4 * q : 4 * q + 4, :].bitcast(I32)
+            )
 
-        w1p = keep.tile([P, 2 * H], U8, name="w1p", align_bytes=64)
-        nc.vector.tensor_copy(
-            w1p[:].bitcast(U16).rearrange("p (b t c i) -> p b c t i", b=HALVES, t=PACK, i=8),
-            w1_raw[:].bitcast(U16).rearrange("p (b c i t) -> p b c t i", b=HALVES, t=PACK, i=8),
-        )
-        wsp = keep.tile([P, H], U8, name="wsp", align_bytes=64)
-        w3p = keep.tile([P, HALVES * H], U32, name="w3p", align_bytes=64)
+        def reorder_columns(dst, src, groups, per_line):
+            nc.vector.tensor_copy(
+                dst.rearrange("p (g t c i) -> p g c t i", g=groups, t=PACK, i=per_line),
+                src.rearrange("p (g c i t) -> p g c t i", g=groups, t=PACK, i=per_line),
+            )
 
         def list_cols(c):
             return slice(c * LIST_COLS, (c + 1) * LIST_COLS)
@@ -105,7 +109,8 @@ def tile_list_cyclone_intensification_guidance_kernel(
             return early
 
         def gather_change(diff, c, t, early):
-            nc.vector.tensor_tensor(diff[:, t, :], planes[t][:].indirect(list_late[:, list_cols(c)]), early[:], ALU.subtract)
+            late = planes[t][:].indirect(list_late[:, list_cols(c)])
+            nc.vector.tensor_tensor(diff[:, t, :], late, early[:], ALU.subtract)
 
         def weave_x(diff, tag):
             x_bf = keep.tile([P, CHUNK * PACK], BF16, name="x_bf", tag=tag, align_bytes=64)
@@ -115,47 +120,47 @@ def tile_list_cyclone_intensification_guidance_kernel(
             )
             return x_bf
 
-        def quantise(src, name):
-            codes = keep.tile([P, PASS], U32, name="codes", tag=name + "_codes", align_bytes=64)
-            scales = keep.tile([P, PASS], U8, name="scales", tag=name + "_scales", align_bytes=64)
-            nc.vector.quantize_mx(out=codes[:].bitcast(FP8X4), scales=scales[:], in_=src[:])
-            return codes, scales
-
         def weave_w2(b):
-            w2_bf = keep.tile([P, PASS * PACK], BF16, name="w2_bf", tag="hold_w2_%d" % b, align_bytes=64)
+            w2_bf = keep.tile([P, PASS * PACK], BF16, name="w2_bf", tag="w2_bf%d" % b, align_bytes=64)
             nc.scalar.copy(
                 w2_bf[:].rearrange("p (u e m j) -> p u m j e", u=2, e=2, j=PACK),
                 w2_raw[b][:].rearrange("p j (m u e) -> p u m j e", u=2, e=2),
             )
             return w2_bf
 
+        def quantise(src, name, tag=None):
+            codes = keep.tile([P, PASS], U32, name="codes", tag=tag or name + "_codes", align_bytes=64)
+            scales = keep.tile([P, PASS], U8, name="scales", tag=name + "_scales", align_bytes=64)
+            nc.vector.quantize_mx(out=codes[:].bitcast(FP8X4), scales=scales[:], in_=src[:])
+            return codes, scales
+
         def memory_product(c, b, tag):
-            a_sb = keep.tile([P, PACK, CHUNK], F32, name="a_sb", tag=tag)
+            a_sb = keep.tile([P, PACK, CHUNK], F32, name="a_sb", tag=tag, align_bytes=64)
             for t in range(PACK):
                 m0 = (b * PACK + t) * P
-                acc = ps_a.tile([P, CHUNK], F32, name="acc_a")
+                acc = ps_first.tile([P, CHUNK], F32, name="acc_first")
                 nc.tensor.matmul_mx(
                     out=acc[:],
-                    lhsT=w1p[:, 2 * m0 : 2 * (m0 + P)].bitcast(FP4X4),
-                    lhsT_scale=wsp[:, m0 : m0 + P],
-                    rhs=vw[:, c * CHUNK : (c + 1) * CHUNK].bitcast(FP8X4),
-                    rhs_scale=vs[:, c * CHUNK : (c + 1) * CHUNK],
+                    lhsT=w1_w[:, 2 * m0 : 2 * (m0 + P)].bitcast(FP4X4),
+                    lhsT_scale=w_s[:, m0 : m0 + P],
+                    rhs=v_w[:, c * CHUNK : (c + 1) * CHUNK].bitcast(FP8X4),
+                    rhs_scale=v_s[:, c * CHUNK : (c + 1) * CHUNK],
                     start=True,
                     stop=True,
                 )
                 nc.scalar.copy(a_sb[:, t, :], acc[:])
             return a_sb
 
-        def frame_gate(b, w2q, xq):
-            gate = work.tile([P, PACK, CHUNK], F32, name="gate")
+        def frame_gate(b, w2_q, x_q, tag):
+            gate = keep.tile([P, PACK, CHUNK], F32, name="gate", tag=tag, align_bytes=64)
             for t in range(PACK):
-                acc = ps_d.tile([P, CHUNK], F32, name="acc_d")
+                acc = ps_first.tile([P, CHUNK], F32, name="acc_first")
                 nc.tensor.matmul_mx(
                     out=acc[:],
-                    lhsT=w2q[0][:, t * P : (t + 1) * P].bitcast(FP8X4),
-                    lhsT_scale=w2q[1][:, t * P : (t + 1) * P],
-                    rhs=xq[0][:].bitcast(FP8X4),
-                    rhs_scale=xq[1][:],
+                    lhsT=w2_q[0][:, t * P : (t + 1) * P].bitcast(FP8X4),
+                    lhsT_scale=w2_q[1][:, t * P : (t + 1) * P],
+                    rhs=x_q[0][:].bitcast(FP8X4),
+                    rhs_scale=x_q[1][:],
                     start=True,
                     stop=True,
                 )
@@ -174,16 +179,19 @@ def tile_list_cyclone_intensification_guidance_kernel(
 
         out_rows = out.rearrange("(b p t) j -> b t p j", b=HALVES, t=PACK)
 
-        def finish(c, b, t, a_sb, hq, tag=None):
+        def finish(c, b, t, a_sb, h_q, tag=None):
             m0 = (b * PACK + t) * P
-            acc = ps_y.tile([P, CHUNK], F32, name="acc_y")
+            if (c, b) == (1, 0):
+                acc = ps_first.tile([P, CHUNK], F32, name="acc_first")
+            else:
+                acc = ps_last.tile([P, CHUNK], F32, name="acc_last")
             for g in range(HALVES):
                 nc.tensor.matmul_mx(
                     out=acc[:],
-                    lhsT=w3p[:, g * H + m0 : g * H + m0 + P].bitcast(FP8X4),
-                    lhsT_scale=wsp[4 + 4 * g : P, m0 : m0 + P],
-                    rhs=hq[g][0][:].bitcast(FP8X4),
-                    rhs_scale=hq[g][1][:],
+                    lhsT=w3_w[:, g * H + m0 : g * H + m0 + P].bitcast(FP8X4),
+                    lhsT_scale=w_s[4 + 4 * g : P, m0 : m0 + P],
+                    rhs=h_q[g][0][:].bitcast(FP8X4),
+                    rhs_scale=h_q[g][1][:],
                     start=(g == 0),
                     stop=(g == HALVES - 1),
                 )
@@ -194,13 +202,14 @@ def tile_list_cyclone_intensification_guidance_kernel(
             nc.vector.scalar_tensor_tensor(result[:], a_sb[:, t, :], gain[:, b, t : t + 1], acc[:], ALU.mult, ALU.add)
             nc.sync.dma_start(out_rows[b, t][:, c * CHUNK : (c + 1) * CHUNK], result[:])
 
-        nc.vector.tensor_copy(
-            wsp[:].rearrange("p (b t c i) -> p b c t i", b=HALVES, t=PACK, i=16),
-            ws_raw[:].rearrange("p (b c i t) -> p b c t i", b=HALVES, t=PACK, i=16),
-        )
+        w1_w = keep.tile([P, 2 * H], U8, name="w1_w", align_bytes=64)
+        reorder_columns(w1_w[:].bitcast(U16), w1_raw[:].bitcast(U16), HALVES, LINE // 2)
+        w_s = keep.tile([P, H], U8, name="w_s", align_bytes=64)
+        reorder_columns(w_s[:], ws_raw[:], HALVES, LINE)
+
         w2_bf0 = weave_w2(0)
-        a0 = [memory_product(0, b, "a0_%d" % b) for b in range(HALVES)]
         w2_bf1 = weave_w2(1)
+        a0 = [memory_product(0, 0, "w2_raw1"), memory_product(0, 1, "w2_raw0")]
 
         diff0 = keep.tile([P, PACK, CHUNK], F32, name="diff0", tag="diff0", align_bytes=64)
         early1 = []
@@ -208,48 +217,51 @@ def tile_list_cyclone_intensification_guidance_kernel(
             early = gather_early(0, t, "early0_%d" % t)
             early1.append(gather_early(1, t, "early1_%d" % t))
             gather_change(diff0, 0, t, early)
-        early = gather_early(0, 2, "early0_0")
-        w2q0 = quantise(w2_bf0, "w2q0")
-        gather_change(diff0, 0, 2, early)
-        early = gather_early(0, 3, "diff1")
-        w2q1 = quantise(w2_bf1, "w2q1")
-        gather_change(diff0, 0, 3, early)
+        early02 = gather_early(0, 2, "early0_0")
+        early03 = gather_early(0, 3, "diff1")
+        gather_change(diff0, 0, 2, early02)
+        gather_change(diff0, 0, 3, early03)
         x_bf0 = weave_x(diff0, "x_bf0")
 
         diff1 = keep.tile([P, PACK, CHUNK], F32, name="diff1", tag="diff1", align_bytes=64)
-        for t in range(2):
-            gather_change(diff1, 1, t, early1[t])
-        nc.vector.tensor_copy(
-            w3p[:].rearrange("p (g t c i) -> p g c t i", g=HALVES * HALVES, t=PACK, i=4),
-            w3_raw[:].rearrange("p (g c i t) -> p g c t i", g=HALVES * HALVES, t=PACK, i=4),
-        )
-        xq0 = quantise(x_bf0, "xq0")
-        gate00 = frame_gate(0, w2q0, xq0)
-        gate01 = frame_gate(1, w2q1, xq0)
-        early1.append(gather_early(1, 2, "x_bf0"))
-        early1.append(gather_early(1, 3, "diff0"))
-        for t in range(2, 4):
-            gather_change(diff1, 1, t, early1[t])
-        x_bf1 = weave_x(diff1, "xq0_codes")
+        gather_change(diff1, 1, 0, early1[0])
+        w2_q0 = quantise(w2_bf0, "w2_q0", "early1_0")
+        gather_change(diff1, 1, 1, early1[1])
+        w2_q1 = quantise(w2_bf1, "w2_q1", "early1_1")
+        x_q0 = quantise(x_bf0, "x_q0")
+
+        gate00 = frame_gate(0, w2_q0, x_q0, "gate00")
+        gate01 = frame_gate(1, w2_q1, x_q0, "gate01")
+        early12 = gather_early(1, 2, "x_bf0")
+        early13 = gather_early(1, 3, "diff0")
+        gather_change(diff1, 1, 2, early12)
+        gather_change(diff1, 1, 3, early13)
+        x_bf1 = weave_x(diff1, "x_q0_codes")
+        a1 = [memory_product(1, 0, "x_bf0"), memory_product(1, 1, "diff1")]
 
         h00 = gated(a0[0], gate00, "h0")
+        w3_w = keep.tile([P, HALVES * H], U32, name="w3_w", tag="gate00", align_bytes=64)
+        reorder_columns(w3_w[:], w3_raw[:], HALVES * HALVES, LINE // 4)
+        h_q00 = quantise(h00, "h_q00")
         h01 = gated(a0[1], gate01, "h1")
-        xq1 = quantise(x_bf1, "xq1")
-        hq0 = [quantise(h00, "hq00"), quantise(h01, "hq01")]
-        a10 = memory_product(1, 0, "a1_0")
-        gate10 = frame_gate(0, w2q0, xq1)
-        a11 = memory_product(1, 1, "a1_1")
-        gate11 = frame_gate(1, w2q1, xq1)
-        a1 = [a10, a11]
-        for b in range(HALVES):
-            for t in range(PACK):
-                if (b, t) < (1, 2):
-                    finish(0, b, t, a0[b], hq0)
+        x_q1 = quantise(x_bf1, "x_q1")
+        h_q0 = [h_q00, quantise(h01, "h_q01")]
+
+        finish(0, 0, 0, a0[0], h_q0)
+        finish(0, 0, 1, a0[0], h_q0)
+        gate10 = frame_gate(0, w2_q0, x_q1, "diff0")
+        finish(0, 0, 2, a0[0], h_q0)
+        finish(0, 0, 3, a0[0], h_q0)
+        finish(0, 1, 0, a0[1], h_q0)
+        gate11 = frame_gate(1, w2_q1, x_q1, "gate01")
+
         h10 = gated(a1[0], gate10, "h0")
+        finish(0, 1, 1, a0[1], h_q0, "diff0")
+        h_q10 = quantise(h10, "h_q10")
         h11 = gated(a1[1], gate11, "h1")
-        hq1 = [quantise(h10, "hq10"), quantise(h11, "hq11")]
-        finish(0, 1, 2, a0[1], hq0, "h1")
-        finish(0, 1, 3, a0[1], hq0, "h0")
+        finish(0, 1, 2, a0[1], h_q0, "gate01")
+        h_q1 = [h_q10, quantise(h11, "h_q11")]
+        finish(0, 1, 3, a0[1], h_q0, "h1")
         for b in range(HALVES):
             for t in range(PACK):
-                finish(1, b, t, a1[b], hq1)
+                finish(1, b, t, a1[b], h_q1)

@@ -56,14 +56,14 @@ def tile_list_cyclone_intensification_guidance_kernel(
         gain = keep.tile([P, HALVES, PACK], F32, name="gain")
         v_s = keep.tile([P, S], U8, name="v_s", align_bytes=64)
 
-        nc.vector.memset(tab_s[:].bitcast(I32), 0)
         nc.gpsimd.memset(ws_raw[:].bitcast(I32), 0)
-        nc.gpsimd.memset(v_s[:].bitcast(I32), 0)
 
         x_rows = xT.rearrange("(p t) c -> t p c", t=PACK)
         w2_rows = w2.rearrange("(p j) c -> p j c", j=PACK)
         nc.sync.dma_start(list_tab[:], offs)
-        nc.scalar.dma_start(tab_s[0:SCALE_ROWS, :].bitcast(I32), tab_scales[0].bitcast(I32))
+        for q in range(QUADRANTS):
+            rows = tab_scales[0, 4 * q : 4 * q + 4, :].bitcast(I32)
+            nc.sync.dma_start(tab_s[32 * q : 32 * q + 32, :].bitcast(I32), rows.partition_broadcast(8))
         nc.sync.dma_start(tab_w[:].bitcast(I32), tab_words[0].rearrange("p c i -> p (c i)").bitcast(I32))
         nc.sync.dma_start(w1_raw[:].bitcast(I32), w1_words[0].bitcast(I32))
         nc.sync.dma_start(planes[0][:], x_rows[0])
@@ -75,9 +75,9 @@ def tile_list_cyclone_intensification_guidance_kernel(
         nc.sync.dma_start(list_late[:], offs2)
         nc.sync.dma_start(w2_raw[0][:], w2_rows[:, :, 0:PASS])
         nc.sync.dma_start(planes[1][:], x_rows[1])
-        nc.sync.dma_start(w2_raw[1][:], w2_rows[:, :, PASS : 2 * PASS])
         nc.sync.dma_start(planes[2][:], x_rows[2])
         nc.sync.dma_start(planes[3][:], x_rows[3])
+        nc.sync.dma_start(w2_raw[1][:], w2_rows[:, :, PASS : 2 * PASS])
         nc.sync.dma_start(bias[:], b2.rearrange("(b p t) -> p b t", b=HALVES, t=PACK))
         nc.sync.dma_start(gain[:], res.rearrange("(b p t) -> p b t", b=HALVES, t=PACK))
         nc.sync.dma_start(
@@ -86,37 +86,33 @@ def tile_list_cyclone_intensification_guidance_kernel(
         )
 
         v_w = keep.tile([P, S], U32, name="v_w", align_bytes=64)
-        v_s_rows = keep.tile([P, S], U8, name="v_s_rows", align_bytes=64)
-        nc.vector.tensor_copy(v_s_rows[:], tab_s[:].indirect(list_tab[:]))
+        nc.vector.tensor_copy(v_s[:], tab_s[:].indirect(list_tab[:]))
         nc.vector.tensor_copy(v_w[:], tab_w[:].indirect(list_tab[:]))
-        for q in range(QUADRANTS):
-            nc.scalar.dma_start(
-                v_s[32 * q : 32 * q + 4, :].bitcast(I32), v_s_rows[4 * q : 4 * q + 4, :].bitcast(I32)
-            )
 
-        def reorder_columns(dst, src, groups, per_line):
-            nc.vector.tensor_copy(
-                dst.rearrange("p (g t c i) -> p g c t i", g=groups, t=PACK, i=per_line),
-                src.rearrange("p (g c i t) -> p g c t i", g=groups, t=PACK, i=per_line),
+        def deal_columns(dst, src, groups, width):
+            nc.gpsimd.tensor_copy(
+                dst.rearrange("p (g t m e) -> p g t m e", g=groups, t=PACK, e=width),
+                src.rearrange("p (g m t e) -> p g t m e", g=groups, t=PACK, e=width),
             )
 
         def list_cols(c):
             return slice(c * LIST_COLS, (c + 1) * LIST_COLS)
 
-        def gather_early(c, t, tag):
-            early = keep.tile([P, CHUNK], F32, name="early", tag=tag, align_bytes=64)
-            nc.vector.tensor_copy(early[:], planes[t][:].indirect(list_early[:, list_cols(c)]))
-            return early
+        def gather_early(c, t, early):
+            nc.vector.tensor_copy(early, planes[t][:].indirect(list_early[:, list_cols(c)]))
+
+        def early_tile(count, tag):
+            return keep.tile([P, count, CHUNK], F32, name="early", tag=tag, align_bytes=64)
 
         def gather_change(diff, c, t, early):
             late = planes[t][:].indirect(list_late[:, list_cols(c)])
-            nc.vector.tensor_tensor(diff[:, t, :], late, early[:], ALU.subtract)
+            nc.vector.tensor_tensor(diff[:, t, :], late, early, ALU.subtract)
 
         def weave_x(diff, tag):
             x_bf = keep.tile([P, CHUNK * PACK], BF16, name="x_bf", tag=tag, align_bytes=64)
             nc.scalar.copy(
                 x_bf[:].rearrange("p (c i t) -> p c t i", i=2, t=PACK),
-                diff[:].rearrange("p t (c i) -> p c t i", i=2),
+                diff.rearrange("p t (c i) -> p c t i", i=2),
             )
             return x_bf
 
@@ -203,63 +199,68 @@ def tile_list_cyclone_intensification_guidance_kernel(
             nc.sync.dma_start(out_rows[b, t][:, c * CHUNK : (c + 1) * CHUNK], result[:])
 
         w1_w = keep.tile([P, 2 * H], U8, name="w1_w", align_bytes=64)
-        reorder_columns(w1_w[:].bitcast(U16), w1_raw[:].bitcast(U16), HALVES, LINE // 2)
+        deal_columns(w1_w[:], w1_raw[:], HALVES, 2)
         w_s = keep.tile([P, H], U8, name="w_s", align_bytes=64)
-        reorder_columns(w_s[:], ws_raw[:], HALVES, LINE)
+        deal_columns(w_s[:], ws_raw[:], HALVES, 1)
 
         w2_bf0 = weave_w2(0)
+        a0 = [memory_product(0, 0, "a00"), memory_product(0, 1, "a01")]
         w2_bf1 = weave_w2(1)
-        a0 = [memory_product(0, 0, "w2_raw1"), memory_product(0, 1, "w2_raw0")]
 
-        diff0 = keep.tile([P, PACK, CHUNK], F32, name="diff0", tag="diff0", align_bytes=64)
-        early1 = []
-        for t in range(2):
-            early = gather_early(0, t, "early0_%d" % t)
-            early1.append(gather_early(1, t, "early1_%d" % t))
-            gather_change(diff0, 0, t, early)
-        early02 = gather_early(0, 2, "early0_0")
-        early03 = gather_early(0, 3, "diff1")
-        gather_change(diff0, 0, 2, early02)
-        gather_change(diff0, 0, 3, early03)
-        x_bf0 = weave_x(diff0, "x_bf0")
+        diffs = keep.tile([P, PACK + 1, CHUNK], F32, name="diffs", tag="diffs", align_bytes=64)
+        diff0 = diffs[:, 1 : PACK + 1, :]
+        diff1 = diffs[:, 0:PACK, :]
+        early = [early_tile(1, "early%d" % n) for n in range(6)]
+        gather_early(0, 0, early[0][:, 0, :])
+        gather_early(1, 0, early[1][:, 0, :])
+        gather_change(diff0, 0, 0, early[0][:, 0, :])
+        gather_change(diff1, 1, 0, early[1][:, 0, :])
+        gather_early(0, 1, early[2][:, 0, :])
+        gather_early(1, 1, early[3][:, 0, :])
+        gather_change(diff0, 0, 1, early[2][:, 0, :])
+        gather_early(0, 2, early[4][:, 0, :])
+        gather_early(0, 3, early[5][:, 0, :])
+        gather_change(diff0, 0, 2, early[4][:, 0, :])
+        gather_change(diff0, 0, 3, early[5][:, 0, :])
+        x_bf0 = weave_x(diff0, "w2_raw1")
+        a10 = memory_product(1, 0, "w2_raw0")
 
-        diff1 = keep.tile([P, PACK, CHUNK], F32, name="diff1", tag="diff1", align_bytes=64)
-        gather_change(diff1, 1, 0, early1[0])
-        w2_q0 = quantise(w2_bf0, "w2_q0", "early1_0")
-        gather_change(diff1, 1, 1, early1[1])
-        w2_q1 = quantise(w2_bf1, "w2_q1", "early1_1")
+        w2_q0 = quantise(w2_bf0, "w2_q0", "early4")
+        w3_w = keep.tile([P, HALVES * H], U32, name="w3_w", tag="w2_bf0", align_bytes=64)
+        deal_columns(w3_w[:], w3_raw[:], HALVES * HALVES, 1)
+        early_last = early_tile(2, "early5")
+        gather_early(1, 2, early_last[:, 0, :])
+        gather_early(1, 3, early_last[:, 1, :])
+        w2_q1 = quantise(w2_bf1, "w2_q1")
         x_q0 = quantise(x_bf0, "x_q0")
 
         gate00 = frame_gate(0, w2_q0, x_q0, "gate00")
         gate01 = frame_gate(1, w2_q1, x_q0, "gate01")
-        early12 = gather_early(1, 2, "x_bf0")
-        early13 = gather_early(1, 3, "diff0")
-        gather_change(diff1, 1, 2, early12)
-        gather_change(diff1, 1, 3, early13)
+        gather_change(diff1, 1, 1, early[3][:, 0, :])
+        gather_change(diff1, 1, 2, early_last[:, 0, :])
+        gather_change(diff1, 1, 3, early_last[:, 1, :])
         x_bf1 = weave_x(diff1, "x_q0_codes")
-        a1 = [memory_product(1, 0, "x_bf0"), memory_product(1, 1, "diff1")]
+        a1 = [a10, memory_product(1, 1, "diffs")]
 
         h00 = gated(a0[0], gate00, "h0")
-        w3_w = keep.tile([P, HALVES * H], U32, name="w3_w", tag="gate00", align_bytes=64)
-        reorder_columns(w3_w[:], w3_raw[:], HALVES * HALVES, LINE // 4)
-        h_q00 = quantise(h00, "h_q00")
         h01 = gated(a0[1], gate01, "h1")
+        h_q00 = quantise(h00, "h_q00", "gate01")
         x_q1 = quantise(x_bf1, "x_q1")
         h_q0 = [h_q00, quantise(h01, "h_q01")]
 
         finish(0, 0, 0, a0[0], h_q0)
         finish(0, 0, 1, a0[0], h_q0)
-        gate10 = frame_gate(0, w2_q0, x_q1, "diff0")
+        gate10 = frame_gate(0, w2_q0, x_q1, "gate10")
         finish(0, 0, 2, a0[0], h_q0)
         finish(0, 0, 3, a0[0], h_q0)
         finish(0, 1, 0, a0[1], h_q0)
-        gate11 = frame_gate(1, w2_q1, x_q1, "gate01")
+        gate11 = frame_gate(1, w2_q1, x_q1, "gate00")
 
         h10 = gated(a1[0], gate10, "h0")
-        finish(0, 1, 1, a0[1], h_q0, "diff0")
+        finish(0, 1, 1, a0[1], h_q0, "gate10")
         h_q10 = quantise(h10, "h_q10")
         h11 = gated(a1[1], gate11, "h1")
-        finish(0, 1, 2, a0[1], h_q0, "gate01")
+        finish(0, 1, 2, a0[1], h_q0, "gate00")
         h_q1 = [h_q10, quantise(h11, "h_q11")]
         finish(0, 1, 3, a0[1], h_q0, "h1")
         for b in range(HALVES):

@@ -111,8 +111,8 @@ def tile_list_cyclone_intensification_guidance_kernel(
         def weave_x(diff, tag):
             x_bf = keep.tile([P, CHUNK * PACK], BF16, name="x_bf", tag=tag, align_bytes=64)
             nc.scalar.copy(
-                x_bf[:].rearrange("p (c i t) -> p c t i", i=2, t=PACK),
-                diff.rearrange("p t (c i) -> p c t i", i=2),
+                x_bf[:].rearrange("p (c i t) -> p c t i", i=4, t=PACK),
+                diff.rearrange("p t (c i) -> p c t i", i=4),
             )
             return x_bf
 
@@ -166,9 +166,9 @@ def tile_list_cyclone_intensification_guidance_kernel(
         def gated(a_sb, gate, tag):
             h_bf = keep.tile([P, CHUNK * PACK], BF16, name="h_bf", tag=tag, align_bytes=64)
             nc.vector.tensor_tensor(
-                h_bf[:].rearrange("p (c i t) -> p c t i", i=2, t=PACK),
-                a_sb[:].rearrange("p t (c i) -> p c t i", i=2),
-                gate[:].rearrange("p t (c i) -> p c t i", i=2),
+                h_bf[:].rearrange("p (c i t) -> p c t i", i=4, t=PACK),
+                a_sb[:].rearrange("p t (c i) -> p c t i", i=4),
+                gate[:].rearrange("p t (c i) -> p c t i", i=4),
                 ALU.mult,
             )
             return h_bf

@@ -27,7 +27,7 @@ SCALE_ROWS = 16
 LINE = 16
 FIRST_BANKS = 4
 LAST_BANKS = 4
-PLAIN_RESULTS = 13
+PLAIN_RESULTS = 14
 
 
 def tile_list_cyclone_intensification_guidance_kernel(
@@ -108,9 +108,9 @@ def tile_list_cyclone_intensification_guidance_kernel(
             late = planes[t][:].indirect(list_late[:, list_cols(c)])
             nc.vector.tensor_tensor(diff[:, t, :], late, early, ALU.subtract)
 
-        def weave_x(diff, tag):
+        def weave_x(copy, diff, tag):
             x_bf = keep.tile([P, CHUNK * PACK], BF16, name="x_bf", tag=tag, align_bytes=64)
-            nc.scalar.copy(
+            copy(
                 x_bf[:].rearrange("p (c i t) -> p c t i", i=4, t=PACK),
                 diff.rearrange("p t (c i) -> p c t i", i=4),
             )
@@ -222,8 +222,7 @@ def tile_list_cyclone_intensification_guidance_kernel(
         gather_early(0, 3, early[5][:, 0, :])
         gather_change(diff0, 0, 2, early[4][:, 0, :])
         gather_change(diff0, 0, 3, early[5][:, 0, :])
-        x_bf0 = weave_x(diff0, "w2_raw1")
-        a10 = memory_product(1, 0, "w2_raw0")
+        x_bf0 = weave_x(nc.scalar.copy, diff0, "w2_raw1")
 
         w2_q0 = quantise(w2_bf0, "w2_q0", "early4")
         w3_w = keep.tile([P, HALVES * H], U32, name="w3_w", tag="w2_bf0", align_bytes=64)
@@ -239,30 +238,25 @@ def tile_list_cyclone_intensification_guidance_kernel(
         gather_change(diff1, 1, 1, early[3][:, 0, :])
         gather_change(diff1, 1, 2, early_last[:, 0, :])
         gather_change(diff1, 1, 3, early_last[:, 1, :])
-        x_bf1 = weave_x(diff1, "x_q0_codes")
+        x_bf1 = weave_x(nc.vector.tensor_copy, diff1, "x_bf1")
+        x_q1 = quantise(x_bf1, "x_q1")
+        a10 = memory_product(1, 0, "w2_raw0")
+        gate10 = frame_gate(0, w2_q0, x_q1, "gate10")
+        gate11 = frame_gate(1, w2_q1, x_q1, "w2_raw1")
         a1 = [a10, memory_product(1, 1, "diffs")]
 
         h00 = gated(a0[0], gate00, "h0")
+        h_q00 = quantise(h00, "h_q00")
         h01 = gated(a0[1], gate01, "h1")
-        h_q00 = quantise(h00, "h_q00", "gate01")
-        x_q1 = quantise(x_bf1, "x_q1")
         h_q0 = [h_q00, quantise(h01, "h_q01")]
-
-        finish(0, 0, 0, a0[0], h_q0)
-        finish(0, 0, 1, a0[0], h_q0)
-        gate10 = frame_gate(0, w2_q0, x_q1, "gate10")
-        finish(0, 0, 2, a0[0], h_q0)
-        finish(0, 0, 3, a0[0], h_q0)
-        finish(0, 1, 0, a0[1], h_q0)
-        gate11 = frame_gate(1, w2_q1, x_q1, "gate00")
-
+        for n in range(6):
+            finish(0, n // PACK, n % PACK, a0[n // PACK], h_q0)
         h10 = gated(a1[0], gate10, "h0")
-        finish(0, 1, 1, a0[1], h_q0, "gate10")
         h_q10 = quantise(h10, "h_q10")
-        h11 = gated(a1[1], gate11, "h1")
-        finish(0, 1, 2, a0[1], h_q0, "gate00")
+        h11 = gated(a1[1], gate11, "gate00")
         h_q1 = [h_q10, quantise(h11, "h_q11")]
-        finish(0, 1, 3, a0[1], h_q0, "h1")
+        finish(0, 1, 2, a0[1], h_q0)
+        finish(0, 1, 3, a0[1], h_q0)
         for b in range(HALVES):
             for t in range(PACK):
                 finish(1, b, t, a1[b], h_q1)

@@ -95,6 +95,12 @@ def tile_list_cyclone_intensification_guidance_kernel(
                 src.rearrange("p (g m t e) -> p g t m e", g=groups, t=PACK, e=width),
             )
 
+        def reorder_columns(dst, src, groups, per_line):
+            nc.vector.tensor_copy(
+                dst.rearrange("p (g t c i) -> p g c t i", g=groups, t=PACK, i=per_line),
+                src.rearrange("p (g c i t) -> p g c t i", g=groups, t=PACK, i=per_line),
+            )
+
         def list_cols(c):
             return slice(c * LIST_COLS, (c + 1) * LIST_COLS)
 
@@ -199,13 +205,8 @@ def tile_list_cyclone_intensification_guidance_kernel(
             nc.sync.dma_start(out_rows[b, t][:, c * CHUNK : (c + 1) * CHUNK], result[:])
 
         w1_w = keep.tile([P, 2 * H], U8, name="w1_w", align_bytes=64)
-        deal_columns(w1_w[:], w1_raw[:], HALVES, 2)
-        w_s = keep.tile([P, H], U8, name="w_s", align_bytes=64)
-        deal_columns(w_s[:], ws_raw[:], HALVES, 1)
-
+        reorder_columns(w1_w[:].bitcast(U16), w1_raw[:].bitcast(U16), HALVES, LINE // 2)
         w2_bf0 = weave_w2(0)
-        a0 = [memory_product(0, 0, "a00"), memory_product(0, 1, "a01")]
-        w2_bf1 = weave_w2(1)
 
         diffs = keep.tile([P, PACK + 1, CHUNK], F32, name="diffs", tag="diffs", align_bytes=64)
         diff0 = diffs[:, 1 : PACK + 1, :]
@@ -215,6 +216,10 @@ def tile_list_cyclone_intensification_guidance_kernel(
         gather_early(1, 0, early[1][:, 0, :])
         gather_change(diff0, 0, 0, early[0][:, 0, :])
         gather_change(diff1, 1, 0, early[1][:, 0, :])
+        w_s = keep.tile([P, H], U8, name="w_s", tag="early0", align_bytes=64)
+        reorder_columns(w_s[:], ws_raw[:], HALVES, LINE)
+        a0 = [memory_product(0, 0, "a00"), memory_product(0, 1, "a01")]
+        w2_bf1 = weave_w2(1)
         gather_early(0, 1, early[2][:, 0, :])
         gather_early(1, 1, early[3][:, 0, :])
         gather_change(diff0, 0, 1, early[2][:, 0, :])

@@ -27,6 +27,7 @@ SCALE_ROWS = 16
 LINE = 16
 FIRST_BANKS = 4
 LAST_BANKS = 4
+POOL_COLS = 256
 PLAIN_RESULTS = 14
 
 
@@ -169,6 +170,16 @@ def tile_list_cyclone_intensification_guidance_kernel(
                 nc.scalar.activation(gate[:, t, :], acc[:], ACT.Sigmoid, bias=bias[:, b, t : t + 1])
             return gate
 
+        def gated_part(engine, a_sb, gate, lo, hi, tag):
+            h_bf = keep.tile([P, (hi - lo) * PACK], BF16, name="h_part", tag=tag, align_bytes=64)
+            engine.tensor_tensor(
+                h_bf[:].rearrange("p (c i t) -> p c t i", i=4, t=PACK),
+                a_sb[:, :, lo:hi].rearrange("p t (c i) -> p c t i", i=4),
+                gate[:, :, lo:hi].rearrange("p t (c i) -> p c t i", i=4),
+                ALU.mult,
+            )
+            return h_bf
+
         def gated(a_sb, gate, tag):
             h_bf = keep.tile([P, CHUNK * PACK], BF16, name="h_bf", tag=tag, align_bytes=64)
             nc.vector.tensor_tensor(
@@ -254,10 +265,18 @@ def tile_list_cyclone_intensification_guidance_kernel(
         h_q00 = quantise(h00, "h_q00")
         h01 = gated(a0[1], gate01, "h1")
         h_q0 = [h_q00, quantise(h01, "h_q01")]
+        codes10 = keep.tile([P, PASS], U32, name="codes10", align_bytes=64)
+        scales10 = keep.tile([P, PASS], U8, name="scales10", align_bytes=64)
+
+        def quantise_part(part, lo, hi):
+            nc.vector.quantize_mx(out=codes10[:, lo:hi].bitcast(FP8X4), scales=scales10[:, lo:hi], in_=part[:])
+
+        quantise_part(gated_part(nc.vector, a1[0], gate10, POOL_COLS, CHUNK, "h0"), POOL_COLS, CHUNK)
+        h10_pool = gated_part(nc.gpsimd, a1[0], gate10, 0, POOL_COLS, "h0")
         for n in range(6):
             finish(0, n // PACK, n % PACK, a0[n // PACK], h_q0)
-        h10 = gated(a1[0], gate10, "h0")
-        h_q10 = quantise(h10, "h_q10")
+        quantise_part(h10_pool, 0, POOL_COLS)
+        h_q10 = (codes10, scales10)
         h11 = gated(a1[1], gate11, "gate00")
         h_q1 = [h_q10, quantise(h11, "h_q11")]
         finish(0, 1, 2, a0[1], h_q0)

@@ -27,7 +27,7 @@ SCALE_ROWS = 16
 LINE = 16
 FIRST_BANKS = 4
 LAST_BANKS = 4
-POOL_COLS = 256
+HALF = CHUNK // 2
 PLAIN_RESULTS = 14
 
 
@@ -194,10 +194,7 @@ def tile_list_cyclone_intensification_guidance_kernel(
 
         def finish(c, b, t, a_sb, h_q, tag=None):
             m0 = (b * PACK + t) * P
-            if (c, b) == (1, 0):
-                acc = ps_first.tile([P, CHUNK], F32, name="acc_first")
-            else:
-                acc = ps_last.tile([P, CHUNK], F32, name="acc_last")
+            acc = ps_last.tile([P, CHUNK], F32, name="acc_last")
             for g in range(HALVES):
                 nc.tensor.matmul_mx(
                     out=acc[:],
@@ -214,6 +211,41 @@ def tile_list_cyclone_intensification_guidance_kernel(
                 result = keep.tile([P, CHUNK], F32, name="result_late", tag=tag, align_bytes=64)
             nc.vector.scalar_tensor_tensor(result[:], a_sb[:, t, :], gain[:, b, t : t + 1], acc[:], ALU.mult, ALU.add)
             nc.sync.dma_start(out_rows[b, t][:, c * CHUNK : (c + 1) * CHUNK], result[:])
+
+        def quantise_half(src, name):
+            codes = keep.tile([P, HALF], U32, name="codes", tag=name + "_codes", align_bytes=64)
+            scales = keep.tile([P, HALF], U8, name="scales", tag=name + "_scales", align_bytes=64)
+            nc.vector.quantize_mx(out=codes[:].bitcast(FP8X4), scales=scales[:], in_=src[:])
+            return codes, scales
+
+        def pair_product(b, u, h_q, acc):
+            for g in range(HALVES):
+                for e in range(2):
+                    m0 = (b * PACK + 2 * u + e) * P
+                    nc.tensor.matmul_mx(
+                        out=acc[:, e * HALF : (e + 1) * HALF],
+                        lhsT=w3_w[:, g * H + m0 : g * H + m0 + P].bitcast(FP8X4),
+                        lhsT_scale=w_s[4 + 4 * g : P, m0 : m0 + P],
+                        rhs=h_q[g][0][:].bitcast(FP8X4),
+                        rhs_scale=h_q[g][1][:],
+                        start=(g == 0 and e == 0),
+                        stop=(g == HALVES - 1 and e == 1),
+                    )
+
+        def finish_pair(b, u, lo, h_q, acc, stores):
+            pair_product(b, u, h_q, acc)
+            result = outs.tile([P, CHUNK], F32, name="result")
+            rows = out_rows[b, 2 * u : 2 * u + 2, :, CHUNK + lo : CHUNK + lo + HALF]
+            for e in range(2):
+                t = 2 * u + e
+                cols = slice(e * HALF, (e + 1) * HALF)
+                nc.vector.scalar_tensor_tensor(
+                    result[:, cols], a1[b][:, t, lo : lo + HALF], gain[:, b, t : t + 1], acc[:, cols], ALU.mult, ALU.add
+                )
+                if stores == 2:
+                    nc.sync.dma_start(rows[e], result[:, cols])
+            if stores == 1:
+                nc.sync.dma_start(rows.rearrange("e p j -> p e j"), result[:].rearrange("p (e j) -> p e j", e=2))
 
         w1_w = keep.tile([P, 2 * H], U8, name="w1_w", align_bytes=64)
         reorder_columns(w1_w[:].bitcast(U16), w1_raw[:].bitcast(U16), HALVES, LINE // 2)
@@ -265,22 +297,21 @@ def tile_list_cyclone_intensification_guidance_kernel(
         h_q00 = quantise(h00, "h_q00")
         h01 = gated(a0[1], gate01, "h1")
         h_q0 = [h_q00, quantise(h01, "h_q01")]
-        codes10 = keep.tile([P, PASS], U32, name="codes10", align_bytes=64)
-        scales10 = keep.tile([P, PASS], U8, name="scales10", align_bytes=64)
-
-        def quantise_part(part, lo, hi):
-            nc.vector.quantize_mx(out=codes10[:, lo:hi].bitcast(FP8X4), scales=scales10[:, lo:hi], in_=part[:])
-
-        quantise_part(gated_part(nc.vector, a1[0], gate10, POOL_COLS, CHUNK, "h0"), POOL_COLS, CHUNK)
-        h10_pool = gated_part(nc.gpsimd, a1[0], gate10, 0, POOL_COLS, "h0")
+        q10_own = quantise_half(gated_part(nc.vector, a1[0], gate10, HALF, CHUNK, "h0"), "q10_own")
+        h10_pool = gated_part(nc.gpsimd, a1[0], gate10, 0, HALF, "h0")
         for n in range(6):
             finish(0, n // PACK, n % PACK, a0[n // PACK], h_q0)
-        quantise_part(h10_pool, 0, POOL_COLS)
-        h_q10 = (codes10, scales10)
-        h11 = gated(a1[1], gate11, "gate00")
-        h_q1 = [h_q10, quantise(h11, "h_q11")]
+        h11_own = gated_part(nc.vector, a1[1], gate11, HALF, CHUNK, "a00")
+        q10_pool = quantise_half(h10_pool, "q10_pool")
+        q11_own = quantise_half(h11_own, "q11_own")
+        h11_pool = gated_part(nc.gpsimd, a1[1], gate11, 0, HALF, "a00")
         finish(0, 1, 2, a0[1], h_q0)
         finish(0, 1, 3, a0[1], h_q0)
-        for b in range(HALVES):
-            for t in range(PACK):
-                finish(1, b, t, a1[b], h_q1)
+        pairs = [(b, u) for b in range(HALVES) for u in range(2)]
+        for b, u in pairs[:-1]:
+            finish_pair(b, u, HALF, (q10_own, q11_own), ps_first.tile([P, CHUNK], F32, name="acc_first"), 1)
+        q11_pool = quantise_half(h11_pool, "q11_pool")
+        finish_pair(1, 1, HALF, (q10_own, q11_own), ps_first.tile([P, CHUNK], F32, name="acc_first"), 1)
+        for b, u in pairs:
+            acc = ps_last.tile([P, CHUNK], F32, name="acc_last")
+            finish_pair(b, u, 0, (q10_pool, q11_pool), acc, 2 if (b, u) == pairs[-1] else 1)

@@ -116,7 +116,7 @@ def tile_list_cyclone_intensification_guidance_kernel(
             nc.vector.tensor_tensor(diff[:, t, :], late, early, ALU.subtract)
 
         def weave_x(copy, diff, tag):
-            x_bf = keep.tile([P, CHUNK * PACK], BF16, name="x_bf", tag=tag, align_bytes=64)
+            x_bf = keep.tile([P, diff.shape[2] * PACK], BF16, name="x_bf", tag=tag, align_bytes=64)
             copy(
                 x_bf[:].rearrange("p (c i t) -> p c t i", i=4, t=PACK),
                 diff.rearrange("p t (c i) -> p c t i", i=4),
@@ -135,6 +135,14 @@ def tile_list_cyclone_intensification_guidance_kernel(
             codes = keep.tile([P, PASS], U32, name="codes", tag=tag or name + "_codes", align_bytes=64)
             scales = keep.tile([P, PASS], U8, name="scales", tag=name + "_scales", align_bytes=64)
             nc.vector.quantize_mx(out=codes[:].bitcast(FP8X4), scales=scales[:], in_=src[:])
+            return codes, scales
+
+        def quantise_halves(parts, name):
+            codes = keep.tile([P, PASS], U32, name="codes", tag=name + "_codes", align_bytes=64)
+            scales = keep.tile([P, PASS], U8, name="scales", tag=name + "_scales", align_bytes=64)
+            for n, part in enumerate(parts):
+                cols = slice(n * HALF, (n + 1) * HALF)
+                nc.vector.quantize_mx(out=codes[:, cols].bitcast(FP8X4), scales=scales[:, cols], in_=part[:])
             return codes, scales
 
         def memory_product(c, b, tag):
@@ -285,16 +293,19 @@ def tile_list_cyclone_intensification_guidance_kernel(
         gate01 = frame_gate(1, w2_q1, x_q0, "gate01")
         gather_change(diff1, 1, 1, early[3][:, 0, :])
         gather_change(diff1, 1, 2, early_last[:, 0, :])
-        gather_change(diff1, 1, 3, early_last[:, 1, :])
-        x_bf1 = weave_x(nc.vector.tensor_copy, diff1, "x_bf1")
-        x_q1 = quantise(x_bf1, "x_q1")
+        halves = (slice(0, HALF), slice(HALF, CHUNK))
+        for n, cols in enumerate(halves):
+            entries = list_late[:, (2 + n) * LIST_COLS // 2 : (3 + n) * LIST_COLS // 2]
+            late = planes[3][:].indirect(entries)
+            nc.vector.tensor_tensor(diff1[:, 3, cols], late, early_last[:, 1, cols], ALU.subtract)
+        x_q1 = quantise_halves([weave_x(nc.vector.tensor_copy, diff1[:, :, cols], "x_bf1_%d" % cols.start) for cols in halves], "x_q1")
         a10 = memory_product(1, 0, "w2_raw0")
         gate10 = frame_gate(0, w2_q0, x_q1, "gate10")
         gate11 = frame_gate(1, w2_q1, x_q1, "w2_raw1")
         a1 = [a10, memory_product(1, 1, "diffs")]
 
-        h00 = gated(a0[0], gate00, "h0")
-        h_q00 = quantise(h00, "h_q00")
+        h00 = [gated_part(nc.vector, a0[0], gate00, cols.start, cols.stop, "h00_%d" % cols.start) for cols in halves]
+        h_q00 = quantise_halves(h00, "h_q00")
         h01 = gated(a0[1], gate01, "h1")
         h_q0 = [h_q00, quantise(h01, "h_q01")]
         q10_own = quantise_half(gated_part(nc.vector, a1[0], gate10, HALF, CHUNK, "h0"), "q10_own")

@@ -20,15 +20,11 @@ P = 128
 PACK = 4
 PASS = P * PACK
 HALVES = H // PASS
-CHUNK = 512
-LIST_COLS = CHUNK // 16
+QUARTER = 256
+PAIR = 2 * QUARTER
 QUADRANTS = 4
-SCALE_ROWS = 16
 LINE = 16
-FIRST_BANKS = 4
-LAST_BANKS = 4
-HALF = CHUNK // 2
-PLAIN_RESULTS = 14
+KB = 1024
 
 
 def tile_list_cyclone_intensification_guidance_kernel(
@@ -37,25 +33,40 @@ def tile_list_cyclone_intensification_guidance_kernel(
     nc = tc.nc
     with ExitStack() as ctx:
         keep = ctx.enter_context(tc.tile_pool(name="keep", bufs=1))
-        outs = ctx.enter_context(tc.tile_pool(name="outs", bufs=PLAIN_RESULTS))
-        ps_first = ctx.enter_context(tc.psum_pool(name="ps_first", bufs=FIRST_BANKS))
-        ps_last = ctx.enter_context(tc.psum_pool(name="ps_last", bufs=LAST_BANKS))
+        arena = ctx.enter_context(tc.tile_pool(name="arena", bufs=1))
+        psum = ctx.enter_context(tc.psum_pool(name="psum", bufs=1))
+
+        top = [0]
+
+        def room(size):
+            at = top[0]
+            top[0] = at + size
+            return at
+
+        def placed(name, shape, dtype, at):
+            return arena.tile(shape, dtype, name=name, tag=name, offset=at, align_bytes=64)
+
+        def kept(name, shape, dtype):
+            return keep.tile(shape, dtype, name=name, tag=name, align_bytes=64)
+
+        def bank(n):
+            return psum.tile([P, PAIR], F32, name="bank", tag="bank%d" % n)
 
         list_tab = keep.tile([P, S // 16], U16, name="list_tab")
         list_late = keep.tile([P, S // 16], U16, name="list_late")
         list_early = keep.tile([P, S // 16], U16, name="list_early")
-        tab_w = keep.tile([P, T], U32, name="tab_w", align_bytes=64)
-        tab_s = keep.tile([P, T], U8, name="tab_s", align_bytes=64)
-        w1_raw = keep.tile([P, 2 * H], U8, name="w1_raw", align_bytes=64)
-        ws_raw = keep.tile([P, H], U8, name="ws_raw", align_bytes=64)
-        w3_raw = keep.tile([P, HALVES * H], U32, name="w3_raw", align_bytes=64)
-        planes = [keep.tile([P, T], F32, name="plane%d" % t) for t in range(PACK)]
-        w2_raw = [
-            keep.tile([P, PACK, PASS], F32, name="w2_raw", tag="w2_raw%d" % b, align_bytes=64) for b in range(HALVES)
-        ]
+        tab_w = kept("tab_w", [P, T], U32)
+        tab_s = kept("tab_s", [P, T], U8)
+        w1_raw = kept("w1_raw", [P, 2 * H], U8)
+        ws_raw = kept("ws_raw", [P, H], U8)
         bias = keep.tile([P, HALVES, PACK], F32, name="bias")
         gain = keep.tile([P, HALVES, PACK], F32, name="gain")
-        v_s = keep.tile([P, S], U8, name="v_s", align_bytes=64)
+        at_planes = room(32 * KB)
+        planes = [placed("plane%d" % t, [P, T], F32, at_planes + 8 * KB * t) for t in range(PACK)]
+        at_w2 = room(16 * KB)
+        w2_raw = [placed("w2_raw%d" % b, [P, PACK, PASS], F32, at_w2 + 8 * KB * b) for b in range(HALVES)]
+        at_w3 = room(8 * KB)
+        w3_raw = placed("w3_raw", [P, HALVES * H], U32, at_w3)
 
         nc.gpsimd.memset(ws_raw[:].bitcast(I32), 0)
 
@@ -74,9 +85,9 @@ def tile_list_cyclone_intensification_guidance_kernel(
             nc.scalar.dma_start(ws_raw[32 * q + 4 : 32 * q + 12, :].bitcast(I32), w3_scales[:, rows, :].bitcast(I32))
         nc.sync.dma_start(list_early[:], offs3)
         nc.sync.dma_start(list_late[:], offs2)
-        nc.sync.dma_start(w2_raw[0][:], w2_rows[:, :, 0:PASS])
         nc.sync.dma_start(planes[1][:], x_rows[1])
         nc.sync.dma_start(planes[2][:], x_rows[2])
+        nc.sync.dma_start(w2_raw[0][:], w2_rows[:, :, 0:PASS])
         nc.sync.dma_start(planes[3][:], x_rows[3])
         nc.sync.dma_start(w2_raw[1][:], w2_rows[:, :, PASS : 2 * PASS])
         nc.sync.dma_start(bias[:], b2.rearrange("(b p t) -> p b t", b=HALVES, t=PACK))
@@ -86,15 +97,10 @@ def tile_list_cyclone_intensification_guidance_kernel(
             w3_words.rearrange("g p c i -> p g (c i)").bitcast(I32),
         )
 
-        v_w = keep.tile([P, S], U32, name="v_w", align_bytes=64)
+        v_s = kept("v_s", [P, S], U8)
+        v_w = kept("v_w", [P, S], U32)
         nc.vector.tensor_copy(v_s[:], tab_s[:].indirect(list_tab[:]))
         nc.vector.tensor_copy(v_w[:], tab_w[:].indirect(list_tab[:]))
-
-        def deal_columns(dst, src, groups, width):
-            nc.gpsimd.tensor_copy(
-                dst.rearrange("p (g t m e) -> p g t m e", g=groups, t=PACK, e=width),
-                src.rearrange("p (g m t e) -> p g t m e", g=groups, t=PACK, e=width),
-            )
 
         def reorder_columns(dst, src, groups, per_line):
             nc.vector.tensor_copy(
@@ -102,136 +108,115 @@ def tile_list_cyclone_intensification_guidance_kernel(
                 src.rearrange("p (g c i t) -> p g c t i", g=groups, t=PACK, i=per_line),
             )
 
-        def list_cols(c):
-            return slice(c * LIST_COLS, (c + 1) * LIST_COLS)
+        def cols(q, count=1):
+            return slice(q * QUARTER, (q + count) * QUARTER)
 
-        def gather_early(c, t, early):
-            nc.vector.tensor_copy(early, planes[t][:].indirect(list_early[:, list_cols(c)]))
+        def entries(frames, q, count):
+            return frames[:, q * QUARTER // 16 : (q + count) * QUARTER // 16]
 
-        def early_tile(count, tag):
-            return keep.tile([P, count, CHUNK], F32, name="early", tag=tag, align_bytes=64)
+        def gather_early(early, t, q, count=1):
+            nc.vector.tensor_copy(early, planes[t][:].indirect(entries(list_early, q, count)))
 
-        def gather_change(diff, c, t, early):
-            late = planes[t][:].indirect(list_late[:, list_cols(c)])
-            nc.vector.tensor_tensor(diff[:, t, :], late, early, ALU.subtract)
+        def gather_change(diff, early, t, q, count=1):
+            nc.vector.tensor_tensor(diff, planes[t][:].indirect(entries(list_late, q, count)), early, ALU.subtract)
 
-        def weave_x(copy, diff, tag):
-            x_bf = keep.tile([P, diff.shape[2] * PACK], BF16, name="x_bf", tag=tag, align_bytes=64)
-            copy(
-                x_bf[:].rearrange("p (c i t) -> p c t i", i=4, t=PACK),
-                diff.rearrange("p t (c i) -> p c t i", i=4),
-            )
-            return x_bf
+        def woven(flat):
+            return flat.rearrange("p (c i t) -> p c t i", i=4, t=PACK)
+
+        def by_fours(rows):
+            return rows.rearrange("p t (c i) -> p c t i", i=4)
 
         def weave_w2(b):
-            w2_bf = keep.tile([P, PASS * PACK], BF16, name="w2_bf", tag="w2_bf%d" % b, align_bytes=64)
+            w2_bf = kept("w2_bf%d" % b, [P, PASS * PACK], BF16)
             nc.scalar.copy(
                 w2_bf[:].rearrange("p (u e m j) -> p u m j e", u=2, e=2, j=PACK),
                 w2_raw[b][:].rearrange("p j (m u e) -> p u m j e", u=2, e=2),
             )
             return w2_bf
 
-        def quantise(src, name, tag=None):
-            codes = keep.tile([P, PASS], U32, name="codes", tag=tag or name + "_codes", align_bytes=64)
-            scales = keep.tile([P, PASS], U8, name="scales", tag=name + "_scales", align_bytes=64)
-            nc.vector.quantize_mx(out=codes[:].bitcast(FP8X4), scales=scales[:], in_=src[:])
+        def quantise(name, src, at=None):
+            width = src.shape[1] // PACK
+            codes = kept(name, [P, width], U32) if at is None else placed(name, [P, width], U32, at)
+            scales = kept(name + "_scales", [P, width], U8)
+            nc.vector.quantize_mx(out=codes[:].bitcast(FP8X4), scales=scales[:], in_=src)
             return codes, scales
 
-        def quantise_halves(parts, name):
-            codes = keep.tile([P, PASS], U32, name="codes", tag=name + "_codes", align_bytes=64)
-            scales = keep.tile([P, PASS], U8, name="scales", tag=name + "_scales", align_bytes=64)
-            for n, part in enumerate(parts):
-                cols = slice(n * HALF, (n + 1) * HALF)
-                nc.vector.quantize_mx(out=codes[:, cols].bitcast(FP8X4), scales=scales[:, cols], in_=part[:])
-            return codes, scales
+        a_sb = [[kept("a%d%d" % (c, b), [P, PACK, PAIR], F32) for b in range(HALVES)] for c in range(2)]
 
-        def memory_product(c, b, tag):
-            a_sb = keep.tile([P, PACK, CHUNK], F32, name="a_sb", tag=tag, align_bytes=64)
-            for t in range(PACK):
-                m0 = (b * PACK + t) * P
-                acc = ps_first.tile([P, CHUNK], F32, name="acc_first")
-                nc.tensor.matmul_mx(
-                    out=acc[:],
-                    lhsT=w1_w[:, 2 * m0 : 2 * (m0 + P)].bitcast(FP4X4),
-                    lhsT_scale=w_s[:, m0 : m0 + P],
-                    rhs=v_w[:, c * CHUNK : (c + 1) * CHUNK].bitcast(FP8X4),
-                    rhs_scale=v_s[:, c * CHUNK : (c + 1) * CHUNK],
-                    start=True,
-                    stop=True,
-                )
-                nc.scalar.copy(a_sb[:, t, :], acc[:])
-            return a_sb
+        def a_rows(q, b):
+            return a_sb[q // 2][b][:, :, cols(q % 2)]
 
-        def frame_gate(b, w2_q, x_q, tag):
-            gate = keep.tile([P, PACK, CHUNK], F32, name="gate", tag=tag, align_bytes=64)
-            for t in range(PACK):
-                acc = ps_first.tile([P, CHUNK], F32, name="acc_first")
-                nc.tensor.matmul_mx(
-                    out=acc[:],
-                    lhsT=w2_q[0][:, t * P : (t + 1) * P].bitcast(FP8X4),
-                    lhsT_scale=w2_q[1][:, t * P : (t + 1) * P],
-                    rhs=x_q[0][:].bitcast(FP8X4),
-                    rhs_scale=x_q[1][:],
-                    start=True,
-                    stop=True,
-                )
-                nc.scalar.activation(gate[:, t, :], acc[:], ACT.Sigmoid, bias=bias[:, b, t : t + 1])
-            return gate
-
-        def gated_part(engine, a_sb, gate, lo, hi, tag):
-            h_bf = keep.tile([P, (hi - lo) * PACK], BF16, name="h_part", tag=tag, align_bytes=64)
-            engine.tensor_tensor(
-                h_bf[:].rearrange("p (c i t) -> p c t i", i=4, t=PACK),
-                a_sb[:, :, lo:hi].rearrange("p t (c i) -> p c t i", i=4),
-                gate[:, :, lo:hi].rearrange("p t (c i) -> p c t i", i=4),
-                ALU.mult,
+        def memory_pass(acc, b, t, lo, width):
+            m0 = (b * PACK + t) * P
+            nc.tensor.matmul_mx(
+                out=acc,
+                lhsT=w1_w[:, 2 * m0 : 2 * (m0 + P)].bitcast(FP4X4),
+                lhsT_scale=w_s[:, m0 : m0 + P],
+                rhs=v_w[:, lo : lo + width].bitcast(FP8X4),
+                rhs_scale=v_s[:, lo : lo + width],
+                start=True,
+                stop=True,
             )
-            return h_bf
 
-        def gated(a_sb, gate, tag):
-            h_bf = keep.tile([P, CHUNK * PACK], BF16, name="h_bf", tag=tag, align_bytes=64)
-            nc.vector.tensor_tensor(
-                h_bf[:].rearrange("p (c i t) -> p c t i", i=4, t=PACK),
-                a_sb[:].rearrange("p t (c i) -> p c t i", i=4),
-                gate[:].rearrange("p t (c i) -> p c t i", i=4),
-                ALU.mult,
-            )
-            return h_bf
+        def memory_banks(q, b, first):
+            accs = []
+            for n in range(2):
+                acc = bank(first + n)
+                for t in range(PACK):
+                    memory_pass(acc[:, t * P : (t + 1) * P], b, t, q * QUARTER + n * P, P)
+                accs.append(acc[:].rearrange("p (t c) -> p t c", t=PACK))
+            return accs
+
+        def copy_banks(q, b, accs):
+            for n, acc in enumerate(accs):
+                nc.scalar.copy(a_rows(q, b)[:, :, n * P : (n + 1) * P], acc)
+
+        def memory_quarter(q, b, first):
+            for u in range(2):
+                acc = bank(first + u)
+                for e in range(2):
+                    memory_pass(acc[:, cols(e)], b, 2 * u + e, q * QUARTER, QUARTER)
+                nc.scalar.copy(a_rows(q, b)[:, 2 * u : 2 * u + 2, :], acc[:].rearrange("p (e c) -> p e c", e=2))
+
+        def frame_gate(gate, b, w2_q, x_codes, x_scales, first):
+            for u in range(2):
+                acc = bank(first + u)
+                for e in range(2):
+                    t = 2 * u + e
+                    nc.tensor.matmul_mx(
+                        out=acc[:, cols(e)],
+                        lhsT=w2_q[0][:, t * P : (t + 1) * P].bitcast(FP8X4),
+                        lhsT_scale=w2_q[1][:, t * P : (t + 1) * P],
+                        rhs=x_codes.bitcast(FP8X4),
+                        rhs_scale=x_scales,
+                        start=True,
+                        stop=True,
+                    )
+                for e in range(2):
+                    t = 2 * u + e
+                    nc.scalar.activation(gate[:, t, :], acc[:, cols(e)], ACT.Sigmoid, bias=bias[:, b, t : t + 1])
+
+        def gated(engine, h_bf, q, b, gate):
+            engine.tensor_tensor(woven(h_bf), by_fours(a_rows(q, b)), by_fours(gate), ALU.mult)
+
+        def gated_from_banks(h_bf, accs, gate):
+            for n, acc in enumerate(accs):
+                nc.vector.tensor_tensor(
+                    woven(h_bf[:, n * PASS : (n + 1) * PASS]),
+                    by_fours(acc),
+                    by_fours(gate[:, :, n * P : (n + 1) * P]),
+                    ALU.mult,
+                )
 
         out_rows = out.rearrange("(b p t) j -> b t p j", b=HALVES, t=PACK)
 
-        def finish(c, b, t, a_sb, h_q, tag=None):
-            m0 = (b * PACK + t) * P
-            acc = ps_last.tile([P, CHUNK], F32, name="acc_last")
-            for g in range(HALVES):
-                nc.tensor.matmul_mx(
-                    out=acc[:],
-                    lhsT=w3_w[:, g * H + m0 : g * H + m0 + P].bitcast(FP8X4),
-                    lhsT_scale=w_s[4 + 4 * g : P, m0 : m0 + P],
-                    rhs=h_q[g][0][:].bitcast(FP8X4),
-                    rhs_scale=h_q[g][1][:],
-                    start=(g == 0),
-                    stop=(g == HALVES - 1),
-                )
-            if tag is None:
-                result = outs.tile([P, CHUNK], F32, name="result")
-            else:
-                result = keep.tile([P, CHUNK], F32, name="result_late", tag=tag, align_bytes=64)
-            nc.vector.scalar_tensor_tensor(result[:], a_sb[:, t, :], gain[:, b, t : t + 1], acc[:], ALU.mult, ALU.add)
-            nc.sync.dma_start(out_rows[b, t][:, c * CHUNK : (c + 1) * CHUNK], result[:])
-
-        def quantise_half(src, name):
-            codes = keep.tile([P, HALF], U32, name="codes", tag=name + "_codes", align_bytes=64)
-            scales = keep.tile([P, HALF], U8, name="scales", tag=name + "_scales", align_bytes=64)
-            nc.vector.quantize_mx(out=codes[:].bitcast(FP8X4), scales=scales[:], in_=src[:])
-            return codes, scales
-
-        def pair_product(b, u, h_q, acc):
+        def finish(q, n, h_q, acc, at, stores=1):
+            b, u = divmod(n, 2)
             for g in range(HALVES):
                 for e in range(2):
                     m0 = (b * PACK + 2 * u + e) * P
                     nc.tensor.matmul_mx(
-                        out=acc[:, e * HALF : (e + 1) * HALF],
+                        out=acc[:, cols(e)],
                         lhsT=w3_w[:, g * H + m0 : g * H + m0 + P].bitcast(FP8X4),
                         lhsT_scale=w_s[4 + 4 * g : P, m0 : m0 + P],
                         rhs=h_q[g][0][:].bitcast(FP8X4),
@@ -239,90 +224,149 @@ def tile_list_cyclone_intensification_guidance_kernel(
                         start=(g == 0 and e == 0),
                         stop=(g == HALVES - 1 and e == 1),
                     )
-
-        def finish_pair(b, u, lo, h_q, acc, stores):
-            pair_product(b, u, h_q, acc)
-            result = outs.tile([P, CHUNK], F32, name="result")
-            rows = out_rows[b, 2 * u : 2 * u + 2, :, CHUNK + lo : CHUNK + lo + HALF]
+            result = placed("result%d%d" % (q, n), [P, PAIR], F32, at)
+            rows = out_rows[b, 2 * u : 2 * u + 2, :, cols(q)]
             for e in range(2):
                 t = 2 * u + e
-                cols = slice(e * HALF, (e + 1) * HALF)
                 nc.vector.scalar_tensor_tensor(
-                    result[:, cols], a1[b][:, t, lo : lo + HALF], gain[:, b, t : t + 1], acc[:, cols], ALU.mult, ALU.add
+                    result[:, cols(e)], a_rows(q, b)[:, t, :], gain[:, b, t : t + 1], acc[:, cols(e)], ALU.mult, ALU.add
                 )
                 if stores == 2:
-                    nc.sync.dma_start(rows[e], result[:, cols])
+                    nc.sync.dma_start(rows[e], result[:, cols(e)])
             if stores == 1:
                 nc.sync.dma_start(rows.rearrange("e p j -> p e j"), result[:].rearrange("p (e j) -> p e j", e=2))
 
-        w1_w = keep.tile([P, 2 * H], U8, name="w1_w", align_bytes=64)
+        w1_w = kept("w1_w", [P, 2 * H], U8)
         reorder_columns(w1_w[:].bitcast(U16), w1_raw[:].bitcast(U16), HALVES, LINE // 2)
         w2_bf0 = weave_w2(0)
 
-        diffs = keep.tile([P, PACK + 1, CHUNK], F32, name="diffs", tag="diffs", align_bytes=64)
-        diff0 = diffs[:, 1 : PACK + 1, :]
-        diff1 = diffs[:, 0:PACK, :]
-        early = [early_tile(1, "early%d" % n) for n in range(6)]
-        gather_early(0, 0, early[0][:, 0, :])
-        gather_early(1, 0, early[1][:, 0, :])
-        gather_change(diff0, 0, 0, early[0][:, 0, :])
-        gather_change(diff1, 1, 0, early[1][:, 0, :])
-        w_s = keep.tile([P, H], U8, name="w_s", tag="early0", align_bytes=64)
+        at_diff = room(8 * KB)
+        diff_first = placed("diff_first", [P, PACK, PAIR], F32, at_diff)
+        at_early = [room(2 * KB) for t in range(PACK)]
+        at_other = room(KB)
+        at_second = room(8 * KB)
+        at_last = room(KB) - KB // 2
+
+        def first_plane(t):
+            at = (at_early[t], at_last if t == PACK - 1 else at_other)
+            early = [placed("early%d%d" % (q, t), [P, QUARTER], F32, at[q]) for q in range(2)]
+            for q in range(2):
+                gather_early(early[q][:], t, q)
+            for q in range(2):
+                gather_change(diff_first[:, t, cols(q)], early[q][:], t, q)
+
+        first_plane(0)
+        w_s = placed("w_s", [P, H], U8, at_early[0])
         reorder_columns(w_s[:], ws_raw[:], HALVES, LINE)
-        a0 = [memory_product(0, 0, "a00"), memory_product(0, 1, "a01")]
+        for t in range(PACK):
+            acc = bank(t)
+            memory_pass(acc[:], 0, t, 0, PAIR)
+            nc.scalar.copy(a_sb[0][0][:, t, :], acc[:])
+        held = [memory_banks(q, 1, 4 + 2 * q) for q in range(2)]
+        for q in range(2):
+            copy_banks(q, 1, held[q])
+        first_plane(1)
+        first_plane(2)
+        early_0 = placed("early_second0", [P, PAIR], F32, at_early[2])
+        gather_early(early_0[:], 0, 2, 2)
+        first_plane(3)
+
+        at_rest = room(6 * KB)
+        at_x = room(4 * KB) - 64
+        at_w3w = room(8 * KB) - 128
+        x_first = placed("x_first", [P, PAIR * PACK], BF16, at_x)
+        for q in range(2):
+            nc.scalar.copy(woven(x_first[:, q * KB : (q + 1) * KB]), by_fours(diff_first[:, :, cols(q)]))
         w2_bf1 = weave_w2(1)
-        gather_early(0, 1, early[2][:, 0, :])
-        gather_early(1, 1, early[3][:, 0, :])
-        gather_change(diff0, 0, 1, early[2][:, 0, :])
-        gather_early(0, 2, early[4][:, 0, :])
-        gather_early(0, 3, early[5][:, 0, :])
-        gather_change(diff0, 0, 2, early[4][:, 0, :])
-        gather_change(diff0, 0, 3, early[5][:, 0, :])
-        x_bf0 = weave_x(nc.scalar.copy, diff0, "w2_raw1")
+        w2_q0 = quantise("w2_q0", w2_bf0[:], at_early[3])
+        diff_second = placed("diff_second", [P, PACK, PAIR], F32, at_second)
+        gather_change(diff_second[:, 0, :], early_0[:], 0, 2, 2)
+        x_q = quantise("x_q", x_first[:])
 
-        w2_q0 = quantise(w2_bf0, "w2_q0", "early4")
-        w3_w = keep.tile([P, HALVES * H], U32, name="w3_w", tag="w2_bf0", align_bytes=64)
-        deal_columns(w3_w[:], w3_raw[:], HALVES * HALVES, 1)
-        early_last = early_tile(2, "early5")
-        gather_early(1, 2, early_last[:, 0, :])
-        gather_early(1, 3, early_last[:, 1, :])
-        w2_q1 = quantise(w2_bf1, "w2_q1")
-        x_q0 = quantise(x_bf0, "x_q0")
+        early_rest = placed("early_rest", [P, PACK - 1, PAIR], F32, at_rest)
+        w3_w = placed("w3_w", [P, HALVES * H], U32, at_w3w)
+        nc.gpsimd.tensor_copy(
+            w3_w[:].rearrange("p (g t m) -> p g t m", g=HALVES * HALVES, t=PACK),
+            w3_raw[:].rearrange("p (g m t) -> p g t m", g=HALVES * HALVES, t=PACK),
+        )
+        for t in range(1, PACK):
+            gather_early(early_rest[:, t - 1, :], t, 2, 2)
+        gather_change(diff_second[:, 1, :], early_rest[:, 0, :], 1, 2, 2)
+        w2_q = [w2_q0, quantise("w2_q1", w2_bf1[:])]
 
-        gate00 = frame_gate(0, w2_q0, x_q0, "gate00")
-        gate01 = frame_gate(1, w2_q1, x_q0, "gate01")
-        gather_change(diff1, 1, 1, early[3][:, 0, :])
-        gather_change(diff1, 1, 2, early_last[:, 0, :])
-        halves = (slice(0, HALF), slice(HALF, CHUNK))
-        for n, cols in enumerate(halves):
-            entries = list_late[:, (2 + n) * LIST_COLS // 2 : (3 + n) * LIST_COLS // 2]
-            late = planes[3][:].indirect(entries)
-            nc.vector.tensor_tensor(diff1[:, 3, cols], late, early_last[:, 1, cols], ALU.subtract)
-        x_q1 = quantise_halves([weave_x(nc.vector.tensor_copy, diff1[:, :, cols], "x_bf1_%d" % cols.start) for cols in halves], "x_q1")
-        a10 = memory_product(1, 0, "w2_raw0")
-        gate10 = frame_gate(0, w2_q0, x_q1, "gate10")
-        gate11 = frame_gate(1, w2_q1, x_q1, "w2_raw1")
-        a1 = [a10, memory_product(1, 1, "diffs")]
+        def gate_tile(q, b, at):
+            return placed("gate%d%d" % (q, b), [P, PACK, QUARTER], F32, at)[:]
 
-        h00 = [gated_part(nc.vector, a0[0], gate00, cols.start, cols.stop, "h00_%d" % cols.start) for cols in halves]
-        h_q00 = quantise_halves(h00, "h_q00")
-        h01 = gated(a0[1], gate01, "h1")
-        h_q0 = [h_q00, quantise(h01, "h_q01")]
-        q10_own = quantise_half(gated_part(nc.vector, a1[0], gate10, HALF, CHUNK, "h0"), "q10_own")
-        h10_pool = gated_part(nc.gpsimd, a1[0], gate10, 0, HALF, "h0")
-        for n in range(6):
-            finish(0, n // PACK, n % PACK, a0[n // PACK], h_q0)
-        h11_own = gated_part(nc.vector, a1[1], gate11, HALF, CHUNK, "a00")
-        q10_pool = quantise_half(h10_pool, "q10_pool")
-        q11_own = quantise_half(h11_own, "q11_own")
-        h11_pool = gated_part(nc.gpsimd, a1[1], gate11, 0, HALF, "a00")
-        finish(0, 1, 2, a0[1], h_q0)
-        finish(0, 1, 3, a0[1], h_q0)
-        pairs = [(b, u) for b in range(HALVES) for u in range(2)]
-        for b, u in pairs[:-1]:
-            finish_pair(b, u, HALF, (q10_own, q11_own), ps_first.tile([P, CHUNK], F32, name="acc_first"), 1)
-        q11_pool = quantise_half(h11_pool, "q11_pool")
-        finish_pair(1, 1, HALF, (q10_own, q11_own), ps_first.tile([P, CHUNK], F32, name="acc_first"), 1)
-        for b, u in pairs:
-            acc = ps_last.tile([P, CHUNK], F32, name="acc_last")
-            finish_pair(b, u, 0, (q10_pool, q11_pool), acc, 2 if (b, u) == pairs[-1] else 1)
+        gate00 = diff_second[:, 2:4, :].rearrange("p s (r c) -> p (s r) c", r=2)
+        gate10 = gate_tile(1, 0, at_w2)
+        gate01 = gate_tile(0, 1, at_w2 + 4 * KB)
+        gate11 = gate_tile(1, 1, at_diff)
+        for q, b, gate in ((0, 0, gate00), (1, 0, gate10), (0, 1, gate01), (1, 1, gate11)):
+            frame_gate(gate, b, w2_q[b], x_q[0][:, cols(q)], x_q[1][:, cols(q)], 2 * q)
+
+        h00 = kept("h00", [P, KB], BF16)
+        gated(nc.vector, h00[:], 0, 0, gate00)
+        for t in (2, 3):
+            gather_change(diff_second[:, t, cols(0)], early_rest[:, t - 1, cols(0)], t, 2)
+        q00 = quantise("q00", h00[:])
+        for t in (2, 3):
+            gather_change(diff_second[:, t, cols(1)], early_rest[:, t - 1, cols(1)], t, 3)
+
+        at_own = room(4 * KB)
+        at_x2 = room(2 * KB) - 64
+        at_pool = room(2 * KB) - 128
+        x_2 = placed("x_2", [P, KB], BF16, at_x2)
+        x_3 = kept("x_3", [P, KB], BF16)
+        nc.scalar.copy(woven(x_2[:]), by_fours(diff_second[:, :, cols(0)]))
+        nc.scalar.copy(woven(x_3[:]), by_fours(diff_second[:, :, cols(1)]))
+        x_q2 = quantise("x_q2", x_2[:])
+        h10 = placed("h10", [P, KB], BF16, at_pool)
+        gated(nc.gpsimd, h10[:], 1, 0, gate10)
+        h_own = placed("h_own", [P, 2, KB], BF16, at_own)
+        gated_from_banks(h_own[:, 0, :], held[0], gate01)
+        gated_from_banks(h_own[:, 1, :], held[1], gate11)
+        q01 = quantise("q01", h_own[:, 0, :], at_w2)
+        x_q3 = quantise("x_q3", x_3[:], at_w2 + KB)
+        q11 = quantise("q11", h_own[:, 1, :], at_w2 + 2 * KB)
+        q10 = quantise("q10", h10[:], at_w2 + 3 * KB)
+
+        gate20 = gate_tile(2, 0, at_w2 + 8 * KB)
+        gate21 = gate_tile(2, 1, at_w2 + 12 * KB)
+        gate30 = gate_tile(3, 0, at_w3)
+        gate31 = gate_tile(3, 1, at_w3 + 4 * KB)
+        frame_gate(gate20, 0, w2_q[0], x_q2[0][:], x_q2[1][:], 0)
+        memory_quarter(2, 0, 2)
+        frame_gate(gate21, 1, w2_q[1], x_q2[0][:], x_q2[1][:], 0)
+        memory_quarter(3, 0, 2)
+        frame_gate(gate30, 0, w2_q[0], x_q3[0][:], x_q3[1][:], 0)
+        frame_gate(gate31, 1, w2_q[1], x_q3[0][:], x_q3[1][:], 2)
+        late = memory_banks(2, 1, 0)
+        memory_quarter(3, 1, 2)
+
+        at_results = [at_planes + 2 * KB * n for n in range(16)]
+        h20 = placed("h20", [P, KB], BF16, at_pool)
+        gated(nc.gpsimd, h20[:], 2, 0, gate20)
+        at_h3 = room(2 * KB)
+        h30 = placed("h30", [P, KB], BF16, at_h3)
+        gated(nc.gpsimd, h30[:], 3, 0, gate30)
+        for n in range(4):
+            finish(0, n, (q00, q01), bank(4 + n), at_results[n])
+        for n in range(2):
+            finish(1, n, (q10, q11), bank(4 + n), at_results[4 + n])
+        h21 = placed("h21", [P, KB], BF16, at_own)
+        gated_from_banks(h21[:], late, gate21)
+        copy_banks(2, 1, late)
+        q20 = quantise("q20", h20[:], at_w3)
+        q21 = quantise("q21", h21[:], at_w3 + KB)
+        q30 = quantise("q30", h30[:], at_w3 + 2 * KB)
+        h31 = placed("h31", [P, KB], BF16, at_h3)
+        gated(nc.gpsimd, h31[:], 3, 1, gate31)
+        finish(1, 2, (q10, q11), bank(6), at_pool)
+        finish(1, 3, (q10, q11), bank(7), at_own)
+        for n in range(2):
+            finish(2, n, (q20, q21), bank(4 + n), at_results[6 + n])
+        q31 = quantise("q31", h31[:])
+        for n in range(2, 4):
+            finish(2, n, (q20, q21), bank(4 + n), at_w3 + 2 * KB * n)
+        for n in range(4):
+            finish(3, n, (q30, q31), bank(n), at_results[8 + n], 2 if n == 3 else 1)

@@ -65,37 +65,48 @@ def tile_list_cyclone_intensification_guidance_kernel(
         planes = [placed("plane%d" % t, [P, T], F32, at_planes + 8 * KB * t) for t in range(PACK)]
         at_w2 = room(16 * KB)
         w2_raw = [placed("w2_raw%d" % b, [P, PACK, PASS], F32, at_w2 + 8 * KB * b) for b in range(HALVES)]
-        at_w3 = room(8 * KB)
+        at_second = room(8 * KB)
+        at_w3 = room(8 * KB) - 64
         w3_raw = placed("w3_raw", [P, HALVES * H], U32, at_w3)
 
-        nc.gpsimd.memset(ws_raw[:].bitcast(I32), 0)
+        nc.vector.memset(ws_raw[:].bitcast(I32), 0)
 
         x_rows = xT.rearrange("(p t) c -> t p c", t=PACK)
         w2_rows = w2.rearrange("(p j) c -> p j c", j=PACK)
+
+        def load_weight_scales(q, first):
+            rows = slice(4 * q, 4 * q + 4)
+            if first:
+                nc.sync.dma_start(ws_raw[32 * q : 32 * q + 4, :].bitcast(I32), w1_scales[0, rows, :].bitcast(I32))
+            else:
+                nc.sync.dma_start(ws_raw[32 * q + 4 : 32 * q + 12, :].bitcast(I32), w3_scales[:, rows, :].bitcast(I32))
+
+        scale_loads = [(q, first) for q in range(QUADRANTS) for first in (True, False)]
         nc.sync.dma_start(list_tab[:], offs)
         for q in range(QUADRANTS):
             rows = tab_scales[0, 4 * q : 4 * q + 4, :].bitcast(I32)
             nc.sync.dma_start(tab_s[32 * q : 32 * q + 32, :].bitcast(I32), rows.partition_broadcast(8))
+        for q, first in scale_loads[:2]:
+            load_weight_scales(q, first)
         nc.sync.dma_start(tab_w[:].bitcast(I32), tab_words[0].rearrange("p c i -> p (c i)").bitcast(I32))
+        for q, first in scale_loads[2:7]:
+            load_weight_scales(q, first)
         nc.sync.dma_start(w1_raw[:].bitcast(I32), w1_words[0].bitcast(I32))
         nc.sync.dma_start(planes[0][:], x_rows[0])
-        for q in range(QUADRANTS):
-            rows = slice(4 * q, 4 * q + 4)
-            nc.scalar.dma_start(ws_raw[32 * q : 32 * q + 4, :].bitcast(I32), w1_scales[0, rows, :].bitcast(I32))
-            nc.scalar.dma_start(ws_raw[32 * q + 4 : 32 * q + 12, :].bitcast(I32), w3_scales[:, rows, :].bitcast(I32))
+        for q, first in scale_loads[7:]:
+            load_weight_scales(q, first)
         nc.sync.dma_start(list_early[:], offs3)
         nc.sync.dma_start(list_late[:], offs2)
-        nc.sync.dma_start(planes[1][:], x_rows[1])
-        nc.sync.dma_start(planes[2][:], x_rows[2])
+        for t in range(1, PACK):
+            nc.sync.dma_start(planes[t][:], x_rows[t])
         nc.sync.dma_start(w2_raw[0][:], w2_rows[:, :, 0:PASS])
-        nc.sync.dma_start(planes[3][:], x_rows[3])
-        nc.sync.dma_start(w2_raw[1][:], w2_rows[:, :, PASS : 2 * PASS])
-        nc.sync.dma_start(bias[:], b2.rearrange("(b p t) -> p b t", b=HALVES, t=PACK))
-        nc.sync.dma_start(gain[:], res.rearrange("(b p t) -> p b t", b=HALVES, t=PACK))
         nc.sync.dma_start(
             w3_raw[:].bitcast(I32).rearrange("p (g c) -> p g c", g=HALVES),
             w3_words.rearrange("g p c i -> p g (c i)").bitcast(I32),
         )
+        nc.sync.dma_start(w2_raw[1][:], w2_rows[:, :, PASS : 2 * PASS])
+        nc.sync.dma_start(bias[:], b2.rearrange("(b p t) -> p b t", b=HALVES, t=PACK))
+        nc.sync.dma_start(gain[:], res.rearrange("(b p t) -> p b t", b=HALVES, t=PACK))
 
         v_s = kept("v_s", [P, S], U8)
         v_w = kept("v_w", [P, S], U32)
@@ -210,20 +221,24 @@ def tile_list_cyclone_intensification_guidance_kernel(
 
         out_rows = out.rearrange("(b p t) j -> b t p j", b=HALVES, t=PACK)
 
+        def last_passes(n, g, h_g, acc):
+            for e in range(2):
+                m0 = (2 * n + e) * P
+                nc.tensor.matmul_mx(
+                    out=acc[:, cols(e)],
+                    lhsT=w3_w[:, g * H + m0 : g * H + m0 + P].bitcast(FP8X4),
+                    lhsT_scale=w_s[4 + 4 * g : P, m0 : m0 + P],
+                    rhs=h_g[0][:].bitcast(FP8X4),
+                    rhs_scale=h_g[1][:],
+                    start=(g == 0 and e == 0),
+                    stop=(g == HALVES - 1 and e == 1),
+                )
+
         def finish(q, n, h_q, acc, at, stores=1):
             b, u = divmod(n, 2)
             for g in range(HALVES):
-                for e in range(2):
-                    m0 = (b * PACK + 2 * u + e) * P
-                    nc.tensor.matmul_mx(
-                        out=acc[:, cols(e)],
-                        lhsT=w3_w[:, g * H + m0 : g * H + m0 + P].bitcast(FP8X4),
-                        lhsT_scale=w_s[4 + 4 * g : P, m0 : m0 + P],
-                        rhs=h_q[g][0][:].bitcast(FP8X4),
-                        rhs_scale=h_q[g][1][:],
-                        start=(g == 0 and e == 0),
-                        stop=(g == HALVES - 1 and e == 1),
-                    )
+                if h_q[g] is not None:
+                    last_passes(n, g, h_q[g], acc)
             result = placed("result%d%d" % (q, n), [P, PAIR], F32, at)
             rows = out_rows[b, 2 * u : 2 * u + 2, :, cols(q)]
             for e in range(2):
@@ -238,50 +253,48 @@ def tile_list_cyclone_intensification_guidance_kernel(
 
         w1_w = kept("w1_w", [P, 2 * H], U8)
         reorder_columns(w1_w[:].bitcast(U16), w1_raw[:].bitcast(U16), HALVES, LINE // 2)
+        w_s = kept("w_s", [P, H], U8)
+        reorder_columns(w_s[:], ws_raw[:], HALVES, LINE)
         w2_bf0 = weave_w2(0)
 
         at_diff = room(8 * KB)
         diff_first = placed("diff_first", [P, PACK, PAIR], F32, at_diff)
-        at_early = [room(2 * KB) for t in range(PACK)]
-        at_other = room(KB)
-        at_second = room(8 * KB)
-        at_last = room(KB) - KB // 2
+        at_rest = room(6 * KB)
+        at_w3w = room(8 * KB)
+        at_early = [room(KB) for q in range(2)]
+        at_last = (at_rest, at_w3w)
 
-        def first_plane(t):
-            at = (at_early[t], at_last if t == PACK - 1 else at_other)
+        def first_plane(t, at):
             early = [placed("early%d%d" % (q, t), [P, QUARTER], F32, at[q]) for q in range(2)]
             for q in range(2):
                 gather_early(early[q][:], t, q)
             for q in range(2):
                 gather_change(diff_first[:, t, cols(q)], early[q][:], t, q)
 
-        first_plane(0)
-        w_s = placed("w_s", [P, H], U8, at_early[0])
-        reorder_columns(w_s[:], ws_raw[:], HALVES, LINE)
-        for t in range(PACK):
-            acc = bank(t)
-            memory_pass(acc[:], 0, t, 0, PAIR)
-            nc.scalar.copy(a_sb[0][0][:, t, :], acc[:])
-        held = [memory_banks(q, 1, 4 + 2 * q) for q in range(2)]
-        for q in range(2):
-            copy_banks(q, 1, held[q])
-        first_plane(1)
-        first_plane(2)
-        early_0 = placed("early_second0", [P, PAIR], F32, at_early[2])
+        first_plane(0, at_early)
+        early_0 = kept("early_second0", [P, PAIR], F32)
         gather_early(early_0[:], 0, 2, 2)
-        first_plane(3)
+        first_plane(1, at_early)
+        first_plane(2, at_early)
+        first_plane(3, at_last)
 
-        at_rest = room(6 * KB)
-        at_x = room(4 * KB) - 64
-        at_w3w = room(8 * KB) - 128
-        x_first = placed("x_first", [P, PAIR * PACK], BF16, at_x)
+        x_first = kept("x_first", [P, PAIR * PACK], BF16)
         for q in range(2):
             nc.scalar.copy(woven(x_first[:, q * KB : (q + 1) * KB]), by_fours(diff_first[:, :, cols(q)]))
         w2_bf1 = weave_w2(1)
-        w2_q0 = quantise("w2_q0", w2_bf0[:], at_early[3])
-        diff_second = placed("diff_second", [P, PACK, PAIR], F32, at_second)
-        gather_change(diff_second[:, 0, :], early_0[:], 0, 2, 2)
-        x_q = quantise("x_q", x_first[:])
+
+        def memory_pair(c):
+            for t in range(PACK):
+                acc = bank(t)
+                memory_pass(acc[:], 0, t, c * PAIR, PAIR)
+                nc.scalar.copy(a_sb[c][0][:, t, :], acc[:])
+
+        memory_pair(0)
+        held = [memory_banks(q, 1, 4 + 2 * q) for q in range(2)]
+        for q in range(2):
+            copy_banks(q, 1, held[q])
+        memory_pair(1)
+        memory_quarter(3, 1, 0)
 
         early_rest = placed("early_rest", [P, PACK - 1, PAIR], F32, at_rest)
         w3_w = placed("w3_w", [P, HALVES * H], U32, at_w3w)
@@ -291,8 +304,12 @@ def tile_list_cyclone_intensification_guidance_kernel(
         )
         for t in range(1, PACK):
             gather_early(early_rest[:, t - 1, :], t, 2, 2)
-        gather_change(diff_second[:, 1, :], early_rest[:, 0, :], 1, 2, 2)
+        w2_q0 = quantise("w2_q0", w2_bf0[:], at_w3 + 64)
+        x_q = quantise("x_q", x_first[:], at_w3 + 64 + 2 * KB)
+        diff_second = placed("diff_second", [P, PACK, PAIR], F32, at_second)
+        gather_change(diff_second[:, 0, :], early_0[:], 0, 2, 2)
         w2_q = [w2_q0, quantise("w2_q1", w2_bf1[:])]
+        gather_change(diff_second[:, 1, :], early_rest[:, 0, :], 1, 2, 2)
 
         def gate_tile(q, b, at):
             return placed("gate%d%d" % (q, b), [P, PACK, QUARTER], F32, at)[:]
@@ -323,50 +340,55 @@ def tile_list_cyclone_intensification_guidance_kernel(
         h10 = placed("h10", [P, KB], BF16, at_pool)
         gated(nc.gpsimd, h10[:], 1, 0, gate10)
         h_own = placed("h_own", [P, 2, KB], BF16, at_own)
+        gate20 = gate_tile(2, 0, at_w2 + 8 * KB)
+        gate21 = gate_tile(2, 1, at_w2 + 12 * KB)
+        gate30 = gate_tile(3, 0, at_rest)
+        gate31 = gate_tile(3, 1, at_diff + 4 * KB)
+        frame_gate(gate20, 0, w2_q[0], x_q2[0][:], x_q2[1][:], 0)
+        frame_gate(gate21, 1, w2_q[1], x_q2[0][:], x_q2[1][:], 2)
+
+        def open_banks(first, count, n0, h_g):
+            accs = [bank(first + n) for n in range(count)]
+            for n, acc in enumerate(accs):
+                last_passes(n0 + n, 0, h_g, acc)
+            return accs
+
         gated_from_banks(h_own[:, 0, :], held[0], gate01)
+        opened = open_banks(4, 2, 0, q00)
         gated_from_banks(h_own[:, 1, :], held[1], gate11)
+        opened = opened + open_banks(6, 2, 2, q00)
         q01 = quantise("q01", h_own[:, 0, :], at_w2)
         x_q3 = quantise("x_q3", x_3[:], at_w2 + KB)
         q11 = quantise("q11", h_own[:, 1, :], at_w2 + 2 * KB)
         q10 = quantise("q10", h10[:], at_w2 + 3 * KB)
 
-        gate20 = gate_tile(2, 0, at_w2 + 8 * KB)
-        gate21 = gate_tile(2, 1, at_w2 + 12 * KB)
-        gate30 = gate_tile(3, 0, at_w3)
-        gate31 = gate_tile(3, 1, at_w3 + 4 * KB)
-        frame_gate(gate20, 0, w2_q[0], x_q2[0][:], x_q2[1][:], 0)
-        memory_quarter(2, 0, 2)
-        frame_gate(gate21, 1, w2_q[1], x_q2[0][:], x_q2[1][:], 0)
-        memory_quarter(3, 0, 2)
-        frame_gate(gate30, 0, w2_q[0], x_q3[0][:], x_q3[1][:], 0)
-        frame_gate(gate31, 1, w2_q[1], x_q3[0][:], x_q3[1][:], 2)
-        late = memory_banks(2, 1, 0)
-        memory_quarter(3, 1, 2)
-
         at_results = [at_planes + 2 * KB * n for n in range(16)]
         h20 = placed("h20", [P, KB], BF16, at_pool)
         gated(nc.gpsimd, h20[:], 2, 0, gate20)
+        for n in range(4):
+            finish(0, n, (None, q01), opened[n], at_results[n])
+        frame_gate(gate30, 0, w2_q[0], x_q3[0][:], x_q3[1][:], 0)
+        frame_gate(gate31, 1, w2_q[1], x_q3[0][:], x_q3[1][:], 2)
+        late = memory_banks(2, 1, 0)
         at_h3 = room(2 * KB)
         h30 = placed("h30", [P, KB], BF16, at_h3)
         gated(nc.gpsimd, h30[:], 3, 0, gate30)
-        for n in range(4):
-            finish(0, n, (q00, q01), bank(4 + n), at_results[n])
         for n in range(2):
             finish(1, n, (q10, q11), bank(4 + n), at_results[4 + n])
         h21 = placed("h21", [P, KB], BF16, at_own)
         gated_from_banks(h21[:], late, gate21)
         copy_banks(2, 1, late)
-        q20 = quantise("q20", h20[:], at_w3)
-        q21 = quantise("q21", h21[:], at_w3 + KB)
-        q30 = quantise("q30", h30[:], at_w3 + 2 * KB)
+        finish(1, 2, (q10, q11), bank(6), at_results[6])
+        q20 = quantise("q20", h20[:], at_rest)
+        q21 = quantise("q21", h21[:], at_rest + KB)
+        q30 = quantise("q30", h30[:], at_rest + 2 * KB)
         h31 = placed("h31", [P, KB], BF16, at_h3)
         gated(nc.gpsimd, h31[:], 3, 1, gate31)
-        finish(1, 2, (q10, q11), bank(6), at_pool)
-        finish(1, 3, (q10, q11), bank(7), at_own)
-        for n in range(2):
-            finish(2, n, (q20, q21), bank(4 + n), at_results[6 + n])
+        finish(1, 3, (q10, q11), bank(7), at_pool)
+        for n in range(3):
+            finish(2, n, (q20, q21), bank(4 + n), at_results[7 + n])
+        opened = open_banks(0, 4, 0, q30)
         q31 = quantise("q31", h31[:])
-        for n in range(2, 4):
-            finish(2, n, (q20, q21), bank(4 + n), at_w3 + 2 * KB * n)
+        finish(2, 3, (q20, q21), bank(7), at_diff + 4 * KB)
         for n in range(4):
-            finish(3, n, (q30, q31), bank(n), at_results[8 + n], 2 if n == 3 else 1)
+            finish(3, n, (None, q31), opened[n], at_results[10 + n], 2 if n == 3 else 1)

@@ -255,6 +255,19 @@ def tile_list_cyclone_intensification_guidance_kernel(
         reorder_columns(w1_w[:].bitcast(U16), w1_raw[:].bitcast(U16), HALVES, LINE // 2)
         w_s = kept("w_s", [P, H], U8)
         reorder_columns(w_s[:], ws_raw[:], HALVES, LINE)
+
+        def memory_pair(c):
+            for t in range(PACK):
+                acc = bank(t)
+                memory_pass(acc[:], 0, t, c * PAIR, PAIR)
+                nc.scalar.copy(a_sb[c][0][:, t, :], acc[:])
+
+        memory_pair(0)
+        held = [memory_banks(q, 1, 4 + 2 * q) for q in range(2)]
+        for q in range(2):
+            copy_banks(q, 1, held[q])
+        memory_pair(1)
+        memory_quarter(3, 1, 0)
         w2_bf0 = weave_w2(0)
 
         at_diff = room(8 * KB)
@@ -278,23 +291,10 @@ def tile_list_cyclone_intensification_guidance_kernel(
         first_plane(2, at_early)
         first_plane(3, at_last)
 
-        x_first = kept("x_first", [P, PAIR * PACK], BF16)
+        x_first = placed("x_first", [P, PAIR * PACK], BF16, at_w2)
         for q in range(2):
             nc.scalar.copy(woven(x_first[:, q * KB : (q + 1) * KB]), by_fours(diff_first[:, :, cols(q)]))
         w2_bf1 = weave_w2(1)
-
-        def memory_pair(c):
-            for t in range(PACK):
-                acc = bank(t)
-                memory_pass(acc[:], 0, t, c * PAIR, PAIR)
-                nc.scalar.copy(a_sb[c][0][:, t, :], acc[:])
-
-        memory_pair(0)
-        held = [memory_banks(q, 1, 4 + 2 * q) for q in range(2)]
-        for q in range(2):
-            copy_banks(q, 1, held[q])
-        memory_pair(1)
-        memory_quarter(3, 1, 0)
 
         early_rest = placed("early_rest", [P, PACK - 1, PAIR], F32, at_rest)
         w3_w = placed("w3_w", [P, HALVES * H], U32, at_w3w)
@@ -315,8 +315,8 @@ def tile_list_cyclone_intensification_guidance_kernel(
             return placed("gate%d%d" % (q, b), [P, PACK, QUARTER], F32, at)[:]
 
         gate00 = diff_second[:, 2:4, :].rearrange("p s (r c) -> p (s r) c", r=2)
-        gate10 = gate_tile(1, 0, at_w2)
-        gate01 = gate_tile(0, 1, at_w2 + 4 * KB)
+        gate10 = gate_tile(1, 0, at_w2 + 4 * KB)
+        gate01 = gate_tile(0, 1, at_w2)
         gate11 = gate_tile(1, 1, at_diff)
         for q, b, gate in ((0, 0, gate00), (1, 0, gate10), (0, 1, gate01), (1, 1, gate11)):
             frame_gate(gate, b, w2_q[b], x_q[0][:, cols(q)], x_q[1][:, cols(q)], 2 * q)
@@ -357,10 +357,10 @@ def tile_list_cyclone_intensification_guidance_kernel(
         opened = open_banks(4, 2, 0, q00)
         gated_from_banks(h_own[:, 1, :], held[1], gate11)
         opened = opened + open_banks(6, 2, 2, q00)
-        q01 = quantise("q01", h_own[:, 0, :], at_w2)
-        x_q3 = quantise("x_q3", x_3[:], at_w2 + KB)
-        q11 = quantise("q11", h_own[:, 1, :], at_w2 + 2 * KB)
-        q10 = quantise("q10", h10[:], at_w2 + 3 * KB)
+        q01 = quantise("q01", h_own[:, 0, :], at_w2 + 4 * KB)
+        x_q3 = quantise("x_q3", x_3[:], at_w2 + 5 * KB)
+        q11 = quantise("q11", h_own[:, 1, :], at_w2 + 6 * KB)
+        q10 = quantise("q10", h10[:], at_w2 + 7 * KB)
 
         at_results = [at_planes + 2 * KB * n for n in range(16)]
         h20 = placed("h20", [P, KB], BF16, at_pool)

@@ -145,12 +145,15 @@ def tile_list_cyclone_intensification_guidance_kernel(
             )
             return w2_bf
 
+        def quantise_into(codes, name, src):
+            scales = kept(name + "_scales", [P, codes.shape[1]], U8)
+            nc.vector.quantize_mx(out=codes.bitcast(FP8X4), scales=scales[:], in_=src)
+            return codes, scales
+
         def quantise(name, src, at=None):
             width = src.shape[1] // PACK
             codes = kept(name, [P, width], U32) if at is None else placed(name, [P, width], U32, at)
-            scales = kept(name + "_scales", [P, width], U8)
-            nc.vector.quantize_mx(out=codes[:].bitcast(FP8X4), scales=scales[:], in_=src)
-            return codes, scales
+            return quantise_into(codes[:], name, src)
 
         a_sb = [[kept("a%d%d" % (c, b), [P, PACK, PAIR], F32) for b in range(HALVES)] for c in range(2)]
 
@@ -228,7 +231,7 @@ def tile_list_cyclone_intensification_guidance_kernel(
                     out=acc[:, cols(e)],
                     lhsT=w3_w[:, g * H + m0 : g * H + m0 + P].bitcast(FP8X4),
                     lhsT_scale=w_s[4 + 4 * g : P, m0 : m0 + P],
-                    rhs=h_g[0][:].bitcast(FP8X4),
+                    rhs=h_g[0].bitcast(FP8X4),
                     rhs_scale=h_g[1][:],
                     start=(g == 0 and e == 0),
                     stop=(g == HALVES - 1 and e == 1),
@@ -315,9 +318,10 @@ def tile_list_cyclone_intensification_guidance_kernel(
             return placed("gate%d%d" % (q, b), [P, PACK, QUARTER], F32, at)[:]
 
         gate00 = diff_second[:, 2:4, :].rearrange("p s (r c) -> p (s r) c", r=2)
-        gate10 = gate_tile(1, 0, at_w2 + 4 * KB)
+        at_gates = room(8 * KB)
+        gate10 = gate_tile(1, 0, at_gates)
         gate01 = gate_tile(0, 1, at_w2)
-        gate11 = gate_tile(1, 1, at_diff)
+        gate11 = gate_tile(1, 1, at_gates + 4 * KB)
         for q, b, gate in ((0, 0, gate00), (1, 0, gate10), (0, 1, gate01), (1, 1, gate11)):
             frame_gate(gate, b, w2_q[b], x_q[0][:, cols(q)], x_q[1][:, cols(q)], 2 * q)
 
@@ -326,15 +330,14 @@ def tile_list_cyclone_intensification_guidance_kernel(
         for t in (2, 3):
             gather_change(diff_second[:, t, cols(0)], early_rest[:, t - 1, cols(0)], t, 2)
         q00 = quantise("q00", h00[:])
-        for t in (2, 3):
-            gather_change(diff_second[:, t, cols(1)], early_rest[:, t - 1, cols(1)], t, 3)
-
         at_own = room(4 * KB)
         at_x2 = room(2 * KB) - 64
         at_pool = room(2 * KB) - 128
         x_2 = placed("x_2", [P, KB], BF16, at_x2)
         x_3 = kept("x_3", [P, KB], BF16)
-        nc.scalar.copy(woven(x_2[:]), by_fours(diff_second[:, :, cols(0)]))
+        gather_change(diff_second[:, 2, cols(1)], early_rest[:, 1, cols(1)], 2, 3)
+        nc.vector.tensor_copy(woven(x_2[:]), by_fours(diff_second[:, :, cols(0)]))
+        gather_change(diff_second[:, 3, cols(1)], early_rest[:, 2, cols(1)], 3, 3)
         nc.scalar.copy(woven(x_3[:]), by_fours(diff_second[:, :, cols(1)]))
         x_q2 = quantise("x_q2", x_2[:])
         h10 = placed("h10", [P, KB], BF16, at_pool)
@@ -344,8 +347,8 @@ def tile_list_cyclone_intensification_guidance_kernel(
         gate21 = gate_tile(2, 1, at_w2 + 12 * KB)
         gate30 = gate_tile(3, 0, at_rest)
         gate31 = gate_tile(3, 1, at_diff + 4 * KB)
-        frame_gate(gate20, 0, w2_q[0], x_q2[0][:], x_q2[1][:], 0)
-        frame_gate(gate21, 1, w2_q[1], x_q2[0][:], x_q2[1][:], 2)
+        frame_gate(gate20, 0, w2_q[0], x_q2[0], x_q2[1][:], 0)
+        frame_gate(gate21, 1, w2_q[1], x_q2[0], x_q2[1][:], 2)
 
         def open_banks(first, count, n0, h_g):
             accs = [bank(first + n) for n in range(count)]
@@ -357,18 +360,19 @@ def tile_list_cyclone_intensification_guidance_kernel(
         opened = open_banks(4, 2, 0, q00)
         gated_from_banks(h_own[:, 1, :], held[1], gate11)
         opened = opened + open_banks(6, 2, 2, q00)
-        q01 = quantise("q01", h_own[:, 0, :], at_w2 + 4 * KB)
-        x_q3 = quantise("x_q3", x_3[:], at_w2 + 5 * KB)
-        q11 = quantise("q11", h_own[:, 1, :], at_w2 + 6 * KB)
-        q10 = quantise("q10", h10[:], at_w2 + 7 * KB)
+        bundle = placed("bundle", [P, 4 * QUARTER], U32, at_gates + 2 * KB)
+        q01 = quantise_into(bundle[:, cols(0)], "q01", h_own[:, 0, :])
+        x_q3 = quantise_into(bundle[:, cols(1)], "x_q3", x_3[:])
+        q11 = quantise_into(bundle[:, cols(2)], "q11", h_own[:, 1, :])
+        q10 = quantise_into(bundle[:, cols(3)], "q10", h10[:])
 
         at_results = [at_planes + 2 * KB * n for n in range(16)]
         h20 = placed("h20", [P, KB], BF16, at_pool)
         gated(nc.gpsimd, h20[:], 2, 0, gate20)
         for n in range(4):
             finish(0, n, (None, q01), opened[n], at_results[n])
-        frame_gate(gate30, 0, w2_q[0], x_q3[0][:], x_q3[1][:], 0)
-        frame_gate(gate31, 1, w2_q[1], x_q3[0][:], x_q3[1][:], 2)
+        frame_gate(gate30, 0, w2_q[0], x_q3[0], x_q3[1][:], 0)
+        frame_gate(gate31, 1, w2_q[1], x_q3[0], x_q3[1][:], 2)
         late = memory_banks(2, 1, 0)
         at_h3 = room(2 * KB)
         h30 = placed("h30", [P, KB], BF16, at_h3)

@@ -137,8 +137,8 @@ def tile_list_cyclone_intensification_guidance_kernel(
         def by_fours(rows):
             return rows.rearrange("p t (c i) -> p c t i", i=4)
 
-        def weave_w2(b):
-            w2_bf = kept("w2_bf%d" % b, [P, PASS * PACK], BF16)
+        def weave_w2(b, at):
+            w2_bf = placed("w2_bf%d" % b, [P, PASS * PACK], BF16, at)
             nc.scalar.copy(
                 w2_bf[:].rearrange("p (u e m j) -> p u m j e", u=2, e=2, j=PACK),
                 w2_raw[b][:].rearrange("p j (m u e) -> p u m j e", u=2, e=2),
@@ -271,7 +271,7 @@ def tile_list_cyclone_intensification_guidance_kernel(
             copy_banks(q, 1, held[q])
         memory_pair(1)
         memory_quarter(3, 1, 0)
-        w2_bf0 = weave_w2(0)
+        w2_bf0 = weave_w2(0, room(4 * KB))
 
         at_diff = room(8 * KB)
         diff_first = placed("diff_first", [P, PACK, PAIR], F32, at_diff)
@@ -297,7 +297,8 @@ def tile_list_cyclone_intensification_guidance_kernel(
         x_first = placed("x_first", [P, PAIR * PACK], BF16, at_w2)
         for q in range(2):
             nc.scalar.copy(woven(x_first[:, q * KB : (q + 1) * KB]), by_fours(diff_first[:, :, cols(q)]))
-        w2_bf1 = weave_w2(1)
+        at_w2bf = room(4 * KB)
+        w2_bf1 = weave_w2(1, at_w2bf)
 
         early_rest = placed("early_rest", [P, PACK - 1, PAIR], F32, at_rest)
         w3_w = placed("w3_w", [P, HALVES * H], U32, at_w3w)
@@ -308,38 +309,41 @@ def tile_list_cyclone_intensification_guidance_kernel(
         for t in range(1, PACK):
             gather_early(early_rest[:, t - 1, :], t, 2, 2)
         w2_q0 = quantise("w2_q0", w2_bf0[:], at_w3 + 64)
+        diff_2 = placed("diff_2", [P, PACK, QUARTER], F32, at_second + 4 * KB)
+
+        def second_early(t, q):
+            return early_0[:, cols(q)] if t == 0 else early_rest[:, t - 1, cols(q)]
+
+        for t in range(PACK):
+            gather_change(diff_2[:, t, :], second_early(t, 0), t, 2)
+        x_2 = kept("x_2", [P, KB], BF16)
+        nc.vector.tensor_copy(woven(x_2[:]), by_fours(diff_2[:]))
         x_q = quantise("x_q", x_first[:], at_w3 + 64 + 2 * KB)
-        diff_second = placed("diff_second", [P, PACK, PAIR], F32, at_second)
-        gather_change(diff_second[:, 0, :], early_0[:], 0, 2, 2)
+        x_q2 = quantise("x_q2", x_2[:])
         w2_q = [w2_q0, quantise("w2_q1", w2_bf1[:])]
-        gather_change(diff_second[:, 1, :], early_rest[:, 0, :], 1, 2, 2)
+        diff_3 = placed("diff_3", [P, PACK, QUARTER], F32, at_w2bf)
+        for t in range(PACK):
+            gather_change(diff_3[:, t, :], second_early(t, 1), t, 3)
 
         def gate_tile(q, b, at):
             return placed("gate%d%d" % (q, b), [P, PACK, QUARTER], F32, at)[:]
 
-        gate00 = diff_second[:, 2:4, :].rearrange("p s (r c) -> p (s r) c", r=2)
         at_gates = room(8 * KB)
+        gate00 = gate_tile(0, 0, at_second)
         gate10 = gate_tile(1, 0, at_gates)
         gate01 = gate_tile(0, 1, at_w2)
         gate11 = gate_tile(1, 1, at_gates + 4 * KB)
         for q, b, gate in ((0, 0, gate00), (1, 0, gate10), (0, 1, gate01), (1, 1, gate11)):
             frame_gate(gate, b, w2_q[b], x_q[0][:, cols(q)], x_q[1][:, cols(q)], 2 * q)
 
-        h00 = kept("h00", [P, KB], BF16)
-        gated(nc.vector, h00[:], 0, 0, gate00)
-        for t in (2, 3):
-            gather_change(diff_second[:, t, cols(0)], early_rest[:, t - 1, cols(0)], t, 2)
-        q00 = quantise("q00", h00[:])
         at_own = room(4 * KB)
-        at_x2 = room(2 * KB) - 64
+        at_h00 = room(2 * KB) - 64
         at_pool = room(2 * KB) - 128
-        x_2 = placed("x_2", [P, KB], BF16, at_x2)
         x_3 = kept("x_3", [P, KB], BF16)
-        gather_change(diff_second[:, 2, cols(1)], early_rest[:, 1, cols(1)], 2, 3)
-        nc.vector.tensor_copy(woven(x_2[:]), by_fours(diff_second[:, :, cols(0)]))
-        gather_change(diff_second[:, 3, cols(1)], early_rest[:, 2, cols(1)], 3, 3)
-        nc.scalar.copy(woven(x_3[:]), by_fours(diff_second[:, :, cols(1)]))
-        x_q2 = quantise("x_q2", x_2[:])
+        nc.scalar.copy(woven(x_3[:]), by_fours(diff_3[:]))
+        h00 = placed("h00", [P, KB], BF16, at_h00)
+        gated(nc.vector, h00[:], 0, 0, gate00)
+        q00 = quantise("q00", h00[:])
         h10 = placed("h10", [P, KB], BF16, at_pool)
         gated(nc.gpsimd, h10[:], 1, 0, gate10)
         h_own = placed("h_own", [P, 2, KB], BF16, at_own)

@@ -113,8 +113,8 @@ def tile_list_cyclone_intensification_guidance_kernel(
         nc.vector.tensor_copy(v_s[:], tab_s[:].indirect(list_tab[:]))
         nc.vector.tensor_copy(v_w[:], tab_w[:].indirect(list_tab[:]))
 
-        def reorder_columns(dst, src, groups, per_line):
-            nc.vector.tensor_copy(
+        def reorder_columns(engine, dst, src, groups, per_line):
+            engine.tensor_copy(
                 dst.rearrange("p (g t c i) -> p g c t i", g=groups, t=PACK, i=per_line),
                 src.rearrange("p (g c i t) -> p g c t i", g=groups, t=PACK, i=per_line),
             )
@@ -255,9 +255,9 @@ def tile_list_cyclone_intensification_guidance_kernel(
                 nc.sync.dma_start(rows.rearrange("e p j -> p e j"), result[:].rearrange("p (e j) -> p e j", e=2))
 
         w1_w = kept("w1_w", [P, 2 * H], U8)
-        reorder_columns(w1_w[:].bitcast(U16), w1_raw[:].bitcast(U16), HALVES, LINE // 2)
+        reorder_columns(nc.vector, w1_w[:].bitcast(U16), w1_raw[:].bitcast(U16), HALVES, LINE // 2)
         w_s = kept("w_s", [P, H], U8)
-        reorder_columns(w_s[:], ws_raw[:], HALVES, LINE)
+        reorder_columns(nc.vector, w_s[:], ws_raw[:], HALVES, LINE)
 
         def memory_pair(c):
             for t in range(PACK):
@@ -275,7 +275,7 @@ def tile_list_cyclone_intensification_guidance_kernel(
 
         at_diff = room(8 * KB)
         diff_first = placed("diff_first", [P, PACK, PAIR], F32, at_diff)
-        at_rest = room(6 * KB)
+        at_rest = room(8 * KB)
         at_w3w = room(8 * KB)
         at_early = [room(KB) for q in range(2)]
         at_last = (at_rest, at_w3w)
@@ -288,8 +288,6 @@ def tile_list_cyclone_intensification_guidance_kernel(
                 gather_change(diff_first[:, t, cols(q)], early[q][:], t, q)
 
         first_plane(0, at_early)
-        early_0 = kept("early_second0", [P, PAIR], F32)
-        gather_early(early_0[:], 0, 2, 2)
         first_plane(1, at_early)
         first_plane(2, at_early)
         first_plane(3, at_last)
@@ -300,19 +298,16 @@ def tile_list_cyclone_intensification_guidance_kernel(
         at_w2bf = room(4 * KB)
         w2_bf1 = weave_w2(1, at_w2bf)
 
-        early_rest = placed("early_rest", [P, PACK - 1, PAIR], F32, at_rest)
+        early_rest = placed("early_rest", [P, PACK, PAIR], F32, at_rest)
         w3_w = placed("w3_w", [P, HALVES * H], U32, at_w3w)
-        nc.gpsimd.tensor_copy(
-            w3_w[:].rearrange("p (g t m) -> p g t m", g=HALVES * HALVES, t=PACK),
-            w3_raw[:].rearrange("p (g m t) -> p g t m", g=HALVES * HALVES, t=PACK),
-        )
-        for t in range(1, PACK):
-            gather_early(early_rest[:, t - 1, :], t, 2, 2)
+        reorder_columns(nc.gpsimd, w3_w[:], w3_raw[:], HALVES * HALVES, LINE // 4)
+        for t in range(PACK):
+            gather_early(early_rest[:, t, :], t, 2, 2)
         w2_q0 = quantise("w2_q0", w2_bf0[:], at_w3 + 64)
         diff_2 = placed("diff_2", [P, PACK, QUARTER], F32, at_second + 4 * KB)
 
         def second_early(t, q):
-            return early_0[:, cols(q)] if t == 0 else early_rest[:, t - 1, cols(q)]
+            return early_rest[:, t, cols(q)]
 
         for t in range(PACK):
             gather_change(diff_2[:, t, :], second_early(t, 0), t, 2)

@@ -304,7 +304,8 @@ def tile_list_cyclone_intensification_guidance_kernel(
         for t in range(PACK):
             gather_early(early_rest[:, t, :], t, 2, 2)
         w2_q0 = quantise("w2_q0", w2_bf0[:], at_w3 + 64)
-        diff_2 = placed("diff_2", [P, PACK, QUARTER], F32, at_second + 4 * KB)
+        x_q = quantise("x_q", x_first[:], at_w3 + 64 + 2 * KB)
+        diff_2 = placed("diff_2", [P, PACK, QUARTER], F32, at_w2)
 
         def second_early(t, q):
             return early_rest[:, t, cols(q)]
@@ -312,9 +313,7 @@ def tile_list_cyclone_intensification_guidance_kernel(
         for t in range(PACK):
             gather_change(diff_2[:, t, :], second_early(t, 0), t, 2)
         x_2 = kept("x_2", [P, KB], BF16)
-        nc.vector.tensor_copy(woven(x_2[:]), by_fours(diff_2[:]))
-        x_q = quantise("x_q", x_first[:], at_w3 + 64 + 2 * KB)
-        x_q2 = quantise("x_q2", x_2[:])
+        nc.scalar.copy(woven(x_2[:]), by_fours(diff_2[:]))
         w2_q = [w2_q0, quantise("w2_q1", w2_bf1[:])]
         diff_3 = placed("diff_3", [P, PACK, QUARTER], F32, at_w2bf)
         for t in range(PACK):
@@ -326,7 +325,7 @@ def tile_list_cyclone_intensification_guidance_kernel(
         at_gates = room(8 * KB)
         gate00 = gate_tile(0, 0, at_second)
         gate10 = gate_tile(1, 0, at_gates)
-        gate01 = gate_tile(0, 1, at_w2)
+        gate01 = gate_tile(0, 1, at_second + 4 * KB)
         gate11 = gate_tile(1, 1, at_gates + 4 * KB)
         for q, b, gate in ((0, 0, gate00), (1, 0, gate10), (0, 1, gate01), (1, 1, gate11)):
             frame_gate(gate, b, w2_q[b], x_q[0][:, cols(q)], x_q[1][:, cols(q)], 2 * q)
@@ -338,6 +337,7 @@ def tile_list_cyclone_intensification_guidance_kernel(
         nc.scalar.copy(woven(x_3[:]), by_fours(diff_3[:]))
         h00 = placed("h00", [P, KB], BF16, at_h00)
         gated(nc.vector, h00[:], 0, 0, gate00)
+        x_q2 = quantise("x_q2", x_2[:])
         q00 = quantise("q00", h00[:])
         h10 = placed("h10", [P, KB], BF16, at_pool)
         gated(nc.gpsimd, h10[:], 1, 0, gate10)
@@ -348,6 +348,8 @@ def tile_list_cyclone_intensification_guidance_kernel(
         gate31 = gate_tile(3, 1, at_diff + 4 * KB)
         frame_gate(gate20, 0, w2_q[0], x_q2[0], x_q2[1][:], 0)
         frame_gate(gate21, 1, w2_q[1], x_q2[0], x_q2[1][:], 2)
+        late = memory_banks(2, 1, 0)
+        copy_banks(2, 1, late)
 
         def open_banks(first, count, n0, h_g):
             accs = [bank(first + n) for n in range(count)]
@@ -370,9 +372,8 @@ def tile_list_cyclone_intensification_guidance_kernel(
         gated(nc.gpsimd, h20[:], 2, 0, gate20)
         for n in range(4):
             finish(0, n, (None, q01), opened[n], at_results[n])
-        frame_gate(gate30, 0, w2_q[0], x_q3[0], x_q3[1][:], 0)
+        frame_gate(gate30, 0, w2_q[0], x_q3[0], x_q3[1][:], 2)
         frame_gate(gate31, 1, w2_q[1], x_q3[0], x_q3[1][:], 2)
-        late = memory_banks(2, 1, 0)
         at_h3 = room(2 * KB)
         h30 = placed("h30", [P, KB], BF16, at_h3)
         gated(nc.gpsimd, h30[:], 3, 0, gate30)
@@ -380,7 +381,6 @@ def tile_list_cyclone_intensification_guidance_kernel(
             finish(1, n, (q10, q11), bank(4 + n), at_results[4 + n])
         h21 = placed("h21", [P, KB], BF16, at_own)
         gated_from_banks(h21[:], late, gate21)
-        copy_banks(2, 1, late)
         finish(1, 2, (q10, q11), bank(6), at_results[6])
         q20 = quantise("q20", h20[:], at_rest)
         q21 = quantise("q21", h21[:], at_rest + KB)

@@ -57,44 +57,45 @@ def tile_list_cyclone_intensification_guidance_kernel(
         list_early = keep.tile([P, S // 16], U16, name="list_early")
         tab_w = kept("tab_w", [P, T], U32)
         tab_s = kept("tab_s", [P, T], U8)
-        w1_raw = kept("w1_raw", [P, 2 * H], U8)
-        ws_raw = kept("ws_raw", [P, H], U8)
+        at_w1 = room(4 * KB) + 2 * KB
+        w1_raw = placed("w1_raw", [P, 2 * H], U8, at_w1)
+        ws_raw = kept("ws_raw", [P, 2, H], U8)
         bias = keep.tile([P, HALVES, PACK], F32, name="bias")
         gain = keep.tile([P, HALVES, PACK], F32, name="gain")
         at_planes = room(32 * KB)
         planes = [placed("plane%d" % t, [P, T], F32, at_planes + 8 * KB * t) for t in range(PACK)]
         at_w2 = room(16 * KB)
         w2_raw = [placed("w2_raw%d" % b, [P, PACK, PASS], F32, at_w2 + 8 * KB * b) for b in range(HALVES)]
-        at_second = room(8 * KB)
-        at_w3 = room(8 * KB) - 64
+        at_w3 = room(8 * KB)
         w3_raw = placed("w3_raw", [P, HALVES * H], U32, at_w3)
 
-        nc.vector.memset(ws_raw[:].bitcast(I32), 0)
+        nc.vector.memset(ws_raw[:, 0, :].bitcast(I32), 0)
+        nc.gpsimd.memset(ws_raw[:, 1, :].bitcast(I32), 0)
 
         x_rows = xT.rearrange("(p t) c -> t p c", t=PACK)
         w2_rows = w2.rearrange("(p j) c -> p j c", j=PACK)
 
-        def load_weight_scales(q, first):
-            rows = slice(4 * q, 4 * q + 4)
-            if first:
-                nc.sync.dma_start(ws_raw[32 * q : 32 * q + 4, :].bitcast(I32), w1_scales[0, rows, :].bitcast(I32))
-            else:
-                nc.sync.dma_start(ws_raw[32 * q + 4 : 32 * q + 12, :].bitcast(I32), w3_scales[:, rows, :].bitcast(I32))
+        def scale_rows(q):
+            return slice(4 * q, 4 * q + 4)
 
-        scale_loads = [(q, first) for q in range(QUADRANTS) for first in (True, False)]
+        def load_w1_scales(q):
+            nc.sync.dma_start(
+                ws_raw[32 * q : 32 * q + 4, 0, :].bitcast(I32), w1_scales[0, scale_rows(q), :].bitcast(I32)
+            )
+
         nc.sync.dma_start(list_tab[:], offs)
         for q in range(QUADRANTS):
-            rows = tab_scales[0, 4 * q : 4 * q + 4, :].bitcast(I32)
+            rows = tab_scales[0, scale_rows(q), :].bitcast(I32)
             nc.sync.dma_start(tab_s[32 * q : 32 * q + 32, :].bitcast(I32), rows.partition_broadcast(8))
-        for q, first in scale_loads[:2]:
-            load_weight_scales(q, first)
         nc.sync.dma_start(tab_w[:].bitcast(I32), tab_words[0].rearrange("p c i -> p (c i)").bitcast(I32))
-        for q, first in scale_loads[2:7]:
-            load_weight_scales(q, first)
+        for q in range(QUADRANTS):
+            load_w1_scales(q)
         nc.sync.dma_start(w1_raw[:].bitcast(I32), w1_words[0].bitcast(I32))
         nc.sync.dma_start(planes[0][:], x_rows[0])
-        for q, first in scale_loads[7:]:
-            load_weight_scales(q, first)
+        for q in range(QUADRANTS):
+            nc.sync.dma_start(
+                ws_raw[32 * q : 32 * q + 8, 1, :].bitcast(I32), w3_scales[:, scale_rows(q), :].bitcast(I32)
+            )
         nc.sync.dma_start(list_early[:], offs3)
         nc.sync.dma_start(list_late[:], offs2)
         for t in range(1, PACK):
@@ -109,9 +110,8 @@ def tile_list_cyclone_intensification_guidance_kernel(
         nc.sync.dma_start(gain[:], res.rearrange("(b p t) -> p b t", b=HALVES, t=PACK))
 
         v_s = kept("v_s", [P, S], U8)
-        v_w = kept("v_w", [P, S], U32)
+        v_w = [kept("v_w0", [P, PAIR], U32)]
         nc.vector.tensor_copy(v_s[:], tab_s[:].indirect(list_tab[:]))
-        nc.vector.tensor_copy(v_w[:], tab_w[:].indirect(list_tab[:]))
 
         def reorder_columns(engine, dst, src, groups, per_line):
             engine.tensor_copy(
@@ -137,13 +137,11 @@ def tile_list_cyclone_intensification_guidance_kernel(
         def by_fours(rows):
             return rows.rearrange("p t (c i) -> p c t i", i=4)
 
-        def weave_w2(b, at):
-            w2_bf = placed("w2_bf%d" % b, [P, PASS * PACK], BF16, at)
+        def weave_w2(b, w2_bf):
             nc.scalar.copy(
-                w2_bf[:].rearrange("p (u e m j) -> p u m j e", u=2, e=2, j=PACK),
+                w2_bf.rearrange("p (u e m j) -> p u m j e", u=2, e=2, j=PACK),
                 w2_raw[b][:].rearrange("p j (m u e) -> p u m j e", u=2, e=2),
             )
-            return w2_bf
 
         def quantise_into(codes, name, src):
             scales = kept(name + "_scales", [P, codes.shape[1]], U8)
@@ -165,8 +163,8 @@ def tile_list_cyclone_intensification_guidance_kernel(
             nc.tensor.matmul_mx(
                 out=acc,
                 lhsT=w1_w[:, 2 * m0 : 2 * (m0 + P)].bitcast(FP4X4),
-                lhsT_scale=w_s[:, m0 : m0 + P],
-                rhs=v_w[:, lo : lo + width].bitcast(FP8X4),
+                lhsT_scale=w1_s[:, m0 : m0 + P],
+                rhs=v_w[lo // PAIR][:, lo % PAIR : lo % PAIR + width].bitcast(FP8X4),
                 rhs_scale=v_s[:, lo : lo + width],
                 start=True,
                 stop=True,
@@ -192,20 +190,22 @@ def tile_list_cyclone_intensification_guidance_kernel(
                     memory_pass(acc[:, cols(e)], b, 2 * u + e, q * QUARTER, QUARTER)
                 nc.scalar.copy(a_rows(q, b)[:, 2 * u : 2 * u + 2, :], acc[:].rearrange("p (e c) -> p e c", e=2))
 
-        def frame_gate(gate, b, w2_q, x_codes, x_scales, first):
+        def gate_pass(acc, w2_half, t, x_codes, x_scales):
+            nc.tensor.matmul_mx(
+                out=acc,
+                lhsT=w2_half[0][:, t * P : (t + 1) * P].bitcast(FP8X4),
+                lhsT_scale=w2_half[1][:, t * P : (t + 1) * P],
+                rhs=x_codes.bitcast(FP8X4),
+                rhs_scale=x_scales,
+                start=True,
+                stop=True,
+            )
+
+        def frame_gate(gate, b, w2_half, x_codes, x_scales, first):
             for u in range(2):
                 acc = bank(first + u)
                 for e in range(2):
-                    t = 2 * u + e
-                    nc.tensor.matmul_mx(
-                        out=acc[:, cols(e)],
-                        lhsT=w2_q[0][:, t * P : (t + 1) * P].bitcast(FP8X4),
-                        lhsT_scale=w2_q[1][:, t * P : (t + 1) * P],
-                        rhs=x_codes.bitcast(FP8X4),
-                        rhs_scale=x_scales,
-                        start=True,
-                        stop=True,
-                    )
+                    gate_pass(acc[:, cols(e)], w2_half, 2 * u + e, x_codes, x_scales)
                 for e in range(2):
                     t = 2 * u + e
                     nc.scalar.activation(gate[:, t, :], acc[:, cols(e)], ACT.Sigmoid, bias=bias[:, b, t : t + 1])
@@ -230,7 +230,7 @@ def tile_list_cyclone_intensification_guidance_kernel(
                 nc.tensor.matmul_mx(
                     out=acc[:, cols(e)],
                     lhsT=w3_w[:, g * H + m0 : g * H + m0 + P].bitcast(FP8X4),
-                    lhsT_scale=w_s[4 + 4 * g : P, m0 : m0 + P],
+                    lhsT_scale=w3_s[4 * g : P, m0 : m0 + P],
                     rhs=h_g[0].bitcast(FP8X4),
                     rhs_scale=h_g[1][:],
                     start=(g == 0 and e == 0),
@@ -254,10 +254,15 @@ def tile_list_cyclone_intensification_guidance_kernel(
             if stores == 1:
                 nc.sync.dma_start(rows.rearrange("e p j -> p e j"), result[:].rearrange("p (e j) -> p e j", e=2))
 
+        nc.vector.tensor_copy(v_w[0][:], tab_w[:].indirect(entries(list_tab, 0, 2)))
+        w1_s = kept("w1_s", [P, H], U8)
+        reorder_columns(nc.vector, w1_s[:], ws_raw[:, 0, :], HALVES, LINE)
         w1_w = kept("w1_w", [P, 2 * H], U8)
         reorder_columns(nc.vector, w1_w[:].bitcast(U16), w1_raw[:].bitcast(U16), HALVES, LINE // 2)
-        w_s = kept("w_s", [P, H], U8)
-        reorder_columns(nc.vector, w_s[:], ws_raw[:], HALVES, LINE)
+        v_w.append(placed("v_w1", [P, PAIR], U32, at_w1 - 2 * KB + 64))
+        nc.vector.tensor_copy(v_w[1][:], tab_w[:].indirect(entries(list_tab, 2, 2)))
+        w3_s = placed("w3_s", [P, H], U8, at_w1 + 64)
+        reorder_columns(nc.gpsimd, w3_s[:], ws_raw[:, 1, :], HALVES, LINE)
 
         def memory_pair(c):
             for t in range(PACK):
@@ -271,7 +276,8 @@ def tile_list_cyclone_intensification_guidance_kernel(
             copy_banks(q, 1, held[q])
         memory_pair(1)
         memory_quarter(3, 1, 0)
-        w2_bf0 = weave_w2(0, room(4 * KB))
+        w2_bf0 = kept("w2_bf0", [P, PASS * PACK], BF16)
+        weave_w2(0, w2_bf0[:])
 
         at_diff = room(8 * KB)
         diff_first = placed("diff_first", [P, PACK, PAIR], F32, at_diff)
@@ -292,49 +298,57 @@ def tile_list_cyclone_intensification_guidance_kernel(
         first_plane(2, at_early)
         first_plane(3, at_last)
 
-        x_first = placed("x_first", [P, PAIR * PACK], BF16, at_w2)
+        third = placed("third", [P, 6 * QUARTER], F32, at_w2)
+        x_first = third[:, 2 * QUARTER : 6 * QUARTER].bitcast(BF16)
+        diff_2 = third[:, 0 : 4 * QUARTER].rearrange("p (t c) -> p t c", t=PACK)
         for q in range(2):
             nc.scalar.copy(woven(x_first[:, q * KB : (q + 1) * KB]), by_fours(diff_first[:, :, cols(q)]))
         at_w2bf = room(4 * KB)
-        w2_bf1 = weave_w2(1, at_w2bf)
+        w2_bf1 = placed("w2_bf1", [P, PASS * PACK], BF16, at_w2bf)
+        weave_w2(1, w2_bf1[:])
 
         early_rest = placed("early_rest", [P, PACK, PAIR], F32, at_rest)
         w3_w = placed("w3_w", [P, HALVES * H], U32, at_w3w)
         reorder_columns(nc.gpsimd, w3_w[:], w3_raw[:], HALVES * HALVES, LINE // 4)
         for t in range(PACK):
             gather_early(early_rest[:, t, :], t, 2, 2)
+
+        def second_change(diff, t, q):
+            gather_change(diff[:, t, :], early_rest[:, t, cols(q - 2)], t, q)
+
+        second_change(diff_2, 0, 2)
+        second_change(diff_2, 1, 2)
         w2_q0 = quantise("w2_q0", w2_bf0[:], at_w3 + 64)
-        x_q = quantise("x_q", x_first[:], at_w3 + 64 + 2 * KB)
-        diff_2 = placed("diff_2", [P, PACK, QUARTER], F32, at_w2)
-
-        def second_early(t, q):
-            return early_rest[:, t, cols(q)]
-
-        for t in range(PACK):
-            gather_change(diff_2[:, t, :], second_early(t, 0), t, 2)
-        x_2 = kept("x_2", [P, KB], BF16)
-        nc.scalar.copy(woven(x_2[:]), by_fours(diff_2[:]))
+        x_q = quantise("x_q", x_first, at_w3 + 64 + 2 * KB)
+        second_change(diff_2, 2, 2)
+        second_change(diff_2, 3, 2)
         w2_q = [w2_q0, quantise("w2_q1", w2_bf1[:])]
-        diff_3 = placed("diff_3", [P, PACK, QUARTER], F32, at_w2bf)
+        diff_3 = placed("diff_3", [P, PACK, QUARTER], F32, at_w2bf)[:]
         for t in range(PACK):
-            gather_change(diff_3[:, t, :], second_early(t, 1), t, 3)
+            second_change(diff_3, t, 3)
 
         def gate_tile(q, b, at):
             return placed("gate%d%d" % (q, b), [P, PACK, QUARTER], F32, at)[:]
 
-        at_gates = room(8 * KB)
-        gate00 = gate_tile(0, 0, at_second)
-        gate10 = gate_tile(1, 0, at_gates)
-        gate01 = gate_tile(0, 1, at_second + 4 * KB)
-        gate11 = gate_tile(1, 1, at_gates + 4 * KB)
-        for q, b, gate in ((0, 0, gate00), (1, 0, gate10), (0, 1, gate01), (1, 1, gate11)):
-            frame_gate(gate, b, w2_q[b], x_q[0][:, cols(q)], x_q[1][:, cols(q)], 2 * q)
+        at_gates = room(16 * KB)
+        gates = placed("gates", [P, PACK, PAIR], F32, at_gates)
+        gate00, gate10 = (gates[:, :, cols(q)] for q in range(2))
+        gate11 = gate_tile(1, 1, at_gates + 8 * KB)
+        gate01 = gate_tile(0, 1, at_gates + 12 * KB)
+        for t in range(PACK):
+            acc = bank(t)
+            gate_pass(acc[:], w2_q[0], t, x_q[0], x_q[1][:])
+            nc.scalar.activation(gates[:, t, :], acc[:], ACT.Sigmoid, bias=bias[:, 0, t : t + 1])
+        x_2 = kept("x_2", [P, KB], BF16)
+        nc.scalar.copy(woven(x_2[:]), by_fours(diff_2))
+        for q, gate in enumerate((gate01, gate11)):
+            frame_gate(gate, 1, w2_q[1], x_q[0][:, cols(q)], x_q[1][:, cols(q)], 2 * q)
 
         at_own = room(4 * KB)
         at_h00 = room(2 * KB) - 64
         at_pool = room(2 * KB) - 128
         x_3 = kept("x_3", [P, KB], BF16)
-        nc.scalar.copy(woven(x_3[:]), by_fours(diff_3[:]))
+        nc.scalar.copy(woven(x_3[:]), by_fours(diff_3))
         h00 = placed("h00", [P, KB], BF16, at_h00)
         gated(nc.vector, h00[:], 0, 0, gate00)
         x_q2 = quantise("x_q2", x_2[:])
@@ -361,7 +375,7 @@ def tile_list_cyclone_intensification_guidance_kernel(
         opened = open_banks(4, 2, 0, q00)
         gated_from_banks(h_own[:, 1, :], held[1], gate11)
         opened = opened + open_banks(6, 2, 2, q00)
-        bundle = placed("bundle", [P, 4 * QUARTER], U32, at_gates + 2 * KB)
+        bundle = placed("bundle", [P, 4 * QUARTER], U32, at_gates + 6 * KB)
         q01 = quantise_into(bundle[:, cols(0)], "q01", h_own[:, 0, :])
         x_q3 = quantise_into(bundle[:, cols(1)], "x_q3", x_3[:])
         q11 = quantise_into(bundle[:, cols(2)], "q11", h_own[:, 1, :])

@@ -57,15 +57,18 @@ def tile_list_cyclone_intensification_guidance_kernel(
         list_early = keep.tile([P, S // 16], U16, name="list_early")
         tab_w = kept("tab_w", [P, T], U32)
         tab_s = kept("tab_s", [P, T], U8)
-        at_w1 = room(4 * KB) + 2 * KB
-        w1_raw = placed("w1_raw", [P, 2 * H], U8, at_w1)
+        w1_raw = kept("w1_raw", [P, 2 * H], U8)
         ws_raw = kept("ws_raw", [P, 2, H], U8)
         bias = keep.tile([P, HALVES, PACK], F32, name="bias")
         gain = keep.tile([P, HALVES, PACK], F32, name="gain")
         at_planes = room(32 * KB)
         planes = [placed("plane%d" % t, [P, T], F32, at_planes + 8 * KB * t) for t in range(PACK)]
         at_w2 = room(16 * KB)
-        w2_raw = [placed("w2_raw%d" % b, [P, PACK, PASS], F32, at_w2 + 8 * KB * b) for b in range(HALVES)]
+        w2_parts = [(0, 0, PASS // 2), (0, PASS // 2, PASS // 2), (1, 0, PASS)]
+        w2_raw = [
+            placed("w2_raw%d" % n, [P, PACK, width], F32, at_w2 + 16 * (b * PASS + lo))
+            for n, (b, lo, width) in enumerate(w2_parts)
+        ]
         at_w3 = room(8 * KB)
         w3_raw = placed("w3_raw", [P, HALVES * H], U32, at_w3)
 
@@ -92,25 +95,26 @@ def tile_list_cyclone_intensification_guidance_kernel(
             load_w1_scales(q)
         nc.sync.dma_start(w1_raw[:].bitcast(I32), w1_words[0].bitcast(I32))
         nc.sync.dma_start(planes[0][:], x_rows[0])
-        for q in range(QUADRANTS):
-            nc.sync.dma_start(
-                ws_raw[32 * q : 32 * q + 8, 1, :].bitcast(I32), w3_scales[:, scale_rows(q), :].bitcast(I32)
-            )
         nc.sync.dma_start(list_early[:], offs3)
         nc.sync.dma_start(list_late[:], offs2)
         for t in range(1, PACK):
             nc.sync.dma_start(planes[t][:], x_rows[t])
-        nc.sync.dma_start(w2_raw[0][:], w2_rows[:, :, 0:PASS])
+        for q in range(QUADRANTS):
+            nc.sync.dma_start(
+                ws_raw[32 * q : 32 * q + 8, 1, :].bitcast(I32), w3_scales[:, scale_rows(q), :].bitcast(I32)
+            )
+        for n in range(2):
+            nc.sync.dma_start(w2_raw[n][:], w2_rows[:, :, n * PASS // 2 : (n + 1) * PASS // 2])
         nc.sync.dma_start(
             w3_raw[:].bitcast(I32).rearrange("p (g c) -> p g c", g=HALVES),
             w3_words.rearrange("g p c i -> p g (c i)").bitcast(I32),
         )
-        nc.sync.dma_start(w2_raw[1][:], w2_rows[:, :, PASS : 2 * PASS])
+        nc.sync.dma_start(w2_raw[2][:], w2_rows[:, :, PASS : 2 * PASS])
         nc.sync.dma_start(bias[:], b2.rearrange("(b p t) -> p b t", b=HALVES, t=PACK))
         nc.sync.dma_start(gain[:], res.rearrange("(b p t) -> p b t", b=HALVES, t=PACK))
 
         v_s = kept("v_s", [P, S], U8)
-        v_w = [kept("v_w0", [P, PAIR], U32)]
+        v_w = kept("v_w", [P, S], U32)
         nc.vector.tensor_copy(v_s[:], tab_s[:].indirect(list_tab[:]))
 
         def reorder_columns(engine, dst, src, groups, per_line):
@@ -137,10 +141,11 @@ def tile_list_cyclone_intensification_guidance_kernel(
         def by_fours(rows):
             return rows.rearrange("p t (c i) -> p c t i", i=4)
 
-        def weave_w2(b, w2_bf):
+        def weave_w2(n, w2_bf):
+            lo, width = w2_parts[n][1:]
             nc.scalar.copy(
-                w2_bf.rearrange("p (u e m j) -> p u m j e", u=2, e=2, j=PACK),
-                w2_raw[b][:].rearrange("p j (m u e) -> p u m j e", u=2, e=2),
+                w2_bf.rearrange("p (u e m j) -> p u m j e", u=2, e=2, j=PACK)[:, :, lo // PACK : (lo + width) // PACK],
+                w2_raw[n][:].rearrange("p j (m u e) -> p u m j e", u=2, e=2),
             )
 
         def quantise_into(codes, name, src):
@@ -164,7 +169,7 @@ def tile_list_cyclone_intensification_guidance_kernel(
                 out=acc,
                 lhsT=w1_w[:, 2 * m0 : 2 * (m0 + P)].bitcast(FP4X4),
                 lhsT_scale=w1_s[:, m0 : m0 + P],
-                rhs=v_w[lo // PAIR][:, lo % PAIR : lo % PAIR + width].bitcast(FP8X4),
+                rhs=v_w[:, lo : lo + width].bitcast(FP8X4),
                 rhs_scale=v_s[:, lo : lo + width],
                 start=True,
                 stop=True,
@@ -254,15 +259,11 @@ def tile_list_cyclone_intensification_guidance_kernel(
             if stores == 1:
                 nc.sync.dma_start(rows.rearrange("e p j -> p e j"), result[:].rearrange("p (e j) -> p e j", e=2))
 
-        nc.vector.tensor_copy(v_w[0][:], tab_w[:].indirect(entries(list_tab, 0, 2)))
+        nc.vector.tensor_copy(v_w[:], tab_w[:].indirect(list_tab[:]))
         w1_s = kept("w1_s", [P, H], U8)
-        reorder_columns(nc.vector, w1_s[:], ws_raw[:, 0, :], HALVES, LINE)
+        reorder_columns(nc.gpsimd, w1_s[:], ws_raw[:, 0, :], HALVES, LINE)
         w1_w = kept("w1_w", [P, 2 * H], U8)
         reorder_columns(nc.vector, w1_w[:].bitcast(U16), w1_raw[:].bitcast(U16), HALVES, LINE // 2)
-        v_w.append(placed("v_w1", [P, PAIR], U32, at_w1 - 2 * KB + 64))
-        nc.vector.tensor_copy(v_w[1][:], tab_w[:].indirect(entries(list_tab, 2, 2)))
-        w3_s = placed("w3_s", [P, H], U8, at_w1 + 64)
-        reorder_columns(nc.gpsimd, w3_s[:], ws_raw[:, 1, :], HALVES, LINE)
 
         def memory_pair(c):
             for t in range(PACK):
@@ -278,11 +279,12 @@ def tile_list_cyclone_intensification_guidance_kernel(
         memory_quarter(3, 1, 0)
         w2_bf0 = kept("w2_bf0", [P, PASS * PACK], BF16)
         weave_w2(0, w2_bf0[:])
+        weave_w2(1, w2_bf0[:])
 
         at_diff = room(8 * KB)
         diff_first = placed("diff_first", [P, PACK, PAIR], F32, at_diff)
         at_rest = room(8 * KB)
-        at_w3w = room(8 * KB)
+        at_w3w = room(10 * KB) + KB
         at_early = [room(KB) for q in range(2)]
         at_last = (at_rest, at_w3w)
 
@@ -305,10 +307,12 @@ def tile_list_cyclone_intensification_guidance_kernel(
             nc.scalar.copy(woven(x_first[:, q * KB : (q + 1) * KB]), by_fours(diff_first[:, :, cols(q)]))
         at_w2bf = room(4 * KB)
         w2_bf1 = placed("w2_bf1", [P, PASS * PACK], BF16, at_w2bf)
-        weave_w2(1, w2_bf1[:])
+        weave_w2(2, w2_bf1[:])
 
         early_rest = placed("early_rest", [P, PACK, PAIR], F32, at_rest)
-        w3_w = placed("w3_w", [P, HALVES * H], U32, at_w3w)
+        w3_s = placed("w3_s", [P, H], U8, at_w3w - KB + 64)
+        reorder_columns(nc.gpsimd, w3_s[:], ws_raw[:, 1, :], HALVES, LINE)
+        w3_w = placed("w3_w", [P, HALVES * H], U32, at_w3w + 64)
         reorder_columns(nc.gpsimd, w3_w[:], w3_raw[:], HALVES * HALVES, LINE // 4)
         for t in range(PACK):
             gather_early(early_rest[:, t, :], t, 2, 2)

@@ -64,6 +64,7 @@ def tile_list_cyclone_intensification_guidance_kernel(
         at_planes = room(32 * KB)
         planes = [placed("plane%d" % t, [P, T], F32, at_planes + 8 * KB * t) for t in range(PACK)]
         at_w2 = room(16 * KB)
+        at_gates = room(8 * KB) - 8 * KB
         w2_parts = [(0, 0, PASS // 2), (0, PASS // 2, PASS // 2), (1, 0, PASS)]
         w2_raw = [
             placed("w2_raw%d" % n, [P, PACK, width], F32, at_w2 + 16 * (b * PASS + lo))
@@ -72,8 +73,13 @@ def tile_list_cyclone_intensification_guidance_kernel(
         at_w3 = room(8 * KB)
         w3_raw = placed("w3_raw", [P, HALVES * H], U32, at_w3)
 
+        nc.gpsimd.memset(tab_s[:].bitcast(I32), 0)
         nc.vector.memset(ws_raw[:, 0, :].bitcast(I32), 0)
         nc.gpsimd.memset(ws_raw[:, 1, :].bitcast(I32), 0)
+
+        warm = keep.tile([P, 2], F32, name="warm")
+        nc.gpsimd.memset(warm[:, 0:1], 0.0)
+        nc.scalar.activation(warm[:, 1:2], warm[:, 0:1], ACT.Sigmoid)
 
         x_rows = xT.rearrange("(p t) c -> t p c", t=PACK)
         w2_rows = w2.rearrange("(p j) c -> p j c", j=PACK)
@@ -89,7 +95,7 @@ def tile_list_cyclone_intensification_guidance_kernel(
         nc.sync.dma_start(list_tab[:], offs)
         for q in range(QUADRANTS):
             rows = tab_scales[0, scale_rows(q), :].bitcast(I32)
-            nc.sync.dma_start(tab_s[32 * q : 32 * q + 32, :].bitcast(I32), rows.partition_broadcast(8))
+            nc.scalar.dma_start(tab_s[32 * q : 32 * q + 4, :].bitcast(I32), rows)
         nc.sync.dma_start(tab_w[:].bitcast(I32), tab_words[0].rearrange("p c i -> p (c i)").bitcast(I32))
         for q in range(QUADRANTS):
             load_w1_scales(q)
@@ -117,8 +123,8 @@ def tile_list_cyclone_intensification_guidance_kernel(
         v_w = kept("v_w", [P, S], U32)
         nc.vector.tensor_copy(v_s[:], tab_s[:].indirect(list_tab[:]))
 
-        def reorder_columns(engine, dst, src, groups, per_line):
-            engine.tensor_copy(
+        def reorder_columns(move, dst, src, groups, per_line):
+            move(
                 dst.rearrange("p (g t c i) -> p g c t i", g=groups, t=PACK, i=per_line),
                 src.rearrange("p (g c i t) -> p g c t i", g=groups, t=PACK, i=per_line),
             )
@@ -261,9 +267,9 @@ def tile_list_cyclone_intensification_guidance_kernel(
 
         nc.vector.tensor_copy(v_w[:], tab_w[:].indirect(list_tab[:]))
         w1_s = kept("w1_s", [P, H], U8)
-        reorder_columns(nc.gpsimd, w1_s[:], ws_raw[:, 0, :], HALVES, LINE)
+        reorder_columns(nc.gpsimd.tensor_copy, w1_s[:], ws_raw[:, 0, :], HALVES, LINE)
         w1_w = kept("w1_w", [P, 2 * H], U8)
-        reorder_columns(nc.vector, w1_w[:].bitcast(U16), w1_raw[:].bitcast(U16), HALVES, LINE // 2)
+        reorder_columns(nc.scalar.copy, w1_w[:].bitcast(U16), w1_raw[:].bitcast(U16), HALVES, LINE // 2)
 
         def memory_pair(c):
             for t in range(PACK):
@@ -311,9 +317,9 @@ def tile_list_cyclone_intensification_guidance_kernel(
 
         early_rest = placed("early_rest", [P, PACK, PAIR], F32, at_rest)
         w3_s = placed("w3_s", [P, H], U8, at_w3w - KB + 64)
-        reorder_columns(nc.gpsimd, w3_s[:], ws_raw[:, 1, :], HALVES, LINE)
+        reorder_columns(nc.gpsimd.tensor_copy, w3_s[:], ws_raw[:, 1, :], HALVES, LINE)
         w3_w = placed("w3_w", [P, HALVES * H], U32, at_w3w + 64)
-        reorder_columns(nc.gpsimd, w3_w[:], w3_raw[:], HALVES * HALVES, LINE // 4)
+        reorder_columns(nc.gpsimd.tensor_copy, w3_w[:], w3_raw[:], HALVES * HALVES, LINE // 4)
         for t in range(PACK):
             gather_early(early_rest[:, t, :], t, 2, 2)
 
@@ -334,7 +340,7 @@ def tile_list_cyclone_intensification_guidance_kernel(
         def gate_tile(q, b, at):
             return placed("gate%d%d" % (q, b), [P, PACK, QUARTER], F32, at)[:]
 
-        at_gates = room(16 * KB)
+        at_later = room(8 * KB)
         gates = placed("gates", [P, PACK, PAIR], F32, at_gates)
         gate00, gate10 = (gates[:, :, cols(q)] for q in range(2))
         gate11 = gate_tile(1, 1, at_gates + 8 * KB)
@@ -343,14 +349,14 @@ def tile_list_cyclone_intensification_guidance_kernel(
             acc = bank(t)
             gate_pass(acc[:], w2_q[0], t, x_q[0], x_q[1][:])
             nc.scalar.activation(gates[:, t, :], acc[:], ACT.Sigmoid, bias=bias[:, 0, t : t + 1])
-        x_2 = kept("x_2", [P, KB], BF16)
+        at_pool = room(2 * KB)
+        x_2 = placed("x_2", [P, KB], BF16, at_pool)
         nc.scalar.copy(woven(x_2[:]), by_fours(diff_2))
         for q, gate in enumerate((gate01, gate11)):
             frame_gate(gate, 1, w2_q[1], x_q[0][:, cols(q)], x_q[1][:, cols(q)], 2 * q)
 
         at_own = room(4 * KB)
         at_h00 = room(2 * KB) - 64
-        at_pool = room(2 * KB) - 128
         x_3 = kept("x_3", [P, KB], BF16)
         nc.scalar.copy(woven(x_3[:]), by_fours(diff_3))
         h00 = placed("h00", [P, KB], BF16, at_h00)
@@ -360,8 +366,8 @@ def tile_list_cyclone_intensification_guidance_kernel(
         h10 = placed("h10", [P, KB], BF16, at_pool)
         gated(nc.gpsimd, h10[:], 1, 0, gate10)
         h_own = placed("h_own", [P, 2, KB], BF16, at_own)
-        gate20 = gate_tile(2, 0, at_w2 + 8 * KB)
-        gate21 = gate_tile(2, 1, at_w2 + 12 * KB)
+        gate20 = gate_tile(2, 0, at_later)
+        gate21 = gate_tile(2, 1, at_later + 4 * KB)
         gate30 = gate_tile(3, 0, at_rest)
         gate31 = gate_tile(3, 1, at_diff + 4 * KB)
         frame_gate(gate20, 0, w2_q[0], x_q2[0], x_q2[1][:], 0)
@@ -382,8 +388,8 @@ def tile_list_cyclone_intensification_guidance_kernel(
         bundle = placed("bundle", [P, 4 * QUARTER], U32, at_gates + 6 * KB)
         q01 = quantise_into(bundle[:, cols(0)], "q01", h_own[:, 0, :])
         x_q3 = quantise_into(bundle[:, cols(1)], "x_q3", x_3[:])
-        q11 = quantise_into(bundle[:, cols(2)], "q11", h_own[:, 1, :])
         q10 = quantise_into(bundle[:, cols(3)], "q10", h10[:])
+        q11 = quantise_into(bundle[:, cols(2)], "q11", h_own[:, 1, :])
 
         at_results = [at_planes + 2 * KB * n for n in range(16)]
         h20 = placed("h20", [P, KB], BF16, at_pool)
@@ -401,8 +407,8 @@ def tile_list_cyclone_intensification_guidance_kernel(
         gated_from_banks(h21[:], late, gate21)
         finish(1, 2, (q10, q11), bank(6), at_results[6])
         q20 = quantise("q20", h20[:], at_rest)
-        q21 = quantise("q21", h21[:], at_rest + KB)
         q30 = quantise("q30", h30[:], at_rest + 2 * KB)
+        q21 = quantise("q21", h21[:], at_rest + KB)
         h31 = placed("h31", [P, KB], BF16, at_h3)
         gated(nc.gpsimd, h31[:], 3, 1, gate31)
         finish(1, 3, (q10, q11), bank(7), at_pool)

@@ -73,7 +73,6 @@ def tile_list_cyclone_intensification_guidance_kernel(
         at_w3 = room(8 * KB)
         w3_raw = placed("w3_raw", [P, HALVES * H], U32, at_w3)
 
-        nc.gpsimd.memset(tab_s[:].bitcast(I32), 0)
         nc.vector.memset(ws_raw[:, 0, :].bitcast(I32), 0)
         nc.gpsimd.memset(ws_raw[:, 1, :].bitcast(I32), 0)
 
@@ -95,7 +94,7 @@ def tile_list_cyclone_intensification_guidance_kernel(
         nc.sync.dma_start(list_tab[:], offs)
         for q in range(QUADRANTS):
             rows = tab_scales[0, scale_rows(q), :].bitcast(I32)
-            nc.scalar.dma_start(tab_s[32 * q : 32 * q + 4, :].bitcast(I32), rows)
+            nc.sync.dma_start(tab_s[32 * q : 32 * q + 32, :].bitcast(I32), rows.partition_broadcast(8))
         nc.sync.dma_start(tab_w[:].bitcast(I32), tab_words[0].rearrange("p c i -> p (c i)").bitcast(I32))
         for q in range(QUADRANTS):
             load_w1_scales(q)
@@ -407,15 +406,17 @@ def tile_list_cyclone_intensification_guidance_kernel(
         gated_from_banks(h21[:], late, gate21)
         finish(1, 2, (q10, q11), bank(6), at_results[6])
         q20 = quantise("q20", h20[:], at_rest)
-        q30 = quantise("q30", h30[:], at_rest + 2 * KB)
+        opened = [open_banks(first, 1, n, q20)[0] for n, first in enumerate((4, 7))]
         q21 = quantise("q21", h21[:], at_rest + KB)
+        q30 = quantise("q30", h30[:], at_rest + 2 * KB)
         h31 = placed("h31", [P, KB], BF16, at_h3)
         gated(nc.gpsimd, h31[:], 3, 1, gate31)
-        finish(1, 3, (q10, q11), bank(7), at_pool)
-        for n in range(3):
-            finish(2, n, (q20, q21), bank(4 + n), at_results[7 + n])
+        finish(1, 3, (q10, q11), bank(5), at_pool)
+        for n in range(2):
+            finish(2, n, (None, q21), opened[n], at_results[7 + n])
+        finish(2, 2, (q20, q21), bank(6), at_results[9])
         opened = open_banks(0, 4, 0, q30)
         q31 = quantise("q31", h31[:])
-        finish(2, 3, (q20, q21), bank(7), at_diff + 4 * KB)
+        finish(2, 3, (q20, q21), bank(5), at_diff + 4 * KB)
         for n in range(4):
             finish(3, n, (None, q31), opened[n], at_results[10 + n], 2 if n == 3 else 1)

@@ -64,7 +64,6 @@ def tile_list_cyclone_intensification_guidance_kernel(
         at_planes = room(32 * KB)
         planes = [placed("plane%d" % t, [P, T], F32, at_planes + 8 * KB * t) for t in range(PACK)]
         at_w2 = room(16 * KB)
-        at_gates = room(8 * KB) - 8 * KB
         w2_parts = [(0, 0, PASS // 2), (0, PASS // 2, PASS // 2), (1, 0, PASS)]
         w2_raw = [
             placed("w2_raw%d" % n, [P, PACK, width], F32, at_w2 + 16 * (b * PASS + lo))
@@ -339,7 +338,7 @@ def tile_list_cyclone_intensification_guidance_kernel(
         def gate_tile(q, b, at):
             return placed("gate%d%d" % (q, b), [P, PACK, QUARTER], F32, at)[:]
 
-        at_later = room(8 * KB)
+        at_gates = room(16 * KB)
         gates = placed("gates", [P, PACK, PAIR], F32, at_gates)
         gate00, gate10 = (gates[:, :, cols(q)] for q in range(2))
         gate11 = gate_tile(1, 1, at_gates + 8 * KB)
@@ -365,8 +364,8 @@ def tile_list_cyclone_intensification_guidance_kernel(
         h10 = placed("h10", [P, KB], BF16, at_pool)
         gated(nc.gpsimd, h10[:], 1, 0, gate10)
         h_own = placed("h_own", [P, 2, KB], BF16, at_own)
-        gate20 = gate_tile(2, 0, at_later)
-        gate21 = gate_tile(2, 1, at_later + 4 * KB)
+        gate20 = gate_tile(2, 0, at_w2 + 8 * KB)
+        gate21 = gate_tile(2, 1, at_w2 + 12 * KB)
         gate30 = gate_tile(3, 0, at_rest)
         gate31 = gate_tile(3, 1, at_diff + 4 * KB)
         frame_gate(gate20, 0, w2_q[0], x_q2[0], x_q2[1][:], 0)

@@ -72,6 +72,7 @@ def tile_list_cyclone_intensification_guidance_kernel(
         at_w3 = room(8 * KB)
         w3_raw = placed("w3_raw", [P, HALVES * H], U32, at_w3)
 
+        nc.gpsimd.memset(tab_s[:].bitcast(I32), 0)
         nc.vector.memset(ws_raw[:, 0, :].bitcast(I32), 0)
         nc.gpsimd.memset(ws_raw[:, 1, :].bitcast(I32), 0)
 
@@ -93,7 +94,7 @@ def tile_list_cyclone_intensification_guidance_kernel(
         nc.sync.dma_start(list_tab[:], offs)
         for q in range(QUADRANTS):
             rows = tab_scales[0, scale_rows(q), :].bitcast(I32)
-            nc.sync.dma_start(tab_s[32 * q : 32 * q + 32, :].bitcast(I32), rows.partition_broadcast(8))
+            nc.scalar.dma_start(tab_s[32 * q : 32 * q + 4, :].bitcast(I32), rows)
         nc.sync.dma_start(tab_w[:].bitcast(I32), tab_words[0].rearrange("p c i -> p (c i)").bitcast(I32))
         for q in range(QUADRANTS):
             load_w1_scales(q)

@@ -92,15 +92,15 @@ def tile_list_cyclone_intensification_guidance_kernel(
             )
 
         nc.sync.dma_start(list_tab[:], offs)
+        nc.sync.dma_start(w1_raw[:].bitcast(I32), w1_words[0].bitcast(I32))
+        nc.sync.dma_start(list_early[:], offs3)
         for q in range(QUADRANTS):
             rows = tab_scales[0, scale_rows(q), :].bitcast(I32)
-            nc.scalar.dma_start(tab_s[32 * q : 32 * q + 4, :].bitcast(I32), rows)
+            nc.sync.dma_start(tab_s[32 * q : 32 * q + 4, :].bitcast(I32), rows)
         nc.sync.dma_start(tab_w[:].bitcast(I32), tab_words[0].rearrange("p c i -> p (c i)").bitcast(I32))
         for q in range(QUADRANTS):
             load_w1_scales(q)
-        nc.sync.dma_start(w1_raw[:].bitcast(I32), w1_words[0].bitcast(I32))
         nc.sync.dma_start(planes[0][:], x_rows[0])
-        nc.sync.dma_start(list_early[:], offs3)
         nc.sync.dma_start(list_late[:], offs2)
         for t in range(1, PACK):
             nc.sync.dma_start(planes[t][:], x_rows[t])

@@ -64,7 +64,7 @@ def tile_list_cyclone_intensification_guidance_kernel(
         at_planes = room(32 * KB)
         planes = [placed("plane%d" % t, [P, T], F32, at_planes + 8 * KB * t) for t in range(PACK)]
         at_w2 = room(16 * KB)
-        w2_parts = [(0, 0, PASS // 2), (0, PASS // 2, PASS // 2), (1, 0, PASS)]
+        w2_parts = [(b, lo, PASS // 2) for b in range(HALVES) for lo in (0, PASS // 2)]
         w2_raw = [
             placed("w2_raw%d" % n, [P, PACK, width], F32, at_w2 + 16 * (b * PASS + lo))
             for n, (b, lo, width) in enumerate(w2_parts)
@@ -114,7 +114,8 @@ def tile_list_cyclone_intensification_guidance_kernel(
             w3_raw[:].bitcast(I32).rearrange("p (g c) -> p g c", g=HALVES),
             w3_words.rearrange("g p c i -> p g (c i)").bitcast(I32),
         )
-        nc.sync.dma_start(w2_raw[2][:], w2_rows[:, :, PASS : 2 * PASS])
+        for n in range(2, 4):
+            nc.sync.dma_start(w2_raw[n][:], w2_rows[:, :, n * PASS // 2 : (n + 1) * PASS // 2])
         nc.sync.dma_start(bias[:], b2.rearrange("(b p t) -> p b t", b=HALVES, t=PACK))
         nc.sync.dma_start(gain[:], res.rearrange("(b p t) -> p b t", b=HALVES, t=PACK))
 
@@ -264,7 +265,8 @@ def tile_list_cyclone_intensification_guidance_kernel(
             if stores == 1:
                 nc.sync.dma_start(rows.rearrange("e p j -> p e j"), result[:].rearrange("p (e j) -> p e j", e=2))
 
-        nc.vector.tensor_copy(v_w[:], tab_w[:].indirect(list_tab[:]))
+        for c in range(2):
+            nc.vector.tensor_copy(v_w[:, cols(2 * c, 2)], tab_w[:].indirect(entries(list_tab, 2 * c, 2)))
         w1_s = kept("w1_s", [P, H], U8)
         reorder_columns(nc.gpsimd.tensor_copy, w1_s[:], ws_raw[:, 0, :], HALVES, LINE)
         w1_w = kept("w1_w", [P, 2 * H], U8)
@@ -313,6 +315,7 @@ def tile_list_cyclone_intensification_guidance_kernel(
         at_w2bf = room(4 * KB)
         w2_bf1 = placed("w2_bf1", [P, PASS * PACK], BF16, at_w2bf)
         weave_w2(2, w2_bf1[:])
+        weave_w2(3, w2_bf1[:])
 
         early_rest = placed("early_rest", [P, PACK, PAIR], F32, at_rest)
         w3_s = placed("w3_s", [P, H], U8, at_w3w - KB + 64)

@@ -108,13 +108,11 @@ def tile_list_cyclone_intensification_guidance_kernel(
             nc.sync.dma_start(
                 ws_raw[32 * q : 32 * q + 8, 1, :].bitcast(I32), w3_scales[:, scale_rows(q), :].bitcast(I32)
             )
-        for n in range(2):
-            nc.sync.dma_start(w2_raw[n][:], w2_rows[:, :, n * PASS // 2 : (n + 1) * PASS // 2])
         nc.sync.dma_start(
             w3_raw[:].bitcast(I32).rearrange("p (g c) -> p g c", g=HALVES),
             w3_words.rearrange("g p c i -> p g (c i)").bitcast(I32),
         )
-        for n in range(2, 4):
+        for n in range(4):
             nc.sync.dma_start(w2_raw[n][:], w2_rows[:, :, n * PASS // 2 : (n + 1) * PASS // 2])
         nc.sync.dma_start(bias[:], b2.rearrange("(b p t) -> p b t", b=HALVES, t=PACK))
         nc.sync.dma_start(gain[:], res.rearrange("(b p t) -> p b t", b=HALVES, t=PACK))
@@ -284,9 +282,6 @@ def tile_list_cyclone_intensification_guidance_kernel(
             copy_banks(q, 1, held[q])
         memory_pair(1)
         memory_quarter(3, 1, 0)
-        w2_bf0 = kept("w2_bf0", [P, PASS * PACK], BF16)
-        weave_w2(0, w2_bf0[:])
-        weave_w2(1, w2_bf0[:])
 
         at_diff = room(8 * KB)
         diff_first = placed("diff_first", [P, PACK, PAIR], F32, at_diff)
@@ -307,15 +302,12 @@ def tile_list_cyclone_intensification_guidance_kernel(
         first_plane(2, at_early)
         first_plane(3, at_last)
 
-        third = placed("third", [P, 6 * QUARTER], F32, at_w2)
-        x_first = third[:, 2 * QUARTER : 6 * QUARTER].bitcast(BF16)
-        diff_2 = third[:, 0 : 4 * QUARTER].rearrange("p (t c) -> p t c", t=PACK)
+        x_first = kept("x_first", [P, 2 * KB], BF16)
         for q in range(2):
             nc.scalar.copy(woven(x_first[:, q * KB : (q + 1) * KB]), by_fours(diff_first[:, :, cols(q)]))
-        at_w2bf = room(4 * KB)
-        w2_bf1 = placed("w2_bf1", [P, PASS * PACK], BF16, at_w2bf)
-        weave_w2(2, w2_bf1[:])
-        weave_w2(3, w2_bf1[:])
+        w2_bf = [kept("w2_bf%d" % b, [P, PASS * PACK], BF16) for b in range(HALVES)]
+        for n in range(4):
+            weave_w2(n, w2_bf[n // 2][:])
 
         early_rest = placed("early_rest", [P, PACK, PAIR], F32, at_rest)
         w3_s = placed("w3_s", [P, H], U8, at_w3w - KB + 64)
@@ -328,14 +320,12 @@ def tile_list_cyclone_intensification_guidance_kernel(
         def second_change(diff, t, q):
             gather_change(diff[:, t, :], early_rest[:, t, cols(q - 2)], t, q)
 
-        second_change(diff_2, 0, 2)
-        second_change(diff_2, 1, 2)
-        w2_q0 = quantise("w2_q0", w2_bf0[:], at_w3 + 64)
-        x_q = quantise("x_q", x_first, at_w3 + 64 + 2 * KB)
-        second_change(diff_2, 2, 2)
-        second_change(diff_2, 3, 2)
-        w2_q = [w2_q0, quantise("w2_q1", w2_bf1[:])]
-        diff_3 = placed("diff_3", [P, PACK, QUARTER], F32, at_w2bf)[:]
+        diff_2, diff_3 = (placed("diff_%d" % q, [P, PACK, QUARTER], F32, at_w2 + (8 * q - 12) * KB)[:] for q in (2, 3))
+        x_q = quantise("x_q", x_first[:])
+        w2_q = [quantise("w2_q0", w2_bf[0][:])]
+        for t in range(PACK):
+            second_change(diff_2, t, 2)
+        w2_q.append(quantise("w2_q1", w2_bf[1][:]))
         for t in range(PACK):
             second_change(diff_3, t, 3)
 

@@ -25,6 +25,7 @@ PAIR = 2 * QUARTER
 QUADRANTS = 4
 LINE = 16
 KB = 1024
+OWN = 48
 
 
 def tile_list_cyclone_intensification_guidance_kernel(
@@ -219,8 +220,8 @@ def tile_list_cyclone_intensification_guidance_kernel(
                     t = 2 * u + e
                     nc.scalar.activation(gate[:, t, :], acc[:, cols(e)], ACT.Sigmoid, bias=bias[:, b, t : t + 1])
 
-        def gated(engine, h_bf, q, b, gate):
-            engine.tensor_tensor(woven(h_bf), by_fours(a_rows(q, b)), by_fours(gate), ALU.mult)
+        def gated(engine, h_bf, a_part, gate):
+            engine.tensor_tensor(woven(h_bf), by_fours(a_part), by_fours(gate), ALU.mult)
 
         def gated_from_banks(h_bf, accs, gate):
             for n, acc in enumerate(accs):
@@ -251,7 +252,7 @@ def tile_list_cyclone_intensification_guidance_kernel(
             for g in range(HALVES):
                 if h_q[g] is not None:
                     last_passes(n, g, h_q[g], acc)
-            result = placed("result%d%d" % (q, n), [P, PAIR], F32, at)
+            result = placed("result%d%d" % (q, n), [P, PAIR], F32, at)[:] if isinstance(at, int) else at
             rows = out_rows[b, 2 * u : 2 * u + 2, :, cols(q)]
             for e in range(2):
                 t = 2 * u + e
@@ -261,7 +262,7 @@ def tile_list_cyclone_intensification_guidance_kernel(
                 if stores == 2:
                     nc.sync.dma_start(rows[e], result[:, cols(e)])
             if stores == 1:
-                nc.sync.dma_start(rows.rearrange("e p j -> p e j"), result[:].rearrange("p (e j) -> p e j", e=2))
+                nc.sync.dma_start(rows.rearrange("e p j -> p e j"), result.rearrange("p (e j) -> p e j", e=2))
 
         for c in range(2):
             nc.vector.tensor_copy(v_w[:, cols(2 * c, 2)], tab_w[:].indirect(entries(list_tab, 2 * c, 2)))
@@ -334,30 +335,27 @@ def tile_list_cyclone_intensification_guidance_kernel(
 
         at_gates = room(16 * KB)
         gates = placed("gates", [P, PACK, PAIR], F32, at_gates)
-        gate00, gate10 = (gates[:, :, cols(q)] for q in range(2))
         gate11 = gate_tile(1, 1, at_gates + 8 * KB)
         gate01 = gate_tile(0, 1, at_gates + 12 * KB)
         for t in range(PACK):
             acc = bank(t)
             gate_pass(acc[:], w2_q[0], t, x_q[0], x_q[1][:])
             nc.scalar.activation(gates[:, t, :], acc[:], ACT.Sigmoid, bias=bias[:, 0, t : t + 1])
-        at_pool = room(2 * KB)
-        x_2 = placed("x_2", [P, KB], BF16, at_pool)
-        nc.scalar.copy(woven(x_2[:]), by_fours(diff_2))
+        pool = kept("pool", [P, 5 * KB], BF16)
+        x_2 = pool[:, KB + PACK * OWN : 2 * KB + PACK * OWN]
+        nc.scalar.copy(woven(x_2), by_fours(diff_2))
         for q, gate in enumerate((gate01, gate11)):
             frame_gate(gate, 1, w2_q[1], x_q[0][:, cols(q)], x_q[1][:, cols(q)], 2 * q)
 
-        at_own = room(4 * KB)
-        at_h00 = room(2 * KB) - 64
         x_3 = kept("x_3", [P, KB], BF16)
         nc.scalar.copy(woven(x_3[:]), by_fours(diff_3))
-        h00 = placed("h00", [P, KB], BF16, at_h00)
-        gated(nc.vector, h00[:], 0, 0, gate00)
-        x_q2 = quantise("x_q2", x_2[:])
-        q00 = quantise("q00", h00[:])
-        h10 = placed("h10", [P, KB], BF16, at_pool)
-        gated(nc.gpsimd, h10[:], 1, 0, gate10)
-        h_own = placed("h_own", [P, 2, KB], BF16, at_own)
+        split = QUARTER + OWN
+        gated(nc.vector, pool[:, 0 : PACK * split], a_sb[0][0][:, :, 0:split], gates[:, :, 0:split])
+        x_q2 = quantise("x_q2", x_2)
+        q00 = quantise("q00", pool[:, 0:KB])
+        h10 = pool[:, KB : 2 * KB]
+        gated(nc.gpsimd, pool[:, PACK * split : 2 * KB], a_sb[0][0][:, :, split:PAIR], gates[:, :, split:PAIR])
+        h01, h11 = pool[:, 2 * KB : 3 * KB], pool[:, 3 * KB : 4 * KB]
         gate20 = gate_tile(2, 0, at_w2 + 8 * KB)
         gate21 = gate_tile(2, 1, at_w2 + 12 * KB)
         gate30 = gate_tile(3, 0, at_rest)
@@ -373,43 +371,45 @@ def tile_list_cyclone_intensification_guidance_kernel(
                 last_passes(n0 + n, 0, h_g, acc)
             return accs
 
-        gated_from_banks(h_own[:, 0, :], held[0], gate01)
+        gated_from_banks(h01, held[0], gate01)
         opened = open_banks(4, 2, 0, q00)
-        gated_from_banks(h_own[:, 1, :], held[1], gate11)
+        gated_from_banks(h11, held[1], gate11)
         opened = opened + open_banks(6, 2, 2, q00)
         bundle = placed("bundle", [P, 4 * QUARTER], U32, at_gates + 6 * KB)
-        q01 = quantise_into(bundle[:, cols(0)], "q01", h_own[:, 0, :])
+        q01 = quantise_into(bundle[:, cols(0)], "q01", h01)
         x_q3 = quantise_into(bundle[:, cols(1)], "x_q3", x_3[:])
-        q10 = quantise_into(bundle[:, cols(3)], "q10", h10[:])
-        q11 = quantise_into(bundle[:, cols(2)], "q11", h_own[:, 1, :])
+        q10 = quantise_into(bundle[:, cols(3)], "q10", h10)
+        q11 = quantise_into(bundle[:, cols(2)], "q11", h11)
 
         at_results = [at_planes + 2 * KB * n for n in range(16)]
-        h20 = placed("h20", [P, KB], BF16, at_pool)
-        gated(nc.gpsimd, h20[:], 2, 0, gate20)
+        h20 = h10
+        gated(nc.gpsimd, h20, a_rows(2, 0), gate20)
         for n in range(4):
             finish(0, n, (None, q01), opened[n], at_results[n])
         frame_gate(gate30, 0, w2_q[0], x_q3[0], x_q3[1][:], 2)
         frame_gate(gate31, 1, w2_q[1], x_q3[0], x_q3[1][:], 2)
-        at_h3 = room(2 * KB)
-        h30 = placed("h30", [P, KB], BF16, at_h3)
-        gated(nc.gpsimd, h30[:], 3, 0, gate30)
+        h30 = pool[:, 4 * KB : 5 * KB]
+        gated(nc.gpsimd, h30, a_rows(3, 0), gate30)
         for n in range(2):
             finish(1, n, (q10, q11), bank(4 + n), at_results[4 + n])
-        h21 = placed("h21", [P, KB], BF16, at_own)
-        gated_from_banks(h21[:], late, gate21)
+        h21 = h11
+        gated_from_banks(h21, late, gate21)
         finish(1, 2, (q10, q11), bank(6), at_results[6])
-        q20 = quantise("q20", h20[:], at_rest)
+        q20 = quantise("q20", h20, at_rest)
         opened = [open_banks(first, 1, n, q20)[0] for n, first in enumerate((4, 7))]
-        q21 = quantise("q21", h21[:], at_rest + KB)
-        q30 = quantise("q30", h30[:], at_rest + 2 * KB)
-        h31 = placed("h31", [P, KB], BF16, at_h3)
-        gated(nc.gpsimd, h31[:], 3, 1, gate31)
-        finish(1, 3, (q10, q11), bank(5), at_pool)
+        q21 = quantise("q21", h21, at_rest + KB)
+        q30 = quantise("q30", h30, at_rest + 2 * KB)
+        h31 = pool[:, 4 * KB - PACK * OWN : 5 * KB - PACK * OWN]
+        gated(nc.vector, h31[:, 0 : PACK * OWN], a_rows(3, 1)[:, :, 0:OWN], gate31[:, :, 0:OWN])
+        gated(nc.gpsimd, h31[:, PACK * OWN : KB], a_rows(3, 1)[:, :, OWN:QUARTER], gate31[:, :, OWN:QUARTER])
+        finish(1, 3, (q10, q11), bank(5), h20.bitcast(F32))
         for n in range(2):
             finish(2, n, (None, q21), opened[n], at_results[7 + n])
         finish(2, 2, (q20, q21), bank(6), at_results[9])
+        closing = open_banks(5, 1, 3, q20)[0]
+        last_passes(3, 1, q21, closing)
         opened = open_banks(0, 4, 0, q30)
-        q31 = quantise("q31", h31[:])
-        finish(2, 3, (q20, q21), bank(5), at_diff + 4 * KB)
+        q31 = quantise("q31", h31, at_rest + KB)
+        finish(2, 3, (None, None), closing, at_diff + 4 * KB)
         for n in range(4):
             finish(3, n, (None, q31), opened[n], at_results[10 + n], 2 if n == 3 else 1)

@@ -153,8 +153,10 @@ def tile_list_cyclone_intensification_guidance_kernel(
                 w2_raw[n][:].rearrange("p j (m u e) -> p u m j e", u=2, e=2),
             )
 
-        def quantise_into(codes, name, src):
-            scales = kept(name + "_scales", [P, codes.shape[1]], U8)
+        def quantise_into(codes, name, src, at_scales=None):
+            shape = [P, codes.shape[1]]
+            name = name + "_scales"
+            scales = kept(name, shape, U8) if at_scales is None else placed(name, shape, U8, at_scales)
             nc.vector.quantize_mx(out=codes.bitcast(FP8X4), scales=scales[:], in_=src)
             return codes, scales
 
@@ -165,8 +167,10 @@ def tile_list_cyclone_intensification_guidance_kernel(
 
         a_sb = [[kept("a%d%d" % (c, b), [P, PACK, PAIR], F32) for b in range(HALVES)] for c in range(2)]
 
+        a_late = []
+
         def a_rows(q, b):
-            return a_sb[q // 2][b][:, :, cols(q % 2)]
+            return a_late[0][:] if (q, b) == (2, 1) else a_sb[q // 2][b][:, :, cols(q % 2)]
 
         def memory_pass(acc, b, t, lo, width):
             m0 = (b * PACK + t) * P
@@ -287,9 +291,9 @@ def tile_list_cyclone_intensification_guidance_kernel(
         at_diff = room(8 * KB)
         diff_first = placed("diff_first", [P, PACK, PAIR], F32, at_diff)
         at_rest = room(8 * KB)
-        at_w3w = room(10 * KB) + KB
+        at_w3s = room(KB)
         at_early = [room(KB) for q in range(2)]
-        at_last = (at_rest, at_w3w)
+        at_last = (at_w3s - KB // 2, at_early[1])
 
         def first_plane(t, at):
             early = [placed("early%d%d" % (q, t), [P, QUARTER], F32, at[q]) for q in range(2)]
@@ -311,9 +315,9 @@ def tile_list_cyclone_intensification_guidance_kernel(
             weave_w2(n, w2_bf[n // 2][:])
 
         early_rest = placed("early_rest", [P, PACK, PAIR], F32, at_rest)
-        w3_s = placed("w3_s", [P, H], U8, at_w3w - KB + 64)
+        w3_s = placed("w3_s", [P, H], U8, at_w3s)
         reorder_columns(nc.gpsimd.tensor_copy, w3_s[:], ws_raw[:, 1, :], HALVES, LINE)
-        w3_w = placed("w3_w", [P, HALVES * H], U32, at_w3w + 64)
+        w3_w = kept("w3_w", [P, HALVES * H], U32)
         reorder_columns(nc.gpsimd.tensor_copy, w3_w[:], w3_raw[:], HALVES * HALVES, LINE // 4)
         for t in range(PACK):
             gather_early(early_rest[:, t, :], t, 2, 2)
@@ -341,7 +345,7 @@ def tile_list_cyclone_intensification_guidance_kernel(
             acc = bank(t)
             gate_pass(acc[:], w2_q[0], t, x_q[0], x_q[1][:])
             nc.scalar.activation(gates[:, t, :], acc[:], ACT.Sigmoid, bias=bias[:, 0, t : t + 1])
-        pool = kept("pool", [P, 5 * KB], BF16)
+        pool = kept("pool", [P, 4 * KB], BF16)
         x_2 = pool[:, KB + PACK * OWN : 2 * KB + PACK * OWN]
         nc.scalar.copy(woven(x_2), by_fours(diff_2))
         for q, gate in enumerate((gate01, gate11)):
@@ -363,7 +367,6 @@ def tile_list_cyclone_intensification_guidance_kernel(
         frame_gate(gate20, 0, w2_q[0], x_q2[0], x_q2[1][:], 0)
         frame_gate(gate21, 1, w2_q[1], x_q2[0], x_q2[1][:], 2)
         late = memory_banks(2, 1, 0)
-        copy_banks(2, 1, late)
 
         def open_banks(first, count, n0, h_g):
             accs = [bank(first + n) for n in range(count)]
@@ -376,8 +379,10 @@ def tile_list_cyclone_intensification_guidance_kernel(
         gated_from_banks(h11, held[1], gate11)
         opened = opened + open_banks(6, 2, 2, q00)
         bundle = placed("bundle", [P, 4 * QUARTER], U32, at_gates + 6 * KB)
-        q01 = quantise_into(bundle[:, cols(0)], "q01", h01)
-        x_q3 = quantise_into(bundle[:, cols(1)], "x_q3", x_3[:])
+        at_ends = room(4 * KB)
+        q01 = quantise_into(bundle[:, cols(0)], "q01", h01, at_ends)
+        at_late = room(4 * KB)
+        x_q3 = quantise_into(bundle[:, cols(1)], "x_q3", x_3[:], at_late)
         q10 = quantise_into(bundle[:, cols(3)], "q10", h10)
         q11 = quantise_into(bundle[:, cols(2)], "q11", h11)
 
@@ -388,18 +393,21 @@ def tile_list_cyclone_intensification_guidance_kernel(
             finish(0, n, (None, q01), opened[n], at_results[n])
         frame_gate(gate30, 0, w2_q[0], x_q3[0], x_q3[1][:], 2)
         frame_gate(gate31, 1, w2_q[1], x_q3[0], x_q3[1][:], 2)
-        h30 = pool[:, 4 * KB : 5 * KB]
+        ends = placed("ends", [P, 2 * KB], BF16, at_ends)
+        h30 = ends[:, KB : 2 * KB]
         gated(nc.gpsimd, h30, a_rows(3, 0), gate30)
         for n in range(2):
             finish(1, n, (q10, q11), bank(4 + n), at_results[4 + n])
-        h21 = h11
+        h21 = ends[:, 0:KB]
         gated_from_banks(h21, late, gate21)
+        a_late.append(placed("a_late", [P, PACK, QUARTER], F32, at_late))
+        copy_banks(2, 1, late)
         finish(1, 2, (q10, q11), bank(6), at_results[6])
         q20 = quantise("q20", h20, at_rest)
         opened = [open_banks(first, 1, n, q20)[0] for n, first in enumerate((4, 7))]
         q21 = quantise("q21", h21, at_rest + KB)
         q30 = quantise("q30", h30, at_rest + 2 * KB)
-        h31 = pool[:, 4 * KB - PACK * OWN : 5 * KB - PACK * OWN]
+        h31 = ends[:, KB - PACK * OWN : 2 * KB - PACK * OWN]
         gated(nc.vector, h31[:, 0 : PACK * OWN], a_rows(3, 1)[:, :, 0:OWN], gate31[:, :, 0:OWN])
         gated(nc.gpsimd, h31[:, PACK * OWN : KB], a_rows(3, 1)[:, :, OWN:QUARTER], gate31[:, :, OWN:QUARTER])
         finish(1, 3, (q10, q11), bank(5), h20.bitcast(F32))
@@ -408,7 +416,7 @@ def tile_list_cyclone_intensification_guidance_kernel(
         finish(2, 2, (q20, q21), bank(6), at_results[9])
         closing = open_banks(5, 1, 3, q20)[0]
         last_passes(3, 1, q21, closing)
-        opened = open_banks(0, 4, 0, q30)
+        opened = open_banks(2, 2, 0, q30) + open_banks(0, 2, 2, q30)
         q31 = quantise("q31", h31, at_rest + KB)
         finish(2, 3, (None, None), closing, at_diff + 4 * KB)
         for n in range(4):

@@ -64,14 +64,17 @@ def tile_list_cyclone_intensification_guidance_kernel(
         gain = keep.tile([P, HALVES, PACK], F32, name="gain")
         at_planes = room(32 * KB)
         planes = [placed("plane%d" % t, [P, T], F32, at_planes + 8 * KB * t) for t in range(PACK)]
-        at_w2 = room(16 * KB)
+        at_x = room(12 * KB) + 7 * KB
+        shared = kept("shared", [P, 10 * QUARTER], F32)
+
+        def four_rows(flat):
+            return flat.rearrange("p (t c) -> p t c", t=PACK)
+
         w2_parts = [(b, lo, PASS // 2) for b in range(HALVES) for lo in (0, PASS // 2)]
-        w2_raw = [
-            placed("w2_raw%d" % n, [P, PACK, width], F32, at_w2 + 16 * (b * PASS + lo))
-            for n, (b, lo, width) in enumerate(w2_parts)
-        ]
-        at_w3 = room(8 * KB)
-        w3_raw = placed("w3_raw", [P, HALVES * H], U32, at_w3)
+        w2_raw = [placed("w2_raw%d" % n, [P, PACK, QUARTER], F32, at)[:] for n, at in enumerate((room(4 * KB), at_x, room(4 * KB)))]
+        w2_raw.append(four_rows(shared[:, 6 * QUARTER : 10 * QUARTER]))
+        diff_2, diff_3 = (four_rows(shared[:, q * KB : (q + 1) * KB]) for q in range(2))
+        w3_raw = [kept("w3_raw%d" % g, [P, H], U32) for g in range(HALVES)]
 
         nc.gpsimd.memset(tab_s[:].bitcast(I32), 0)
         nc.vector.memset(ws_raw[:, 0, :].bitcast(I32), 0)
@@ -103,18 +106,22 @@ def tile_list_cyclone_intensification_guidance_kernel(
             load_w1_scales(q)
         nc.sync.dma_start(planes[0][:], x_rows[0])
         nc.sync.dma_start(list_late[:], offs2)
-        for t in range(1, PACK):
-            nc.sync.dma_start(planes[t][:], x_rows[t])
         for q in range(QUADRANTS):
             nc.sync.dma_start(
                 ws_raw[32 * q : 32 * q + 8, 1, :].bitcast(I32), w3_scales[:, scale_rows(q), :].bitcast(I32)
             )
-        nc.sync.dma_start(
-            w3_raw[:].bitcast(I32).rearrange("p (g c) -> p g c", g=HALVES),
-            w3_words.rearrange("g p c i -> p g (c i)").bitcast(I32),
-        )
-        for n in range(4):
-            nc.sync.dma_start(w2_raw[n][:], w2_rows[:, :, n * PASS // 2 : (n + 1) * PASS // 2])
+
+        def load_w2(n):
+            nc.sync.dma_start(w2_raw[n], w2_rows[:, :, n * QUARTER : (n + 1) * QUARTER])
+
+        nc.sync.dma_start(planes[1][:], x_rows[1])
+        load_w2(0)
+        for t in range(2, PACK):
+            nc.sync.dma_start(planes[t][:], x_rows[t])
+        for n in range(1, 4):
+            load_w2(n)
+        for g in range(HALVES):
+            nc.sync.dma_start(w3_raw[g][:].bitcast(I32), w3_words[g].rearrange("p c i -> p (c i)").bitcast(I32))
         nc.sync.dma_start(bias[:], b2.rearrange("(b p t) -> p b t", b=HALVES, t=PACK))
         nc.sync.dma_start(gain[:], res.rearrange("(b p t) -> p b t", b=HALVES, t=PACK))
 
@@ -150,7 +157,7 @@ def tile_list_cyclone_intensification_guidance_kernel(
             lo, width = w2_parts[n][1:]
             nc.scalar.copy(
                 w2_bf.rearrange("p (u e m j) -> p u m j e", u=2, e=2, j=PACK)[:, :, lo // PACK : (lo + width) // PACK],
-                w2_raw[n][:].rearrange("p j (m u e) -> p u m j e", u=2, e=2),
+                w2_raw[n].rearrange("p j (m u e) -> p u m j e", u=2, e=2),
             )
 
         def quantise_into(codes, name, src, at_scales=None):
@@ -243,7 +250,7 @@ def tile_list_cyclone_intensification_guidance_kernel(
                 m0 = (2 * n + e) * P
                 nc.tensor.matmul_mx(
                     out=acc[:, cols(e)],
-                    lhsT=w3_w[:, g * H + m0 : g * H + m0 + P].bitcast(FP8X4),
+                    lhsT=w3_w[g][:, m0 : m0 + P].bitcast(FP8X4),
                     lhsT_scale=w3_s[4 * g : P, m0 : m0 + P],
                     rhs=h_g[0].bitcast(FP8X4),
                     rhs_scale=h_g[1][:],
@@ -288,51 +295,59 @@ def tile_list_cyclone_intensification_guidance_kernel(
         memory_pair(1)
         memory_quarter(3, 1, 0)
 
+        w2_bf = [kept("w2_bf%d" % b, [P, PASS * PACK], BF16) for b in range(HALVES)]
+        weave_w2(0, w2_bf[0][:])
+        weave_w2(1, w2_bf[0][:])
+
         at_diff = room(8 * KB)
         diff_first = placed("diff_first", [P, PACK, PAIR], F32, at_diff)
-        at_rest = room(8 * KB)
-        at_w3s = room(KB)
-        at_early = [room(KB) for q in range(2)]
-        at_last = (at_w3s - KB // 2, at_early[1])
-
-        def first_plane(t, at):
-            early = [placed("early%d%d" % (q, t), [P, QUARTER], F32, at[q]) for q in range(2)]
+        early_second = []
+        at_first = [room(2 * KB) for t in range(2)]
+        for t in range(2):
+            early = placed("early_first%d" % t, [P, PAIR], F32, at_first[t])
+            early_second.append(kept("early_second%d" % t, [P, PAIR], F32))
+            gather_early(early[:], t, 0, 2)
+            gather_early(early_second[t][:], t, 2, 2)
+            gather_change(diff_first[:, t, :], early[:], t, 0, 2)
+        w3_s = placed("w3_s", [P, H], U8, at_first[0])
+        reorder_columns(nc.gpsimd.tensor_copy, w3_s[:], ws_raw[:, 1, :], HALVES, LINE)
+        early_2 = [kept("early_2%d" % q, [P, QUARTER], F32)[:] for q in range(2)]
+        early_3 = [shared[:, q * KB + P : q * KB + P + QUARTER] for q in range(2)]
+        for t, early in ((2, early_2), (3, early_3)):
             for q in range(2):
-                gather_early(early[q][:], t, q)
+                gather_early(early[q], t, q)
             for q in range(2):
-                gather_change(diff_first[:, t, cols(q)], early[q][:], t, q)
+                gather_change(diff_first[:, t, cols(q)], early[q], t, q)
 
-        first_plane(0, at_early)
-        first_plane(1, at_early)
-        first_plane(2, at_early)
-        first_plane(3, at_last)
-
-        x_first = kept("x_first", [P, 2 * KB], BF16)
+        x_first = placed("x_first", [P, 2 * KB], BF16, at_x)
         for q in range(2):
             nc.scalar.copy(woven(x_first[:, q * KB : (q + 1) * KB]), by_fours(diff_first[:, :, cols(q)]))
-        w2_bf = [kept("w2_bf%d" % b, [P, PASS * PACK], BF16) for b in range(HALVES)]
-        for n in range(4):
-            weave_w2(n, w2_bf[n // 2][:])
+        weave_w2(2, w2_bf[1][:])
+        weave_w2(3, w2_bf[1][:])
 
-        early_rest = placed("early_rest", [P, PACK, PAIR], F32, at_rest)
-        w3_s = placed("w3_s", [P, H], U8, at_w3s)
-        reorder_columns(nc.gpsimd.tensor_copy, w3_s[:], ws_raw[:, 1, :], HALVES, LINE)
-        w3_w = kept("w3_w", [P, HALVES * H], U32)
-        reorder_columns(nc.gpsimd.tensor_copy, w3_w[:], w3_raw[:], HALVES * HALVES, LINE // 4)
-        for t in range(PACK):
-            gather_early(early_rest[:, t, :], t, 2, 2)
+        def second_change(t, q):
+            gather_change((diff_2, diff_3)[q - 2][:, t, :], early_second[t][:, cols(q - 2)], t, q)
 
-        def second_change(diff, t, q):
-            gather_change(diff[:, t, :], early_rest[:, t, cols(q - 2)], t, q)
-
-        diff_2, diff_3 = (placed("diff_%d" % q, [P, PACK, QUARTER], F32, at_w2 + (8 * q - 12) * KB)[:] for q in (2, 3))
+        for q in (2, 3):
+            for t in range(2):
+                second_change(t, q)
         x_q = quantise("x_q", x_first[:])
-        w2_q = [quantise("w2_q0", w2_bf[0][:])]
-        for t in range(PACK):
-            second_change(diff_2, t, 2)
+        w2_q = [quantise("w2_q0", w2_bf[0][:], at_diff)]
+        w3_both = placed("w3_w", [P, HALVES * H], U32, at_x - 7 * KB)
+        w3_w = [w3_both[:, g * H : (g + 1) * H] for g in range(HALVES)]
+        reorder_columns(nc.gpsimd.tensor_copy, w3_w[0][:, 0:PASS], w3_raw[0][:, 0:PASS], 1, LINE // 4)
+        reorder_columns(nc.scalar.copy, w3_w[0][:, PASS:H], w3_raw[0][:, PASS:H], 1, LINE // 4)
+        reorder_columns(nc.gpsimd.tensor_copy, w3_w[1], w3_raw[1][:], HALVES, LINE // 4)
+        for t in range(2, PACK):
+            early_second.append(placed("early_second%d" % t, [P, PAIR], F32, at_x + (2 * t - 3) * KB))
+            gather_early(early_second[t][:], t, 2, 2)
+        second_change(2, 2)
+        second_change(3, 2)
         w2_q.append(quantise("w2_q1", w2_bf[1][:]))
-        for t in range(PACK):
-            second_change(diff_3, t, 3)
+        second_change(2, 3)
+        second_change(3, 3)
+        at_w2 = room(8 * KB) - 8 * KB
+        at_rest = room(4 * KB)
 
         def gate_tile(q, b, at):
             return placed("gate%d%d" % (q, b), [P, PACK, QUARTER], F32, at)[:]

@@ -65,15 +65,15 @@ def tile_list_cyclone_intensification_guidance_kernel(
         at_planes = room(32 * KB)
         planes = [placed("plane%d" % t, [P, T], F32, at_planes + 8 * KB * t) for t in range(PACK)]
         at_x = room(12 * KB) + 7 * KB
-        shared = kept("shared", [P, 10 * QUARTER], F32)
+        shared = kept("shared", [P, 11 * QUARTER], F32)
 
         def four_rows(flat):
             return flat.rearrange("p (t c) -> p t c", t=PACK)
 
         w2_parts = [(b, lo, PASS // 2) for b in range(HALVES) for lo in (0, PASS // 2)]
         w2_raw = [placed("w2_raw%d" % n, [P, PACK, QUARTER], F32, at)[:] for n, at in enumerate((room(4 * KB), at_x, room(4 * KB)))]
-        w2_raw.append(four_rows(shared[:, 6 * QUARTER : 10 * QUARTER]))
-        diff_2, diff_3 = (four_rows(shared[:, q * KB : (q + 1) * KB]) for q in range(2))
+        w2_raw.append(four_rows(shared[:, 7 * QUARTER : 11 * QUARTER]))
+        diff_second = four_rows(shared[:, 0 : PACK * PAIR])
         w3_raw = [kept("w3_raw%d" % g, [P, H], U32) for g in range(HALVES)]
 
         nc.gpsimd.memset(tab_s[:].bitcast(I32), 0)
@@ -311,13 +311,13 @@ def tile_list_cyclone_intensification_guidance_kernel(
             gather_change(diff_first[:, t, :], early[:], t, 0, 2)
         w3_s = placed("w3_s", [P, H], U8, at_first[0])
         reorder_columns(nc.gpsimd.tensor_copy, w3_s[:], ws_raw[:, 1, :], HALVES, LINE)
-        early_2 = [kept("early_2%d" % q, [P, QUARTER], F32)[:] for q in range(2)]
-        early_3 = [shared[:, q * KB + P : q * KB + P + QUARTER] for q in range(2)]
+        early_2 = kept("early_first2", [P, PAIR], F32)[:]
+        early_3 = shared[:, QUARTER : QUARTER + PAIR]
         for t, early in ((2, early_2), (3, early_3)):
             for q in range(2):
-                gather_early(early[q], t, q)
+                gather_early(early[:, cols(q)], t, q)
             for q in range(2):
-                gather_change(diff_first[:, t, cols(q)], early[q], t, q)
+                gather_change(diff_first[:, t, cols(q)], early[:, cols(q)], t, q)
 
         x_first = placed("x_first", [P, 2 * KB], BF16, at_x)
         for q in range(2):
@@ -325,12 +325,12 @@ def tile_list_cyclone_intensification_guidance_kernel(
         weave_w2(2, w2_bf[1][:])
         weave_w2(3, w2_bf[1][:])
 
-        def second_change(t, q):
-            gather_change((diff_2, diff_3)[q - 2][:, t, :], early_second[t][:, cols(q - 2)], t, q)
+        def second_change(t, q, count):
+            where = cols(q - 2, count)
+            gather_change(diff_second[:, t, where], early_second[t][:, where], t, q, count)
 
-        for q in (2, 3):
-            for t in range(2):
-                second_change(t, q)
+        for t in range(2):
+            second_change(t, 2, 2)
         x_q = quantise("x_q", x_first[:])
         w2_q = [quantise("w2_q0", w2_bf[0][:], at_diff)]
         w3_both = placed("w3_w", [P, HALVES * H], U32, at_x - 7 * KB)
@@ -341,11 +341,10 @@ def tile_list_cyclone_intensification_guidance_kernel(
         for t in range(2, PACK):
             early_second.append(placed("early_second%d" % t, [P, PAIR], F32, at_x + (2 * t - 3) * KB))
             gather_early(early_second[t][:], t, 2, 2)
-        second_change(2, 2)
-        second_change(3, 2)
+        second_change(2, 2, 2)
+        second_change(3, 2, 1)
         w2_q.append(quantise("w2_q1", w2_bf[1][:]))
-        second_change(2, 3)
-        second_change(3, 3)
+        second_change(3, 3, 1)
         at_w2 = room(8 * KB) - 8 * KB
         at_rest = room(4 * KB)
 
@@ -362,12 +361,12 @@ def tile_list_cyclone_intensification_guidance_kernel(
             nc.scalar.activation(gates[:, t, :], acc[:], ACT.Sigmoid, bias=bias[:, 0, t : t + 1])
         pool = kept("pool", [P, 4 * KB], BF16)
         x_2 = pool[:, KB + PACK * OWN : 2 * KB + PACK * OWN]
-        nc.scalar.copy(woven(x_2), by_fours(diff_2))
+        nc.scalar.copy(woven(x_2), by_fours(diff_second[:, :, cols(0)]))
         for q, gate in enumerate((gate01, gate11)):
             frame_gate(gate, 1, w2_q[1], x_q[0][:, cols(q)], x_q[1][:, cols(q)], 2 * q)
 
         x_3 = kept("x_3", [P, KB], BF16)
-        nc.scalar.copy(woven(x_3[:]), by_fours(diff_3))
+        nc.scalar.copy(woven(x_3[:]), by_fours(diff_second[:, :, cols(1)]))
         split = QUARTER + OWN
         gated(nc.vector, pool[:, 0 : PACK * split], a_sb[0][0][:, :, 0:split], gates[:, :, 0:split])
         x_q2 = quantise("x_q2", x_2)

from contextlib import ExitStack

import concourse.mybir as mybir

T, S, K, H = 2048, 1024, 512, 1024
FLOPS = 2 * S * (2 * K * H + H * H)

F32 = mybir.dt.float32
BF16 = mybir.dt.bfloat16
I32 = mybir.dt.int32
U32 = mybir.dt.uint32
U16 = mybir.dt.uint16
U8 = mybir.dt.uint8
FP8X4 = mybir.dt.float8_e4m3fn_x4
FP4X4 = mybir.dt.float4_e2m1fn_x4
ALU = mybir.AluOpType
ACT = mybir.ActivationFunctionType

P = 128
PACK = 4
PASS = P * PACK
HALVES = H // PASS
QUARTER = 256
PAIR = 2 * QUARTER
QUADRANTS = 4
LINE = 16
KB = 1024
OWN = 48


def tile_list_cyclone_intensification_guidance_kernel(
    tc, tab_words, tab_scales, offs, xT, offs2, offs3, w1_words, w1_scales, w2, b2, w3_words, w3_scales, res, out
):
    nc = tc.nc
    with ExitStack() as ctx:
        keep = ctx.enter_context(tc.tile_pool(name="keep", bufs=1))
        arena = ctx.enter_context(tc.tile_pool(name="arena", bufs=1))
        psum = ctx.enter_context(tc.psum_pool(name="psum", bufs=1))

        top = [0]

        def room(size):
            at = top[0]
            top[0] = at + size
            return at

        def placed(name, shape, dtype, at):
            return arena.tile(shape, dtype, name=name, tag=name, offset=at, align_bytes=64)

        def kept(name, shape, dtype):
            return keep.tile(shape, dtype, name=name, tag=name, align_bytes=64)

        def bank(n):
            return psum.tile([P, PAIR], F32, name="bank", tag="bank%d" % n)

        list_tab = keep.tile([P, S // 16], U16, name="list_tab")
        list_late = keep.tile([P, S // 16], U16, name="list_late")
        list_early = keep.tile([P, S // 16], U16, name="list_early")
        tab_w = kept("tab_w", [P, T], U32)
        tab_s = kept("tab_s", [P, T], U8)
        w1_raw = kept("w1_raw", [P, 2 * H], U8)
        ws_raw = kept("ws_raw", [P, 2, H], U8)
        bias = keep.tile([P, HALVES, PACK], F32, name="bias")
        gain = keep.tile([P, HALVES, PACK], F32, name="gain")
        at_planes = room(32 * KB)
        planes = [placed("plane%d" % t, [P, T], F32, at_planes + 8 * KB * t) for t in range(PACK)]
        at_x = room(12 * KB) + 7 * KB
        shared = kept("shared", [P, 11 * QUARTER], F32)

        def four_rows(flat):
            return flat.rearrange("p (t c) -> p t c", t=PACK)

        w2_parts = [(b, lo, PASS // 2) for b in range(HALVES) for lo in (0, PASS // 2)]
        w2_raw = [placed("w2_raw%d" % n, [P, PACK, QUARTER], F32, at)[:] for n, at in enumerate((room(4 * KB), at_x, room(4 * KB)))]
        w2_raw.append(four_rows(shared[:, 7 * QUARTER : 11 * QUARTER]))
        diff_second = four_rows(shared[:, 0 : PACK * PAIR])
        w3_raw = [kept("w3_raw%d" % g, [P, H], U32) for g in range(HALVES)]

        nc.gpsimd.memset(tab_s[:].bitcast(I32), 0)
        nc.vector.memset(ws_raw[:, 0, :].bitcast(I32), 0)
        nc.gpsimd.memset(ws_raw[:, 1, :].bitcast(I32), 0)

        warm = keep.tile([P, 2], F32, name="warm")
        nc.gpsimd.memset(warm[:, 0:1], 0.0)
        nc.scalar.activation(warm[:, 1:2], warm[:, 0:1], ACT.Sigmoid)

        x_rows = xT.rearrange("(p t) c -> t p c", t=PACK)
        w2_rows = w2.rearrange("(p j) c -> p j c", j=PACK)

        def scale_rows(q):
            return slice(4 * q, 4 * q + 4)

        def load_w1_scales(q):
            nc.sync.dma_start(
                ws_raw[32 * q : 32 * q + 4, 0, :].bitcast(I32), w1_scales[0, scale_rows(q), :].bitcast(I32)
            )

        nc.sync.dma_start(list_tab[:], offs)
        nc.sync.dma_start(w1_raw[:].bitcast(I32), w1_words[0].bitcast(I32))
        nc.sync.dma_start(list_early[:], offs3)
        for q in range(QUADRANTS):
            rows = tab_scales[0, scale_rows(q), :].bitcast(I32)
            nc.sync.dma_start(tab_s[32 * q : 32 * q + 4, :].bitcast(I32), rows)
        nc.sync.dma_start(tab_w[:].bitcast(I32), tab_words[0].rearrange("p c i -> p (c i)").bitcast(I32))
        for q in range(QUADRANTS):
            load_w1_scales(q)
        nc.sync.dma_start(planes[0][:], x_rows[0])
        nc.sync.dma_start(list_late[:], offs2)
        for q in range(QUADRANTS):
            nc.sync.dma_start(
                ws_raw[32 * q : 32 * q + 8, 1, :].bitcast(I32), w3_scales[:, scale_rows(q), :].bitcast(I32)
            )

        def load_w2(n):
            nc.sync.dma_start(w2_raw[n], w2_rows[:, :, n * QUARTER : (n + 1) * QUARTER])

        nc.sync.dma_start(planes[1][:], x_rows[1])
        load_w2(0)
        for t in range(2, PACK):
            nc.sync.dma_start(planes[t][:], x_rows[t])
        for n in range(1, 4):
            load_w2(n)
        for g in range(HALVES):
            nc.sync.dma_start(w3_raw[g][:].bitcast(I32), w3_words[g].rearrange("p c i -> p (c i)").bitcast(I32))
        nc.sync.dma_start(bias[:], b2.rearrange("(b p t) -> p b t", b=HALVES, t=PACK))
        nc.sync.dma_start(gain[:], res.rearrange("(b p t) -> p b t", b=HALVES, t=PACK))

        v_s = kept("v_s", [P, S], U8)
        v_w = kept("v_w", [P, S], U32)
        nc.vector.tensor_copy(v_s[:], tab_s[:].indirect(list_tab[:]))

        def reorder_columns(move, dst, src, groups, per_line):
            move(
                dst.rearrange("p (g t c i) -> p g c t i", g=groups, t=PACK, i=per_line),
                src.rearrange("p (g c i t) -> p g c t i", g=groups, t=PACK, i=per_line),
            )

        def cols(q, count=1):
            return slice(q * QUARTER, (q + count) * QUARTER)

        def entries(frames, q, count):
            return frames[:, q * QUARTER // 16 : (q + count) * QUARTER // 16]

        def gather_early(early, t, q, count=1):
            nc.vector.tensor_copy(early, planes[t][:].indirect(entries(list_early, q, count)))

        def gather_change(diff, early, t, q, count=1):
            nc.vector.tensor_tensor(diff, planes[t][:].indirect(entries(list_late, q, count)), early, ALU.subtract)

        def woven(flat):
            return flat.rearrange("p (c i t) -> p c t i", i=4, t=PACK)

        def by_fours(rows):
            return rows.rearrange("p t (c i) -> p c t i", i=4)

        def weave_w2(n, w2_bf):
            lo, width = w2_parts[n][1:]
            nc.scalar.copy(
                w2_bf.rearrange("p (u e m j) -> p u m j e", u=2, e=2, j=PACK)[:, :, lo // PACK : (lo + width) // PACK],
                w2_raw[n].rearrange("p j (m u e) -> p u m j e", u=2, e=2),
            )

        def quantise_into(codes, name, src, at_scales=None):
            shape = [P, codes.shape[1]]
            name = name + "_scales"
            scales = kept(name, shape, U8) if at_scales is None else placed(name, shape, U8, at_scales)
            nc.vector.quantize_mx(out=codes.bitcast(FP8X4), scales=scales[:], in_=src)
            return codes, scales

        def quantise(name, src, at=None):
            width = src.shape[1] // PACK
            codes = kept(name, [P, width], U32) if at is None else placed(name, [P, width], U32, at)
            return quantise_into(codes[:], name, src)

        a_sb = [[kept("a%d%d" % (c, b), [P, PACK, PAIR], F32) for b in range(HALVES)] for c in range(2)]

        a_late = []

        def a_rows(q, b):
            return a_late[0][:] if (q, b) == (2, 1) else a_sb[q // 2][b][:, :, cols(q % 2)]

        def memory_pass(acc, b, t, lo, width):
            m0 = (b * PACK + t) * P
            nc.tensor.matmul_mx(
                out=acc,
                lhsT=w1_w[:, 2 * m0 : 2 * (m0 + P)].bitcast(FP4X4),
                lhsT_scale=w1_s[:, m0 : m0 + P],
                rhs=v_w[:, lo : lo + width].bitcast(FP8X4),
                rhs_scale=v_s[:, lo : lo + width],
                start=True,
                stop=True,
            )

        def memory_banks(q, b, first):
            accs = []
            for n in range(2):
                acc = bank(first + n)
                for t in range(PACK):
                    memory_pass(acc[:, t * P : (t + 1) * P], b, t, q * QUARTER + n * P, P)
                accs.append(acc[:].rearrange("p (t c) -> p t c", t=PACK))
            return accs

        def copy_banks(q, b, accs):
            for n, acc in enumerate(accs):
                nc.scalar.copy(a_rows(q, b)[:, :, n * P : (n + 1) * P], acc)

        def memory_quarter(q, b, first):
            for u in range(2):
                acc = bank(first + u)
                for e in range(2):
                    memory_pass(acc[:, cols(e)], b, 2 * u + e, q * QUARTER, QUARTER)
                nc.scalar.copy(a_rows(q, b)[:, 2 * u : 2 * u + 2, :], acc[:].rearrange("p (e c) -> p e c", e=2))

        def gate_pass(acc, w2_half, t, x_codes, x_scales):
            nc.tensor.matmul_mx(
                out=acc,
                lhsT=w2_half[0][:, t * P : (t + 1) * P].bitcast(FP8X4),
                lhsT_scale=w2_half[1][:, t * P : (t + 1) * P],
                rhs=x_codes.bitcast(FP8X4),
                rhs_scale=x_scales,
                start=True,
                stop=True,
            )

        def frame_gate(gate, b, w2_half, x_codes, x_scales, first):
            for u in range(2):
                acc = bank(first + u)
                for e in range(2):
                    gate_pass(acc[:, cols(e)], w2_half, 2 * u + e, x_codes, x_scales)
                for e in range(2):
                    t = 2 * u + e
                    nc.scalar.activation(gate[:, t, :], acc[:, cols(e)], ACT.Sigmoid, bias=bias[:, b, t : t + 1])

        def gated(engine, h_bf, a_part, gate):
            engine.tensor_tensor(woven(h_bf), by_fours(a_part), by_fours(gate), ALU.mult)

        def gated_from_banks(h_bf, accs, gate):
            for n, acc in enumerate(accs):
                nc.vector.tensor_tensor(
                    woven(h_bf[:, n * PASS : (n + 1) * PASS]),
                    by_fours(acc),
                    by_fours(gate[:, :, n * P : (n + 1) * P]),
                    ALU.mult,
                )

        out_rows = out.rearrange("(b p t) j -> b t p j", b=HALVES, t=PACK)

        def last_passes(n, g, h_g, acc):
            for e in range(2):
                m0 = (2 * n + e) * P
                nc.tensor.matmul_mx(
                    out=acc[:, cols(e)],
                    lhsT=w3_w[g][:, m0 : m0 + P].bitcast(FP8X4),
                    lhsT_scale=w3_s[4 * g : P, m0 : m0 + P],
                    rhs=h_g[0].bitcast(FP8X4),
                    rhs_scale=h_g[1][:],
                    start=(g == 0 and e == 0),
                    stop=(g == HALVES - 1 and e == 1),
                )

        def finish(q, n, h_q, acc, at, stores=1):
            b, u = divmod(n, 2)
            for g in range(HALVES):
                if h_q[g] is not None:
                    last_passes(n, g, h_q[g], acc)
            result = placed("result%d%d" % (q, n), [P, PAIR], F32, at)[:] if isinstance(at, int) else at
            rows = out_rows[b, 2 * u : 2 * u + 2, :, cols(q)]
            for e in range(2):
                t = 2 * u + e
                nc.vector.scalar_tensor_tensor(
                    result[:, cols(e)], a_rows(q, b)[:, t, :], gain[:, b, t : t + 1], acc[:, cols(e)], ALU.mult, ALU.add
                )
                if stores == 2:
                    nc.sync.dma_start(rows[e], result[:, cols(e)])
            if stores == 1:
                nc.sync.dma_start(rows.rearrange("e p j -> p e j"), result.rearrange("p (e j) -> p e j", e=2))

        for c in range(2):
            nc.vector.tensor_copy(v_w[:, cols(2 * c, 2)], tab_w[:].indirect(entries(list_tab, 2 * c, 2)))
        w1_s = kept("w1_s", [P, H], U8)
        reorder_columns(nc.gpsimd.tensor_copy, w1_s[:], ws_raw[:, 0, :], HALVES, LINE)
        w1_w = kept("w1_w", [P, 2 * H], U8)
        reorder_columns(nc.scalar.copy, w1_w[:].bitcast(U16), w1_raw[:].bitcast(U16), HALVES, LINE // 2)

        def memory_pair(c):
            for t in range(PACK):
                acc = bank(t)
                memory_pass(acc[:], 0, t, c * PAIR, PAIR)
                nc.scalar.copy(a_sb[c][0][:, t, :], acc[:])

        memory_pair(0)
        held = [memory_banks(q, 1, 4 + 2 * q) for q in range(2)]
        for q in range(2):
            copy_banks(q, 1, held[q])
        memory_pair(1)
        memory_quarter(3, 1, 0)

        w2_bf = [kept("w2_bf%d" % b, [P, PASS * PACK], BF16) for b in range(HALVES)]
        weave_w2(0, w2_bf[0][:])
        weave_w2(1, w2_bf[0][:])

        at_diff = room(8 * KB)
        diff_first = placed("diff_first", [P, PACK, PAIR], F32, at_diff)
        early_second = []
        at_first = [room(2 * KB) for t in range(2)]
        for t in range(2):
            early = placed("early_first%d" % t, [P, PAIR], F32, at_first[t])
            early_second.append(kept("early_second%d" % t, [P, PAIR], F32))
            gather_early(early[:], t, 0, 2)
            gather_early(early_second[t][:], t, 2, 2)
            gather_change(diff_first[:, t, :], early[:], t, 0, 2)
        w3_s = placed("w3_s", [P, H], U8, at_first[0])
        reorder_columns(nc.gpsimd.tensor_copy, w3_s[:], ws_raw[:, 1, :], HALVES, LINE)
        early_2 = kept("early_first2", [P, PAIR], F32)[:]
        early_3 = shared[:, QUARTER : QUARTER + PAIR]
        for t, early in ((2, early_2), (3, early_3)):
            for q in range(2):
                gather_early(early[:, cols(q)], t, q)
            for q in range(2):
                gather_change(diff_first[:, t, cols(q)], early[:, cols(q)], t, q)

        x_first = placed("x_first", [P, 2 * KB], BF16, at_x)
        for q in range(2):
            nc.scalar.copy(woven(x_first[:, q * KB : (q + 1) * KB]), by_fours(diff_first[:, :, cols(q)]))
        weave_w2(2, w2_bf[1][:])
        weave_w2(3, w2_bf[1][:])

        def second_change(t, q, count):
            where = cols(q - 2, count)
            gather_change(diff_second[:, t, where], early_second[t][:, where], t, q, count)

        for t in range(2):
            second_change(t, 2, 2)
        x_q = quantise("x_q", x_first[:])
        w2_q = [quantise("w2_q0", w2_bf[0][:], at_diff)]
        w3_both = placed("w3_w", [P, HALVES * H], U32, at_x - 7 * KB)
        w3_w = [w3_both[:, g * H : (g + 1) * H] for g in range(HALVES)]
        reorder_columns(nc.gpsimd.tensor_copy, w3_w[0][:, 0:PASS], w3_raw[0][:, 0:PASS], 1, LINE // 4)
        reorder_columns(nc.scalar.copy, w3_w[0][:, PASS:H], w3_raw[0][:, PASS:H], 1, LINE // 4)
        reorder_columns(nc.gpsimd.tensor_copy, w3_w[1], w3_raw[1][:], HALVES, LINE // 4)
        for t in range(2, PACK):
            early_second.append(placed("early_second%d" % t, [P, PAIR], F32, at_x + (2 * t - 3) * KB))
            gather_early(early_second[t][:], t, 2, 2)
        second_change(2, 2, 2)
        second_change(3, 2, 1)
        w2_q.append(quantise("w2_q1", w2_bf[1][:]))
        second_change(3, 3, 1)
        at_w2 = room(8 * KB) - 8 * KB
        at_rest = room(4 * KB)

        def gate_tile(q, b, at):
            return placed("gate%d%d" % (q, b), [P, PACK, QUARTER], F32, at)[:]

        at_gates = room(16 * KB)
        gates = placed("gates", [P, PACK, PAIR], F32, at_gates)
        gate11 = gate_tile(1, 1, at_gates + 8 * KB)
        gate01 = gate_tile(0, 1, at_gates + 12 * KB)
        for t in range(PACK):
            acc = bank(t)
            gate_pass(acc[:], w2_q[0], t, x_q[0], x_q[1][:])
            nc.scalar.activation(gates[:, t, :], acc[:], ACT.Sigmoid, bias=bias[:, 0, t : t + 1])
        pool = kept("pool", [P, 4 * KB], BF16)
        x_2 = pool[:, KB + PACK * OWN : 2 * KB + PACK * OWN]
        nc.scalar.copy(woven(x_2), by_fours(diff_second[:, :, cols(0)]))
        for q, gate in enumerate((gate01, gate11)):
            frame_gate(gate, 1, w2_q[1], x_q[0][:, cols(q)], x_q[1][:, cols(q)], 2 * q)

        x_3 = kept("x_3", [P, KB], BF16)
        nc.scalar.copy(woven(x_3[:]), by_fours(diff_second[:, :, cols(1)]))
        split = QUARTER + OWN
        gated(nc.vector, pool[:, 0 : PACK * split], a_sb[0][0][:, :, 0:split], gates[:, :, 0:split])
        x_q2 = quantise("x_q2", x_2)
        q00 = quantise("q00", pool[:, 0:KB])
        h10 = pool[:, KB : 2 * KB]
        gated(nc.gpsimd, pool[:, PACK * split : 2 * KB], a_sb[0][0][:, :, split:PAIR], gates[:, :, split:PAIR])
        h01, h11 = pool[:, 2 * KB : 3 * KB], pool[:, 3 * KB : 4 * KB]
        gate20 = gate_tile(2, 0, at_w2 + 8 * KB)
        gate21 = gate_tile(2, 1, at_w2 + 12 * KB)
        gate30 = gate_tile(3, 0, at_rest)
        gate31 = gate_tile(3, 1, at_diff + 4 * KB)
        frame_gate(gate20, 0, w2_q[0], x_q2[0], x_q2[1][:], 0)
        frame_gate(gate21, 1, w2_q[1], x_q2[0], x_q2[1][:], 2)
        late = memory_banks(2, 1, 0)

        def open_banks(first, count, n0, h_g):
            accs = [bank(first + n) for n in range(count)]
            for n, acc in enumerate(accs):
                last_passes(n0 + n, 0, h_g, acc)
            return accs

        gated_from_banks(h01, held[0], gate01)
        opened = open_banks(4, 2, 0, q00)
        gated_from_banks(h11, held[1], gate11)
        opened = opened + open_banks(6, 2, 2, q00)
        bundle = placed("bundle", [P, 4 * QUARTER], U32, at_gates + 6 * KB)
        at_ends = room(4 * KB)
        q01 = quantise_into(bundle[:, cols(0)], "q01", h01, at_ends)
        at_late = room(4 * KB)
        x_q3 = quantise_into(bundle[:, cols(1)], "x_q3", x_3[:], at_late)
        q10 = quantise_into(bundle[:, cols(3)], "q10", h10)
        q11 = quantise_into(bundle[:, cols(2)], "q11", h11)

        at_results = [at_planes + 2 * KB * n for n in range(16)]
        h20 = h10
        gated(nc.gpsimd, h20, a_rows(2, 0), gate20)
        for n in range(4):
            finish(0, n, (None, q01), opened[n], at_results[n])
        frame_gate(gate30, 0, w2_q[0], x_q3[0], x_q3[1][:], 2)
        frame_gate(gate31, 1, w2_q[1], x_q3[0], x_q3[1][:], 2)
        ends = placed("ends", [P, 2 * KB], BF16, at_ends)
        h30 = ends[:, KB : 2 * KB]
        gated(nc.gpsimd, h30, a_rows(3, 0), gate30)
        for n in range(2):
            finish(1, n, (q10, q11), bank(4 + n), at_results[4 + n])
        h21 = ends[:, 0:KB]
        gated_from_banks(h21, late, gate21)
        a_late.append(placed("a_late", [P, PACK, QUARTER], F32, at_late))
        copy_banks(2, 1, late)
        finish(1, 2, (q10, q11), bank(6), at_results[6])
        q20 = quantise("q20", h20, at_rest)
        opened = [open_banks(first, 1, n, q20)[0] for n, first in enumerate((4, 7))]
        q21 = quantise("q21", h21, at_rest + KB)
        q30 = quantise("q30", h30, at_rest + 2 * KB)
        h31 = ends[:, KB - PACK * OWN : 2 * KB - PACK * OWN]
        gated(nc.vector, h31[:, 0 : PACK * OWN], a_rows(3, 1)[:, :, 0:OWN], gate31[:, :, 0:OWN])
        gated(nc.gpsimd, h31[:, PACK * OWN : KB], a_rows(3, 1)[:, :, OWN:QUARTER], gate31[:, :, OWN:QUARTER])
        finish(1, 3, (q10, q11), bank(5), h20.bitcast(F32))
        for n in range(2):
            finish(2, n, (None, q21), opened[n], at_results[7 + n])
        finish(2, 2, (q20, q21), bank(6), at_results[9])
        closing = open_banks(5, 1, 3, q20)[0]
        last_passes(3, 1, q21, closing)
        opened = open_banks(2, 2, 0, q30) + open_banks(0, 2, 2, q30)
        q31 = quantise("q31", h31, at_rest + KB)
        finish(2, 3, (None, None), closing, at_diff + 4 * KB)
        for n in range(4):
            finish(3, n, (None, q31), opened[n], at_results[10 + n], 2 if n == 3 else 1)
